import numpy as np, ml_dtypes
CORES = [6,15,38,47]
N = 4
BF = ml_dtypes.bfloat16
def gentries(a):
    return np.ascontiguousarray(a.reshape(8, 16, -1).transpose(0, 2, 1)).reshape(8, -1)
def gtable(e):
    e = np.asarray(e); return np.ascontiguousarray(e.reshape(8, -1, 16).transpose(0, 2, 1)).reshape(128, -1).astype(np.int32)
P, BS, T, CAP, G = 5376, 512, 3, 256, 128
S, SB, NEED, KILL = 2, 1, 9, 2
W = P + (N - 1) * G
def clans(rng, kk):
    sc = rng.choice(np.array([191.0, 120.0, 60.0], np.float32), (8, 1, 1)); cen = (sc * rng.random((8, 16, 4))).astype(np.float32); cen[:, :, 0] *= np.float32(0.1)
    t = np.maximum(1, (sc * (0.06 + 0.08 * rng.random((N, 8, 16, 1)))).astype(np.int32)); off = rng.integers(0, 4, (8, 1))
    def near():
        who = ((rng.random((N, 8, P)) * kk[:, None]).astype(np.int64) + off) & 3
        w = sc * (np.float32(0.05) + np.float32(0.15) * rng.random((N, 8, 1, P), dtype=np.float32))
        v = np.take_along_axis(np.broadcast_to(cen, (N, 8, 16, 4)), who[:, :, None, :], 3) + w * (2 * rng.random((N, 8, 16, P), dtype=np.float32) - 1)
        return np.clip(np.rint(v), 0, 191).astype(np.int32)
    x = near(); share = KILL * kk[:, None, None] * rng.choice(np.array([0.03, 0.06, 0.09]), (N, 8, 1, 1))
    y = np.where(rng.random((N, 8, 1, P)) < 0.1, 255, rng.integers(0, 192, (N, 8, 16, P), dtype=np.int32))
    return x, np.where(rng.random((N, 8, 1, P)) < share, near(), y), t
def chosen(key):
    return np.ascontiguousarray(np.argsort(key, axis=-1)[..., :16 * BS])
def deal(pts, num):
    a = np.empty((16, BS), np.int64); a[:, pts] = num.reshape(BS, 16).T
    return a.reshape(-1)
def parts(rng):
    x, y, t = clans(rng, rng.permutation(np.array([1, 1, 2, 2, 2, 3, 3, 4])))
    sd = rng.random((N, 8, BS)) < rng.choice(np.array([0.2, 0.4, 0.6, 0.9]), (N, 8, 1))
    c = chosen(rng.random((N, 8, T, S * W), dtype=np.float32))
    b = np.argsort(rng.random((N, 8, P)) * np.where(np.arange(P) < T * BS, 0.6, 1.0), axis=-1)[..., :(N - 1) * G]
    return x, y, t, sd, c, np.ascontiguousarray(b)
def pack(x, y, t, sd, c, b):
    c = c.reshape(N, 8, T, 16, BS).transpose(0, 1, 3, 2, 4).reshape(N, 128, T * BS)
    return {"x": x.reshape(N, 128, P).astype(np.float32).astype(BF), "y0": y.reshape(N, 128, P).astype(np.float32).astype(BF),
            "tl": t.reshape(N, 128, 1).astype(np.float32).astype(BF), "sd": sd.astype(np.float32).astype(BF),
            "cd": np.ascontiguousarray(c).astype(np.int32), "snd": np.stack([gtable(a) for a in b])}
def setup_inputs(rng):
    return pack(*parts(rng))
def setup_inputs_room(rng):
    x, y, t, sd, c, b = parts(rng)
    o = np.argsort(np.argsort(rng.random((N, 8, BS)), axis=-1), axis=-1); n = rng.choice(np.array([0, 1, CAP - 1, CAP, CAP + 1, BS]), (N, 8))
    n[0] = (CAP, CAP + 1, BS, CAP - 1, 1, 0, CAP, BS); n[1] = (BS, CAP, CAP + 1, CAP, CAP - 1, CAP, 0, 1)
    return pack(x, y, t, o < n[..., None], c, b)
def setup_inputs_ties(rng):
    x, y, t, sd, c, b = parts(rng)
    t = np.tile(rng.integers(0, 21, (1, 8, 16, 1)), (N, 1, 1, 1)); base = rng.integers(10, 121, (8, 16, 1))
    def step():
        return base + t * rng.integers(0, 3, (N, 8, 16, P), dtype=np.int32) + (rng.random((N, 8, 16, P), dtype=np.float32) < 0.3)
    x = step(); y = np.where(rng.random((N, 8, 1, P)) < 0.1 * KILL, step(), 255)
    t[:, 0] = 63; x[:, 0] = rng.choice(np.array([127, 128, 191]), (N, 16, P)); y[:, 0] = rng.choice(np.array([255, 255, 255, 191, 128, 64]), (N, 16, P))
    return pack(x, y, t, sd, c, b)
def setup_inputs_ends(rng):
    x, y, t, sd, c, b = parts(rng); a = np.arange(S * W); n = np.arange(BS); k = np.arange((N - 1) * G)
    key = rng.random((N, 8, T, S * W), dtype=np.float32)
    key[:, 1::2, :, S * P:] -= 1; key[:, 1::2, :, :S] -= 1; key[:, 1::2, :, S * (P - 1):S * P] -= 1
    key[:, 2] += (a >= 16 * BS).astype(np.float32); key[:, 4] += (a < S * W - 16 * BS).astype(np.float32)
    c = rng.permuted(chosen(key), axis=-1); c[:, 6] = np.arange(16 * BS)
    b[:, 1] = k; b[:, 3] = P - 1 - k; b[:, 7] = T * BS - (N - 1) * G + k
    sd[:, ::2] = n >= BS - CAP; sd[:, 1::2] = (n & 1) == 0; sd[:, 5] = (n == 0) | (n == BS - 1)
    return pack(x, y, t, sd, c, b)
def setup_inputs_dark(rng):
    x, y, t, sd, c, b = parts(rng); q = rng.permutation(N); g = rng.permutation(8)
    y[:, g[1]] = 255; t[:, g[2]] = 0
    for j in g[3:7]:
        x[:, j] = x[:, j] & 31; t[:, j] = 63
    y[:, g[3]] = y[:, g[3]] & 31; y[:, g[4]] = 128 + (y[:, g[4]] & 63)
    for r in range(N):
        m = np.isin(np.arange(BS) & 15, rng.permutation(16)[:16 * CAP // BS]); sd[r, g[4]] = m
        num = np.concatenate([rng.permutation(np.arange(S * P, S * W)), np.arange(16 * BS - S * (W - P))])
        c[r, g[4], 0] = deal(np.argsort(rng.random(BS) - m), num)
        m = rng.permutation(BS) < CAP; sd[r, g[5]] = m; o = rng.permutation(16)
        pl = np.argsort(o[np.arange(W) & 15] + rng.random(W))[:16 * CAP]; num = rng.permutation(S * pl + rng.integers(0, S, 16 * CAP))
        num = np.concatenate([num, rng.permutation(np.setdiff1d(np.arange(S * W), num))])[:16 * BS]
        c[r, g[5], 0] = deal(np.argsort(rng.random(BS) - m), num)
    c[:, g[4], 1:] = rng.permuted(np.tile(np.arange(16 * BS), (N, T - 1, 1)), axis=-1)
    key = rng.random((N, S * W)); key[:, S * BS:2 * S * BS] += 1; c[:, g[6], 0] = chosen(key)
    b[:, g[6]] = np.argsort(rng.random((N, P)) + (np.arange(P) // BS == 1), axis=-1)[:, :(N - 1) * G]
    sd[:, g[0]] = False; sd[q[0]] = False; sd[q[1], g[3]] = True
    return pack(x, y, t, sd, c, b)
def setup_inputs_spread(rng):
    x, y, t, sd, c, b = parts(rng)
    x = np.minimum((np.exp2(7.59 * rng.random((N, 8, 1, P))) * rng.random((N, 8, 16, P))).astype(np.int32), 191)
    y = np.minimum((np.exp2(7.59 * rng.random((N, 8, 1, P))) * rng.random((N, 8, 16, P))).astype(np.int32), 191)
    y = np.where(rng.random((N, 8, 1, P)) < rng.choice(np.array([0.1, 0.5, 0.9]), (N, 8, 1, 1)), 255, y)
    low = np.arange(16)[:, None] == rng.integers(0, 16, (N, 8, 1, P))
    y = np.where(rng.random((N, 8, 1, P)) < 0.15, np.where(low, y >> 3, 255), y)
    t = np.rint(np.exp2(6 * rng.random((N, 8, 16, 1)))).astype(np.int32) - 1
    return pack(x, y, np.minimum(t, 63), rng.random((N, 8, BS)) < rng.random((N, 8, 1)), c, b)
def check_inputs(d):
    bad = []
    for k, hi in (("x", 191), ("y0", 191), ("tl", 63), ("sd", 1)):
        v = np.asarray(d[k]).astype(np.float32); ok = (v >= 0) & (v <= hi) & (v == np.floor(v))
        if k == "y0": ok = ok | (v == 255)
        if not np.all(ok): bad.append("range of " + k)
    for k, hi in (("cd", S * W - 1), ("snd", P - 1)):
        if np.min(d[k]) < 0 or np.max(d[k]) > hi: bad.append("range of " + k)
    c = np.sort(np.asarray(d["cd"]).reshape(N, 8, 16, T, BS).transpose(0, 1, 3, 2, 4).reshape(N, 8, T, 16 * BS), axis=-1)
    if np.any(c[..., 1:] == c[..., :-1]): bad.append("equal numbers in a brood of cd")
    s = np.sort(np.stack([gentries(a) for a in d["snd"]]), axis=-1)
    if np.any(s[..., 1:] == s[..., :-1]): bad.append("equal numbers in snd")
    return bad
def windows(a, sl):
    res = []
    for r in range(N):
        w = [a[r]]
        for d in range(1, N):
            q = (r - d) % N; w.append(np.take_along_axis(a[q], sl[q, :, d - 1][:, None, :], 2))
        res.append(np.concatenate(w, axis=2))
    return np.stack(res)
def matches(come, xn, t):
    return np.add.reduce((np.abs(come - xn[:, None, :]) <= t[:, :, None]).astype(np.int64), axis=0) >= NEED
def reference(x, y0, tl, sd, cd, snd):
    X = x.astype(np.float32).astype(np.int32).reshape(N, 8, 16, P); Y = y0.astype(np.float32).astype(np.int32).reshape(N, 8, 16, P)
    t = tl.astype(np.float32).astype(np.int32).reshape(N, 8, 16, 1)
    C = (cd.astype(np.int64) >> SB).reshape(N, 8, 16, T * BS); sl = np.stack([gentries(a) for a in snd]).astype(np.int64).reshape(N, 8, N - 1, G)
    flag = np.zeros((N, 8, P), bool); flag[:, :, :BS] = sd.astype(np.float32) > 0.5; member = np.zeros((N, 8, P), bool)
    xw = windows(X, sl)
    for s in range(T):
        fl = flag[:, :, s * BS:(s + 1) * BS]
        member[:, :, s * BS:(s + 1) * BS] = fl & (np.add.accumulate(fl.astype(np.int64), axis=2) <= CAP)
        new = np.zeros((N, 8, W), bool)
        for r in range(N):
            for g in range(8):
                n = np.flatnonzero(member[r, g, s * BS:(s + 1) * BS]) + s * BS; c = C[r, g][:, n]
                come = xw[r, g][:, c.reshape(-1)].reshape(16, 16, len(n))
                new[r, g][c[matches(come, X[r, g][:, n], t[r, g])]] = True
        for r in range(N):
            flag[r] |= new[r, :, :P]
            for d in range(1, N):
                q = (r - d) % N
                for g in range(8): flag[q, g, sl[q, g, d - 1][new[r, g, P + (d - 1) * G:P + d * G]]] = True
    for s in range(T - 1, -1, -1):
        yw = windows(Y, sl); Z = Y.copy()
        for r in range(N):
            for g in range(8):
                n = np.flatnonzero(member[r, g, s * BS:(s + 1) * BS]) + s * BS; c = C[r, g][:, n]; xn = X[r, g][:, n]
                come = yw[r, g][:, c.reshape(-1)].reshape(16, 16, len(n))
                dead = np.add.reduce(matches(come, xn, t[r, g]).astype(np.int64), axis=0) >= KILL
                Z[r, g][:, n] = np.where(dead, 255, (xn + np.minimum(191, np.minimum.reduce(come, axis=1))) >> 1)
        Y = Z
    return {"yv": np.ascontiguousarray(Y[:, :, :, :T * BS]).reshape(N, 128, T * BS).astype(np.float32).astype(BF), "yf": np.where(member, 2, flag.astype(np.int64)).astype(np.float32).astype(BF)}

@@ -1,0 +1,527 @@
+from concourse.bass import DstId, RemoteDMATransfer
+from concourse.mybir import AluOpType as OP, ActivationFunctionType as AF
+
+P, PL, NB, BS, CAP, BK = 5376, 5760, 384, 512, 256, 128
+ST = 2 * PL
+WW = ST + 1024
+ZV, ZS = 6144, 9216
+BIG = 1023.0
+YO = CAP
+SPLITF, SPLITB = (40, 40, 40, 40), (30, 30, 34, 44)
+
+BT = " G2 X1 N0 L0 A1 G3 N1 C0 X2 L1 A2 P0 N2 C1 X3 L2 A3 "
+BE = " P1 B0 N3 C2 H L3 D0 P2 C3 P3 B1 D1 U "
+FT = " G0 T c G1 X0 A0 G2 X1 L0 A1 G3 C0 X2 L1 A2 P0 C1 X3 L2 A3 P1 C2 S0-4 S4-8 P2 V8-10 L3 C3 V10-12 P3 V12-16 F"
+SCHED = {
+    "out0": "f0" + FT,
+    "out1": "f1" + FT,
+    "back2": "b2 G0 T c G1 X0 A0" + BT + "; f2 g0 g1 ; b2" + BE + "Y",
+    "gap1": "f2 Q v0 v1 X0 A0 G2 X1 L0 A1 G3 C0 X2 L1 A2 P0 C1 X3 ; b1 g0 ; f2 L2 A3 P1 C2 ; b1 v0 g1 ; f2 L3 P2 C3 ; b1 v1 ; f2 P3",
+    "back1": "b1 X0 A0" + BT + "; f2 S0-2 ; b1" + BE + "Y",
+    "gap0": "f2 S2-6 S6-8 V8-12 V12-16 F M",
+    "back0": "b0 G0 G1 X0 A0" + BT + "W R" + BE,
+}
+
+SCRATCH = {
+    "xw": ("sbuf", [128, PL], "bfloat16"),
+    "ya": ("sbuf", [128, YO + PL], "bfloat16"), "yb": ("sbuf", [128, YO + PL], "bfloat16"),
+    "cdt": ("sbuf", [128, 1536], "int32"), "comp": ("sbuf", [128, 1024], "int32"),
+    "snd32": ("sbuf", [128, 24], "int32"), "snd16": ("sbuf", [128, 24], "uint16"), "snd2": ("sbuf", [128, 24], "uint16"),
+    "snd2i": ("sbuf", [128, 24], "int32"),
+    "ci": ("sbuf", [128, 256], "int32"), "xi": ("sbuf", [128, 256], "int32"), "vt": ("sbuf", [128, 256], "int32"),
+    "cf": ("sbuf", [128, 4096], "bfloat16"), "cb": ("sbuf", [128, 4096], "bfloat16"),
+    "scn": ("sbuf", [128, 4096], "bfloat16"),
+    "d0": ("sbuf", [128, 1024], "bfloat16"), "mt": ("sbuf", [128, 256], "bfloat16"), "hi": ("sbuf", [128, 256], "int32"),
+    "vo": ("sbuf", [128, 256], "uint16"), "trash": ("sbuf", [128, 64], "float32"),
+    "w1": ("sbuf", [128, WW], "bfloat16"), "w2": ("sbuf", [128, WW], "float32"),
+    "ones": ("sbuf", [128, 1024], "bfloat16"), "cst": ("sbuf", [128, 1024], "float32"),
+    "C": ("sbuf", [128, 2048], "bfloat16"), "R": ("sbuf", [128, 2048], "bfloat16"), "neg": ("sbuf", [128, 128], "bfloat16"),
+    "ident": ("sbuf", [128, 128], "bfloat16"), "B": ("sbuf", [128, 128], "bfloat16"), "A1": ("sbuf", [128, 128], "bfloat16"),
+    "hI": ("sbuf", [128, 128], "bfloat16"), "qI": ("sbuf", [128, 128], "bfloat16"),
+    "sdrep": ("sbuf", [128, 512], "bfloat16"), "sdblk": ("sbuf", [128, 336], "bfloat16"),
+    "L0": ("sbuf", [128, 400], "bfloat16"), "L1": ("sbuf", [128, 400], "bfloat16"), "L2": ("sbuf", [128, 400], "bfloat16"),
+    "Lg": ("sbuf", [128, 512], "bfloat16"), "fsend": ("sbuf", [128, NB], "bfloat16"),
+    "xsend": ("sbuf", [128, NB], "bfloat16"), "ysend": ("sbuf", [128, NB], "bfloat16"),
+    "bw": ("sbuf", [128, P], "bfloat16"), "io384": ("sbuf", [128, NB], "bfloat16"), "binv": ("sbuf", [128, 64], "uint16"),
+    "c2b": ("sbuf", [128, 768], "bfloat16"), "c2w": ("sbuf", [128, 1024], "bfloat16"),
+    "tlb": ("sbuf", [128, 1], "bfloat16"), "warm": ("sbuf", [128, 8], "float32"),
+    "flw": ("sbuf", [128, 32], "bfloat16"), "one32": ("sbuf", [128, 32], "float32"), "sc32": ("sbuf", [128, 32], "float32"),
+    "pp": ("sbuf", [128, 32], "float32"), "sl": ("sbuf", [128, 32], "float32"), "sl16": ("sbuf", [128, 32], "uint16"),
+    "zz": ("sbuf", [128, 32], "float32"), "t512": ("sbuf", [128, 32], "float32"),
+    "itp": ("sbuf", [128, 64], "int32"), "it2": ("sbuf", [128, 64], "int32"), "it3": ("sbuf", [128, 32], "int32"),
+    "mw": ("sbuf", [128, CAP + 1536], "bfloat16"), "memrep": ("sbuf", [128, 1536], "bfloat16"),
+    "memblk": ("sbuf", [128, 336], "bfloat16"), "w1blk": ("sbuf", [128, 672], "bfloat16"),
+    "w2blk": ("sbuf", [128, 672], "float32"), "w2bb": ("sbuf", [128, 672], "bfloat16"),
+    "tmpR": ("sbuf", [128, NB], "bfloat16"), "yfb": ("sbuf", [128, 336], "bfloat16"),
+    "psd0": ("psum", [128, 1024], "float32"), "psd1": ("psum", [128, 1024], "float32"),
+    "cnt0": ("psum", [128, 512], "float32"), "cnt1": ("psum", [128, 512], "float32"),
+    "psA": ("psum", [128, 512], "float32"), "psB": ("psum", [128, 512], "float32"),
+}
+for _s in range(3):
+    SCRATCH["c16_%d" % _s] = ("sbuf", [128, 256], "uint16")
+    SCRATCH["xm%d" % _s] = ("sbuf", [128, 256], "bfloat16")
+    SCRATCH["xT%d" % _s] = ("sbuf", [128, 256], "bfloat16")
+    SCRATCH["sb16_%d" % _s] = ("sbuf", [128, 32], "uint16")
+    SCRATCH["vs%d" % _s] = ("sbuf", [128, 32], "float32")
+    SCRATCH["ab%d" % _s] = ("sbuf", [128, 1024], "bfloat16")
+    SCRATCH["nr%d" % _s] = ("sbuf", [128, 1024], "bfloat16")
+
+_EX = ["x", "f0", "y", "f1", "b2", "f2", "b1"]
+_DM = ["snd", "xa", "xb", "tl", "sd", "cd0", "cd1", "sk", "zz", "zv", "ya", "yb", "bl1", "bl2", "blm", "cy", "o2", "o1",
+       "o0", "of"]
+SEMAPHORES = ["qv", "qs", "qt", "qg"] + ["ls_" + e for e in _EX] + ["rs_" + e for e in _EX] + ["d_" + d for d in _DM]
+
+
+def rank_program(g, core, T, topo):
+    rank = T.rank_of(core)
+    if rank is None:
+        return
+    nr_ranks = len(T.cores)
+    eng = {"v": g.vector, "s": g.scalar, "t": g.tensor, "g": g, "y": g.sync}
+    known = {q: {} for q in eng}
+    clock = {}
+    total = {}
+    recs = {}
+
+    def width(n):
+        return SCRATCH[n][1][1]
+
+    def reg(r):
+        return r[0], (r[1] if len(r) > 1 else 0), (r[2] if len(r) > 2 else width(r[0]))
+
+    def is_ps(n):
+        return SCRATCH[n][0] == "psum"
+
+    def ap(r):
+        n, a, b = reg(r)
+        if len(r) > 3:
+            return T[n][:, a:b:r[3]]
+        return T[n][:, a:b]
+
+    def need(q, evs):
+        best = {}
+        for sem, n in evs:
+            if known[q].get(sem, 0) < n and best.get(sem, 0) < n:
+                best[sem] = n
+        for sem in list(best):
+            n = best[sem]
+            if any(o != sem and clock[(o, m)].get(sem, 0) >= n for o, m in best.items()):
+                del best[sem]
+        for sem, n in best.items():
+            eng[q].wait_ge(T.sem[sem], n)
+            for k, m in clock[(sem, n)].items():
+                if known[q].get(k, 0) < m:
+                    known[q][k] = m
+
+    def deps(q, R, W):
+        evs = []
+        for r, w in [(r, is_ps(r[0])) for r in R] + [(r, True) for r in W]:
+            n, a, b = reg(r)
+            if is_ps(n):
+                a, b = 0, width(n)
+            for c0, c1, iw, qq, ev in recs.get(n, []):
+                if c0 < b and a < c1 and (w or iw) and not (q == "t" and qq == "t"):
+                    evs.append(ev)
+        return evs
+
+    def note(q, R, W, ev):
+        for r in W:
+            n, a, b = reg(r)
+            if is_ps(n):
+                a, b = 0, width(n)
+                recs[n] = [e for e in recs.get(n, []) if q == "t" and e[3] == "t"]
+            elif len(r) <= 3:
+                recs[n] = [e for e in recs.get(n, []) if not (a <= e[0] and e[1] <= b)]
+            recs.setdefault(n, []).append((a, b, True, q, ev))
+        for r in R:
+            n, a, b = reg(r)
+            if is_ps(n):
+                recs[n] = [(0, width(n), True, q, ev)]
+            else:
+                recs.setdefault(n, []).append((a, b, False, q, ev))
+
+    def event(q, sem, n):
+        total[sem] = total.get(sem, 0) + n
+        ev = (sem, total[sem])
+        clock[ev] = dict(known[q])
+        clock[ev][sem] = total[sem]
+        return ev
+
+    def op(q, fn, R, W):
+        need(q, deps(q, R, W))
+        sem = "q" + q
+        fn().then_inc(T.sem[sem], 1)
+        note(q, R, W, event(q, sem, 1))
+
+    def dma(q, name, pairs, R, W):
+        need(q, deps(q, R, W))
+        for o, i in pairs:
+            eng[q].dma_start(o, i).then_inc(T.sem["d_" + name], 16)
+        note(q, R, W, event(q, "d_" + name, 16 * len(pairs)))
+
+    def act(o, i, f, **k):
+        op("s", lambda: g.scalar.activation(ap(o), ap(i), f, **k), [i], [o])
+
+    def tc(q, o, i):
+        if q == "v":
+            op("v", lambda: g.vector.tensor_copy(ap(o), ap(i)), [i], [o])
+        else:
+            act(o, i, AF.Copy)
+
+    def gat(q, o, win, off):
+        if q == "v":
+            op("v", lambda: g.vector.tensor_copy(ap(o), ap(win).indirect(ap(off))), [win, off], [o])
+        else:
+            op("s", lambda: g.scalar.activation(ap(o), ap(win).indirect(ap(off)), AF.Copy), [win, off], [o])
+
+    def sca(win, off, i):
+        op("v", lambda: g.vector.tensor_copy(ap(win).indirect(ap(off)), ap(i)), [i, off], [win])
+
+    def tt(o, a, b, f):
+        op("v", lambda: g.vector.tensor_tensor(ap(o), ap(a), ap(b), f), [a, b], [o])
+
+    def ts(o, a, s1, f1, s2=None, f2=None):
+        if f2 is None:
+            op("v", lambda: g.vector.tensor_scalar(ap(o), ap(a), s1, None, f1), [a], [o])
+        else:
+            op("v", lambda: g.vector.tensor_scalar(ap(o), ap(a), s1, s2, f1, f2), [a], [o])
+
+    def fill(o, c):
+        op("v", lambda: g.vector.memset(ap(o), c), [], [o])
+
+    def mm(o, l, r, start, stop):
+        op("t", lambda: g.tensor.matmul(ap(o), ap(l), ap(r), start, stop), [l, r], [o])
+
+    def sums(o, terms):
+        for k, (l, r) in enumerate(terms):
+            mm(o, l, r, k == 0, k == len(terms) - 1)
+
+    def sel(o, i, pattern, cmp, fl, base, cm):
+        op("g", lambda: g.affine_select(ap(o), ap(i), pattern, cmp, fl, base, cm), [i], [o])
+
+    def iota(o, pattern, base, cm):
+        if SCRATCH[o[0]][2] == "int32":
+            op("g", lambda: g.iota(ap(o), pattern, base, cm), [], [o])
+        else:
+            op("g", lambda: g.iota(ap(o), pattern, base, cm, allow_small_or_imprecise_dtypes=True), [], [o])
+
+    def send(name, src, dst, col, sign):
+        need("g", deps("g", [(src,)], []))
+        trs, cnt, at = [], 0, 0
+        for d in range(1, nr_ranks):
+            to = T.cores[(rank + sign * d) % nr_ranks]
+            es = topo.engines(core, to)
+            n = len(es) // 4
+            a, b = topo.chip(core), topo.chip(to)
+            if topo.mates(a, b) or topo.same_plane(a, b):
+                mine = es[at:at + n]
+                at += n
+            else:
+                mine = es[2 * n:]
+            rid, pid, _ = topo.addr(to)
+            c0 = col + (d - 1) * BK
+            trs.append(RemoteDMATransfer(dst_ids=[DstId(rid=rid, pnc=pid)], dma_engine_mask=sum(1 << e for e in mine),
+                                         remote_sem=T.sem["rs_" + name], src=T[src][:, (d - 1) * BK:d * BK],
+                                         dst=T[dst][:, c0:c0 + BK]))
+            cnt += len(mine)
+        g.remote_dma_fused(trs, local_sem=T.sem["ls_" + name])
+        note("g", [(src,)], [], event("g", "ls_" + name, cnt))
+        total["rs_" + name] = cnt
+        ev = ("rs_" + name, cnt)
+        clock[ev] = {"rs_" + name: cnt}
+        recs[dst] = [e for e in recs.get(dst, []) if not (col <= e[0] and e[1] <= col + NB)]
+        recs[dst].append((col, col + NB, True, "r", ev))
+
+    def cmat(r):
+        return ("C", 128 * r, 128 * r + 128)
+
+    def pack(s):
+        r = ("cdt", BS * s, BS * s + BS)
+        ts(r, r, 256, OP.mult)
+        tt(r, r, ("xw", BS * s, BS * s + BS), OP.add)
+
+    def offsets(s, a, b):
+        ts(("ci", a, b), ("comp", a, b), 9, OP.arith_shift_right)
+        tc("v", ("c16_%d" % s, a, b), ("ci", a, b))
+
+    def lists(s):
+        ts(("flw",), ("psA", 0, 32), 0.25, OP.is_gt)
+        mm(("psB", 0, 32), ("B",), ("flw",), True, True)
+        mm(("psB", 32, 64), ("A1",), ("flw",), True, True)
+        op("v", lambda: g.vector.tensor_tensor_scan(ap(("sc32",)), ap(("one32",)), ap(("psB", 0, 32)), BIG, OP.mult, OP.add),
+           [("one32",), ("psB", 0, 32)], [("sc32",)])
+        tt(("pp",), ("psB", 32, 64), ("sc32",), OP.add)
+        tt(("sl",), ("pp",), ("t512",), OP.min)
+        tc("v", ("sl16",), ("sl",))
+        sca(("comp",), ("sl16",), ("cdt", BS * s, BS * s + BS))
+        offsets(s, 0, 128)
+        ts(("xi",), ("comp", 0, CAP), 255, OP.bitwise_and)
+        tc("v", ("xm%d" % s,), ("xi",))
+        for k in range(2):
+            mm(("psA", 128 * k, 128 * k + 128), ("xm%d" % s, 128 * k, 128 * k + 128), ("ident",), True, True)
+
+    def slots(s):
+        ts(("zz",), ("pp",), 255.5, OP.is_gt, 8192.0, OP.mult)
+        tt(("zz",), ("pp",), ("zz",), OP.add)
+        tt(("zz",), ("zz",), ("vs%d" % s,), OP.min)
+        tc("v", ("sb16_%d" % s,), ("zz",))
+
+    def own_flags(s):
+        a = 2 * BS * s
+        tc("s", ("c2w",), ("w2", a, a + 1024))
+        for n, lo, hi in (("w1", a, a + 1024), ("c2w", 0, 1024)):
+            for r in range(16):
+                for b in range(2):
+                    mm(("psA", 0, 32), cmat(r), (n, lo + 2 * r + b, hi, 32), n == "w1" and r + b == 0, False)
+
+    def their_flags(s):
+        k = 32 * (s - 1)
+        w = ("L%d" % (s - 1),)
+        gat("s", ("Lg", 256, 512), w, ("binv", k + 16, k + 32))
+        gat("v", ("Lg", 0, 256), w, ("binv", k, k + 16))
+        for r in range(16):
+            mm(("psA", 0, 32), cmat(r), ("Lg", r, 512, 16), False, r == 15)
+
+    def stream(name):
+        s, out = int(name[1]), name[0] == "f"
+        wn, w0, cand, split = ("xw", 0, "cf", SPLITF) if out else (("ya", "yb")[s % 2], YO, "cb", SPLITB)
+        ot = ("yb", "ya")[s % 2]
+        win, off = (wn, w0, w0 + PL), "c16_%d" % s
+
+        def gs(c):
+            k, j, n = 64 * c, 1024 * c, split[c]
+            gat("s", (cand, j + 16 * n, j + 1024), win, (off, k + n, k + 64))
+
+        def gv(c):
+            k, j, n = 64 * c, 1024 * c, split[c]
+            gat("v", (cand, j, j + 16 * n), win, (off, k, k + n))
+
+        def G(c):
+            gs(c)
+            gv(c)
+
+        def X(c):
+            ps, hf = "psd%d" % (c % 2), c // 2
+            for b in range(2):
+                q = (2 * c + b) % 4
+                mm((ps, 512 * b, 512 * b + 512), ("xT%d" % s, 128 * hf, 128 * hf + 128), ("R", 512 * q, 512 * q + 512), True, False)
+            for b in range(2):
+                j = 1024 * c + 512 * b
+                mm((ps, 512 * b, 512 * b + 512), ("ident",), (cand, j, j + 512), False, True)
+
+        def A(c):
+            act(("ab%d" % (c % 3),), ("psd%d" % (c % 2),), AF.Abs)
+
+        def L(c):
+            o, i = ("nr%d" % (c % 3),), ("ab%d" % (c % 3),)
+            op("v", lambda: g.vector.tensor_scalar(ap(o), ap(i), ap(("tlb",)), None, OP.is_le), [i, ("tlb",)], [o])
+
+        def cn(c, at=0):
+            k = at + 64 * (c // 2)
+            return ("cnt%d" % (c % 2), k, k + 64)
+
+        def C(c):
+            sums(cn(c), [(cmat(i), ("nr%d" % (c % 3), i, 1024, 16)) for i in range(16)])
+
+        def Pt(c):
+            r = (64 * c, 64 * c + 64)
+            if out:
+                m = cn(c, 256)
+                ts(m, cn(c), 8.5, OP.is_lt, 30000.0, OP.mult)
+                tt(m, m, ("trash",), OP.min)
+                tt(m, m, ("vt",) + r, OP.max)
+                tc("v", ("vo",) + r, m)
+            else:
+                ts(("mt",) + r, cn(c), 8.5, OP.is_ge)
+
+        def S(a, b):
+            w, o, i = ("w2",), ("vo", 16 * a, 16 * b), ("cst", 0, 256 * (b - a))
+            op("s", lambda: g.scalar.activation(ap(w).indirect(ap(o)), ap(i), AF.Sigmoid), [o, i], [w])
+
+        def V(a, b):
+            sca(("w1",), ("vo", 16 * a, 16 * b), ("ones", 0, 256 * (b - a)))
+
+        def F():
+            tc("s", ("c2b",), ("w2", 2 * P, ST))
+            i = ("ident",)
+            sums(("psB", 0, NB), [(i, ("c2b", 0, 768, 2)), (i, ("c2b", 1, 768, 2)), (i, ("w1", 2 * P, ST, 2)), (i, ("w1", 2 * P + 1, ST, 2))])
+            tc("v", ("fsend",), ("psB", 0, NB))
+            send("f%d" % s, "fsend", "L%d" % s, 0, -1)
+
+        def N(c):
+            i, o = ("cb", 1024 * c, 1024 * c + 1024), ("scn", 1024 * c, 1024 * c + 1024)
+            op("v", lambda: g.vector.tensor_tensor_scan(ap(o), ap(("d0",)), ap(i), 191.0, OP.max, OP.min), [i, ("d0",)], [o])
+
+        def H():
+            sums(("psB", 0, 256), [(("hI",), ("xm%d" % s,)), (("qI",), ("ones", 0, 256)), (("hI",), ("scn", 15, 4096, 16))])
+            tc("v", ("hi",), ("psB", 0, 256))
+
+        def Bm(k):
+            mm(("psA", 128 * k, 128 * k + 128), ("B",), ("mt", 128 * k, 128 * k + 128), True, True)
+
+        def D(k):
+            r = (128 * k, 128 * k + 128)
+            m = ("psA", 256 + 128 * k, 384 + 128 * k)
+            ts(m, ("psA",) + r, 1.5, OP.is_ge, 255.0, OP.mult)
+            tt((wn,) + r, ("hi",) + r, m, OP.max)
+
+        def U():
+            a = YO + BS * s
+            gat("s", (ot, a + 256, a + 512), (wn, 0, YO + P), ("sb16_%d" % s, 16, 32))
+            gat("v", (ot, a, a + 256), (wn, 0, YO + P), ("sb16_%d" % s, 0, 16))
+
+        def Y():
+            w = (ot, YO, YO + P)
+            gat("s", ("ysend", 192, 384), w, ("snd16", 12, 24))
+            gat("v", ("ysend", 0, 192), w, ("snd16", 0, 12))
+            send("b%d" % s, "ysend", ot, YO + P, 1)
+            r = (YO + BS * s, YO + BS * s + BS)
+            dma("y", "o%d" % s, [(T.yv[:, BS * s:BS * s + BS], ap((ot,) + r))], [(ot,) + r], [])
+            if s == 2:
+                dma("y", "cy", [(ap((wn,) + r), ap((ot,) + r))], [(ot,) + r], [(wn,) + r])
+
+        def Tk():
+            tc("s", ("xT%d" % s,), ("psA", 0, 256))
+
+        def ck():
+            offsets(s, 128, 256)
+
+        def Q():
+            ts(("vt",), ("comp", 0, CAP), 8, OP.arith_shift_right)
+
+        def R():
+            w, o, i = ("w1", 0, 2 * P), ("tmpR",), ("L2", 0, NB)
+            op("v", lambda: g.vector.tensor_tensor(ap(o), ap(w).indirect(ap(("snd2",))), ap(i), OP.add), [w, i, ("snd2",)], [o])
+            sca(w, ("snd2",), o)
+            dma("y", "bl1", [(T.w1blk[b::16, :], T.w1[b::16, 672 * b:672 * b + 672]) for b in range(16)], [w], [("w1blk",)])
+
+        def M():
+            gat("s", ("memrep", BS * s, BS * s + BS), ("mw",), ("sb16_%d" % s,))
+            if s == 2:
+                dma("y", "bl2", [(T.w2blk[b::16, :], T.w2[b::16, 672 * b:672 * b + 672]) for b in range(16)], [("w2", 0, 2 * P)], [("w2blk",)])
+                dma("y", "blm", [(T.memblk[b::16, 0:min(336, 1536 - 336 * b)], T.memrep[b::16, 336 * b:min(1536, 336 * b + 336)])
+                                 for b in range(5)], [("memrep",)], [("memblk",)])
+
+        def W():
+            tc("s", ("w2bb",), ("w2blk",))
+        return {"G": G, "g": gs, "v": gv, "X": X, "A": A, "L": L, "C": C, "P": Pt, "S": S, "V": V, "F": F, "N": N, "H": H,
+                "B": Bm, "D": D, "U": U, "Y": Y, "T": Tk, "c": ck, "Q": Q, "R": R, "M": M, "W": W}
+
+    streams = {n: stream(n) for n in ("f0", "f1", "f2", "b2", "b1", "b0")}
+
+    def play(key):
+        for part in SCHED[key].split(";"):
+            words = part.split()
+            for w in words[1:]:
+                streams[words[0]][w[0]](*[int(a) for a in w[1:].split("-") if a])
+
+    h = P // 2
+    dma("y", "xa", [(T.xw[:, 0:h], T.x[:, 0:h])], [], [("xw", 0, h)])
+    dma("s", "snd", [(T.snd32[:, :], T.snd[:, :])], [], [("snd32",)])
+    dma("s", "xb", [(T.xw[:, h:P], T.x[:, h:P])], [], [("xw", h, P)])
+    fill(("sdrep",), 0.0)
+    fill(("ones",), 1.0)
+    fill(("neg",), -1.0)
+    fill(("sdblk",), 0.0)
+    dma("y", "sd", [(T.sdrep[0::16, :], T.sd[:, :])], [], [("sdrep",)])
+    dma("y", "cd0", [(T.cdt[:, 0:BS], T.cd[:, 0:BS])], [], [("cdt", 0, BS)])
+    dma("y", "tl", [(T.tlb[:, :], T.tl[:, :])], [], [("tlb",)])
+    dma("y", "sk", [(T.sdblk[0::16, :], T.sd[:, 0:336]), (T.sdblk[1::16, 0:BS - 336], T.sd[:, 336:BS])], [], [("sdblk",)])
+    dma("y", "cd1", [(T.cdt[:, BS:3 * BS], T.cd[:, BS:3 * BS])], [], [("cdt", BS, 3 * BS)])
+
+    sel(("B",), ("ones", 0, 128), [[-16, 8], [0, 16]], OP.is_ge, 0.0, 0, 1)
+    sel(("B",), ("B",), [[16, 8], [0, 16]], OP.is_ge, 0.0, 15, -1)
+    iota(("itp",), [[0, 64]], 0, 1)
+    iota(("it3",), [[16, 32]], BS, 0)
+    sel(("A1",), ("neg",), [[16, 8], [0, 16]], OP.is_ge, 0.0, 15, -1)
+    sel(("A1",), ("A1",), [[-1, 128]], OP.is_gt, 0.0, 0, 1)
+    sel(("A1",), ("A1",), [[-1, 128]], OP.not_equal, -(BIG + 1), 0, 1)
+    sel(("ident",), ("ones", 0, 128), [[-1, 128]], OP.is_equal, 0.0, 0, 1)
+    iota(("it2",), [[16, 64]], ST, 0)
+
+    act(("warm",), ("ones", 0, 8), AF.Sigmoid)
+    for a in (0, 1024):
+        act(("R", a, a + 1024), ("ones",), AF.Copy, scale=-1.0)
+    for a in range(0, ZS, 1024):
+        act(("w2", a, a + 1024), ("ones",), AF.Copy, scale=0.0)
+
+    fill(("C",), 0.0)
+    fill(("w1", 0, 3072), 0.0)
+    for q in range(8):
+        tc("v", ("C", 16 * q, 16 * q + 129 * 15 + 1, 129), ("B", 16 * q, 16 * q + 16))
+    fill(("one32",), 1.0)
+    ts(("itp",), ("itp",), 15, OP.bitwise_and)
+    tt(("t512",), ("it3",), ("itp", 0, 32), OP.add)
+    fill(("comp", 0, CAP), 255)
+    tc("v", ("snd16",), ("snd32",))
+    fill(("w1", 3072, ZV), 0.0)
+
+    gat("v", ("xsend",), ("xw", 0, P), ("snd16",))
+    send("x", "xsend", "xw", P, 1)
+    sel(("R",), ("R",), [[-1, 128], [0, 16]], OP.is_equal, 0.0, 0, 1)
+    iota(("cst",), [[0, 1024]], 30, 0)
+    iota(("io384",), [[1, NB]], -NB // 2, 0)
+    iota(("bw",), [[0, P]], NB // 2, 0)
+    sums(("psA", 0, 32), [(cmat(r), ("sdrep", r, BS, 16)) for r in range(16)])
+    pack(0)
+    lists(0)
+    streams["f0"]["Q"]()
+    tt(("trash",), ("it2",), ("itp",), OP.add)
+    need("y", [("rs_x", total["rs_x"])])
+    dma("y", "zz", [(T.w2[:, ZS:ST], T.w2[:, 0:ST - ZS])], [("w2", 0, ST - ZS)], [("w2", ZS, ST)])
+    dma("y", "zv", [(T.w1[:, ZV:ST], T.w1[:, 0:ST - ZV])], [("w1", 0, ST - ZV)], [("w1", ZV, ST)])
+    dma("y", "ya", [(T.ya[:, YO:YO + P], T.y0[:, :])], [], [("ya", YO, YO + P)])
+    dma("y", "yb", [(T.yb[:, YO:YO + P], T.y0[:, :])], [], [("yb", YO, YO + P)])
+
+    play("out0")
+    own_flags(1)
+    for s in range(3):
+        ts(("vs%d" % s,), ("t512",), float(512 * s - 256), OP.add)
+    pack(1)
+    sca(("bw",), ("snd16",), ("io384",))
+    sums(("psB", 0, 64), [(cmat(r), ("bw", BS + r, 3 * BS, 16)) for r in range(16)])
+    slots(0)
+    ts(("binv",), ("psB", 0, 64), 1.0 / 16, OP.mult, float(NB // 2), OP.add)
+    fill(("L0", NB, 400), 0.0)
+    fill(("comp", 0, CAP), 255)
+    gat("s", ("ysend",), ("ya", YO, YO + P), ("snd16",))
+    their_flags(1)
+    need("g", [("rs_f0", total["rs_f0"])])
+    send("y", "ysend", "ya", YO + P, 1)
+    lists(1)
+    streams["f1"]["Q"]()
+    play("out1")
+    own_flags(2)
+    slots(1)
+    pack(2)
+    fill(("comp", 0, CAP), 255)
+    fill(("L1", NB, 400), 0.0)
+    fill(("d0",), 0.0)
+    fill(("d0", 0, 1024, 16), 191.0)
+    ts(("hI",), ("ident",), 0.5, OP.mult)
+    ts(("qI",), ("ident",), -0.25, OP.mult)
+    fill(("mw", 0, CAP), 1.0)
+    fill(("mw", CAP, CAP + 1536), 0.0)
+    fill(("memblk",), 0.0)
+    ts(("snd2i",), ("snd32",), 2, OP.mult)
+    tc("v", ("snd2",), ("snd2i",))
+    streams["f0"]["M"]()
+    streams["f1"]["M"]()
+    their_flags(2)
+    lists(2)
+    play("back2a") if "back2a" in SCHED else slots(2)
+    play("back2")
+    play("gap1")
+    play("back1")
+    play("gap0")
+    play("back0")
+    dma("y", "o0", [(T.yv[:, 0:BS], T.yb[:, YO:YO + BS])], [("yb", YO, YO + BS)], [])
+    i = ("ident",)
+    sums(("psB", 0, 336), [(i, ("sdblk",)), (i, ("w2bb", 0, 672, 2)), (i, ("w2bb", 1, 672, 2)), (i, ("w1blk", 0, 672, 2)), (i, ("w1blk", 1, 672, 2))])
+    ts(("psB", 0, 336), ("psB", 0, 336), 0.25, OP.is_gt)
+    tt(("yfb",), ("psB", 0, 336), ("memblk",), OP.add)
+    dma("s", "of", [(T.yf[:, :], T.yfb[:, :])], [("yfb",)], [])
+    need("g", list(total.items()))
+    for s, n in total.items():
+        if s != "qg" and known["g"].get(s, 0) < n:
+            g.wait_ge(T.sem[s], n)

@@ -4,71 +4,79 @@ from concourse.mybir import AluOpType as OP, ActivationFunctionType as AF
 P, PL, NB, BS, CAP, BK = 5376, 5760, 384, 512, 256, 128
 ST = 2 * PL
 WW = ST + 1024
-ZV, ZS = 6144, 9216
-BIG = 1023.0
+BIG = 1024.0
+CS = 32768.0
+FAR = 7.5 * CS
+RND = 12582912.0
 YO = CAP
-SPLITF, SPLITB = (40, 40, 40, 40), (30, 30, 34, 44)
+FB = P // 16
+TAG = [""]
 
-BT = " G2 X1 N0 L0 A1 G3 N1 C0 X2 L1 A2 P0 N2 C1 X3 L2 A3 "
-BE = " P1 B0 N3 C2 H L3 D0 P2 C3 P3 B1 D1 U "
-FT = " G0 T c G1 X0 A0 G2 X1 L0 A1 G3 C0 X2 L1 A2 P0 C1 X3 L2 A3 P1 C2 S0-4 S4-8 P2 V8-10 L3 C3 V10-12 P3 V12-16 F"
+FT = (" s0-32 c s64-104 m v32-64 X0 v104-128 s128-192 X1 L0 Q C0 s192-256 L1 X2 C1 P0 X3 L2 S0-64 C2 L3 S64-128 C3 P1"
+      " S128-144 V144-200 V200-256 F")
+BT = " X0 s128-192 X1 L0 N0 C0 s192-256 L1 N1 X2 C1 X3 L2 C2 P0 N2 B0 H0 "
+BE = " N3 L3 C3 D0 H1 P1 B1 D1 U "
 SCHED = {
     "out0": "f0" + FT,
     "out1": "f1" + FT,
-    "back2": "b2 G0 T c G1 X0 A0" + BT + "; f2 g0 g1 ; b2" + BE + "Y",
-    "gap1": "f2 Q v0 v1 X0 A0 G2 X1 L0 A1 G3 C0 X2 L1 A2 P0 C1 X3 ; b1 g0 ; f2 L2 A3 P1 C2 ; b1 v0 g1 ; f2 L3 P2 C3 ; b1 v1 ; f2 P3",
-    "back1": "b1 X0 A0" + BT + "; f2 S0-2 ; b1" + BE + "Y",
-    "gap0": "f2 S2-6 S6-8 V8-12 V12-16 F M",
-    "back0": "b0 G0 G1 X0 A0" + BT + "W R" + BE,
+    "back2a": "b2 s0-32 c s64-128 m v32-64",
+    "back2": "b2" + BT + "; f2 s0-64 s64-128 s128-192; b2" + BE + "Y",
+    "gap1": "f2 Q X0 s192-256 X1 L0 C0 L1 X2 C1 P0 X3 L2 S0-32 S32-56 C2 L3 C3 P1 ; b1 s0-32 v32-64 s64-128",
+    "back1": "b1" + BT + "; f2 S56-88 S88-120 ; b1" + BE + "Y",
+    "gap0": "f2 S120-176 V176-216 V216-256 F M",
+    "back0": "b0 s0-32 v32-64 s64-128" + BT + "W R N3 L3 C3 D0 H1 P1 B1 D1",
+    "end0": "b0 U",
 }
 
 SCRATCH = {
     "xw": ("sbuf", [128, PL], "bfloat16"),
     "ya": ("sbuf", [128, YO + PL], "bfloat16"), "yb": ("sbuf", [128, YO + PL], "bfloat16"),
     "cdt": ("sbuf", [128, 1536], "int32"), "comp": ("sbuf", [128, 1024], "int32"),
-    "snd32": ("sbuf", [128, 24], "int32"), "snd16": ("sbuf", [128, 24], "uint16"), "snd2": ("sbuf", [128, 24], "uint16"),
-    "snd2i": ("sbuf", [128, 24], "int32"),
-    "ci": ("sbuf", [128, 256], "int32"), "xi": ("sbuf", [128, 256], "int32"), "vt": ("sbuf", [128, 256], "int32"),
+    "snd32": ("sbuf", [128, 24], "int32"), "snd16": ("sbuf", [128, 24], "uint16"),
+    "xi": ("sbuf", [128, 256], "int32"), "vt": ("sbuf", [128, 256], "int32"),
     "cf": ("sbuf", [128, 4096], "bfloat16"), "cb": ("sbuf", [128, 4096], "bfloat16"),
     "scn": ("sbuf", [128, 4096], "bfloat16"),
     "d0": ("sbuf", [128, 1024], "bfloat16"), "mt": ("sbuf", [128, 256], "bfloat16"), "hi": ("sbuf", [128, 256], "int32"),
-    "vo": ("sbuf", [128, 256], "uint16"), "trash": ("sbuf", [128, 64], "float32"),
-    "w1": ("sbuf", [128, WW], "bfloat16"), "w2": ("sbuf", [128, WW], "float32"),
+    "vo": ("sbuf", [128, 256], "uint16"), "trash": ("sbuf", [128, 128], "float32"),
+    "w1": ("sbuf", [128, WW], "bfloat16"), "w2": ("sbuf", [128, WW], "float32"), "w3": ("sbuf", [128, P], "bfloat16"),
+    "zb": ("sbuf", [128, 2 * FB], "bfloat16"), "zf": ("sbuf", [128, 2 * FB], "float32"),
     "ones": ("sbuf", [128, 1024], "bfloat16"), "cst": ("sbuf", [128, 1024], "float32"),
-    "C": ("sbuf", [128, 2048], "bfloat16"), "R": ("sbuf", [128, 2048], "bfloat16"), "neg": ("sbuf", [128, 128], "bfloat16"),
-    "ident": ("sbuf", [128, 128], "bfloat16"), "B": ("sbuf", [128, 128], "bfloat16"), "A1": ("sbuf", [128, 128], "bfloat16"),
+    "C": ("sbuf", [128, 2048], "bfloat16"),
+    "ident": ("sbuf", [128, 128], "bfloat16"), "B": ("sbuf", [128, 128], "bfloat16"),
+    "A": ("sbuf", [128, 128], "bfloat16"), "nA": ("sbuf", [128, 128], "bfloat16"),
+    "dS": ("sbuf", [128, 128], "bfloat16"), "dN": ("sbuf", [128, 128], "bfloat16"),
     "hI": ("sbuf", [128, 128], "bfloat16"), "qI": ("sbuf", [128, 128], "bfloat16"),
-    "sdrep": ("sbuf", [128, 512], "bfloat16"), "sdblk": ("sbuf", [128, 336], "bfloat16"),
+    "sdrep": ("sbuf", [128, 512], "bfloat16"), "sdblk": ("sbuf", [128, FB], "bfloat16"),
     "L0": ("sbuf", [128, 400], "bfloat16"), "L1": ("sbuf", [128, 400], "bfloat16"), "L2": ("sbuf", [128, 400], "bfloat16"),
     "Lg": ("sbuf", [128, 512], "bfloat16"), "fsend": ("sbuf", [128, NB], "bfloat16"),
     "xsend": ("sbuf", [128, NB], "bfloat16"), "ysend": ("sbuf", [128, NB], "bfloat16"),
     "bw": ("sbuf", [128, P], "bfloat16"), "io384": ("sbuf", [128, NB], "bfloat16"), "binv": ("sbuf", [128, 64], "uint16"),
     "c2b": ("sbuf", [128, 768], "bfloat16"), "c2w": ("sbuf", [128, 1024], "bfloat16"),
-    "tlb": ("sbuf", [128, 1], "bfloat16"), "warm": ("sbuf", [128, 8], "float32"),
-    "flw": ("sbuf", [128, 32], "bfloat16"), "one32": ("sbuf", [128, 32], "float32"), "sc32": ("sbuf", [128, 32], "float32"),
+    "tlb": ("sbuf", [128, 1], "bfloat16"), "tlf": ("sbuf", [128, 1], "float32"), "rec": ("sbuf", [128, 1], "float32"),
+    "warm": ("sbuf", [128, 8], "float32"),
+    "flw": ("sbuf", [128, 33], "bfloat16"), "one32": ("sbuf", [128, 32], "float32"),
     "pp": ("sbuf", [128, 32], "float32"), "sl": ("sbuf", [128, 32], "float32"), "sl16": ("sbuf", [128, 32], "uint16"),
     "zz": ("sbuf", [128, 32], "float32"), "t512": ("sbuf", [128, 32], "float32"),
-    "itp": ("sbuf", [128, 64], "int32"), "it2": ("sbuf", [128, 64], "int32"), "it3": ("sbuf", [128, 32], "int32"),
+    "itp": ("sbuf", [128, 128], "int32"), "it2": ("sbuf", [128, 128], "int32"), "it3": ("sbuf", [128, 32], "int32"),
     "mw": ("sbuf", [128, CAP + 1536], "bfloat16"), "memrep": ("sbuf", [128, 1536], "bfloat16"),
-    "memblk": ("sbuf", [128, 336], "bfloat16"), "w1blk": ("sbuf", [128, 672], "bfloat16"),
-    "w2blk": ("sbuf", [128, 672], "float32"), "w2bb": ("sbuf", [128, 672], "bfloat16"),
-    "tmpR": ("sbuf", [128, NB], "bfloat16"), "yfb": ("sbuf", [128, 336], "bfloat16"),
-    "psd0": ("psum", [128, 1024], "float32"), "psd1": ("psum", [128, 1024], "float32"),
+    "memblk": ("sbuf", [128, FB], "bfloat16"), "w1blk": ("sbuf", [128, 2 * FB], "bfloat16"),
+    "w2blk": ("sbuf", [128, 2 * FB], "float32"), "w2bb": ("sbuf", [128, 2 * FB], "bfloat16"),
+    "w3blk": ("sbuf", [128, FB], "bfloat16"), "yfb": ("sbuf", [128, FB], "bfloat16"),
     "cnt0": ("psum", [128, 512], "float32"), "cnt1": ("psum", [128, 512], "float32"),
     "psA": ("psum", [128, 512], "float32"), "psB": ("psum", [128, 512], "float32"),
 }
 for _s in range(3):
     SCRATCH["c16_%d" % _s] = ("sbuf", [128, 256], "uint16")
     SCRATCH["xm%d" % _s] = ("sbuf", [128, 256], "bfloat16")
-    SCRATCH["xT%d" % _s] = ("sbuf", [128, 256], "bfloat16")
     SCRATCH["sb16_%d" % _s] = ("sbuf", [128, 32], "uint16")
     SCRATCH["vs%d" % _s] = ("sbuf", [128, 32], "float32")
-    SCRATCH["ab%d" % _s] = ("sbuf", [128, 1024], "bfloat16")
-    SCRATCH["nr%d" % _s] = ("sbuf", [128, 1024], "bfloat16")
+for _s in range(4):
+    SCRATCH["nr%d" % _s] = ("sbuf", [128, 512], "bfloat16")
+    SCRATCH["pd%d" % _s] = ("psum", [128, 512], "float32")
 
 _EX = ["x", "f0", "y", "f1", "b2", "f2", "b1"]
-_DM = ["snd", "xa", "xb", "tl", "sd", "cd0", "cd1", "sk", "zz", "zv", "ya", "yb", "bl1", "bl2", "blm", "cy", "o2", "o1",
-       "o0", "of"]
+_DM = ["snd", "xa", "xb", "tl", "sd", "cd0", "cd1", "sk", "z1", "z2", "z3", "ya", "yb", "bl1", "bl2", "bl3", "blm", "cy",
+       "o2", "o1", "o0", "of"]
 SEMAPHORES = ["qv", "qs", "qt", "qg"] + ["ls_" + e for e in _EX] + ["rs_" + e for e in _EX] + ["d_" + d for d in _DM]
 
 
@@ -181,10 +189,15 @@ def rank_program(g, core, T, topo):
         op("v", lambda: g.vector.tensor_tensor(ap(o), ap(a), ap(b), f), [a, b], [o])
 
     def ts(o, a, s1, f1, s2=None, f2=None):
+        cols = [s for s in (s1, s2) if isinstance(s, tuple)]
+        s1, s2 = [ap(s) if isinstance(s, tuple) else s for s in (s1, s2)]
         if f2 is None:
-            op("v", lambda: g.vector.tensor_scalar(ap(o), ap(a), s1, None, f1), [a], [o])
+            op("v", lambda: g.vector.tensor_scalar(ap(o), ap(a), s1, None, f1), [a] + cols, [o])
         else:
-            op("v", lambda: g.vector.tensor_scalar(ap(o), ap(a), s1, s2, f1, f2), [a], [o])
+            op("v", lambda: g.vector.tensor_scalar(ap(o), ap(a), s1, s2, f1, f2), [a] + cols, [o])
+
+    def scan(o, d0, d1, first, f0, f1):
+        op("v", lambda: g.vector.tensor_tensor_scan(ap(o), ap(d0), ap(d1), first, f0, f1), [d0, d1], [o])
 
     def fill(o, c):
         op("v", lambda: g.vector.memset(ap(o), c), [], [o])
@@ -235,30 +248,26 @@ def rank_program(g, core, T, topo):
     def cmat(r):
         return ("C", 128 * r, 128 * r + 128)
 
+    def blocks(blk, win, n):
+        return [(T[blk][b::16, :], T[win][b::16, n * b:n * b + n]) for b in range(16)]
+
     def pack(s):
         r = ("cdt", BS * s, BS * s + BS)
         ts(r, r, 256, OP.mult)
         tt(r, r, ("xw", BS * s, BS * s + BS), OP.add)
 
     def offsets(s, a, b):
-        ts(("ci", a, b), ("comp", a, b), 9, OP.arith_shift_right)
-        tc("v", ("c16_%d" % s, a, b), ("ci", a, b))
+        ts(("c16_%d" % s, a, b), ("comp", a, b), 1.0 / 512, OP.mult, -0.44, OP.add)
 
     def lists(s):
-        ts(("flw",), ("psA", 0, 32), 0.25, OP.is_gt)
-        mm(("psB", 0, 32), ("B",), ("flw",), True, True)
-        mm(("psB", 32, 64), ("A1",), ("flw",), True, True)
-        op("v", lambda: g.vector.tensor_tensor_scan(ap(("sc32",)), ap(("one32",)), ap(("psB", 0, 32)), BIG, OP.mult, OP.add),
-           [("one32",), ("psB", 0, 32)], [("sc32",)])
-        tt(("pp",), ("psB", 32, 64), ("sc32",), OP.add)
+        now, was = ("flw", 1, 33), ("flw", 0, 32)
+        ts(now, ("psA", 0, 32), 0.25, OP.is_gt)
+        sums(("psB", 0, 32), [(("A",), now), (("B",), was), (("nA",), was)])
+        scan(("pp",), ("one32",), ("psB", 0, 32), BIG, OP.mult, OP.add)
         tt(("sl",), ("pp",), ("t512",), OP.min)
         tc("v", ("sl16",), ("sl",))
         sca(("comp",), ("sl16",), ("cdt", BS * s, BS * s + BS))
-        offsets(s, 0, 128)
-        ts(("xi",), ("comp", 0, CAP), 255, OP.bitwise_and)
-        tc("v", ("xm%d" % s,), ("xi",))
-        for k in range(2):
-            mm(("psA", 128 * k, 128 * k + 128), ("xm%d" % s, 128 * k, 128 * k + 128), ("ident",), True, True)
+        offsets(s, 0, 64)
 
     def slots(s):
         ts(("zz",), ("pp",), 255.5, OP.is_gt, 8192.0, OP.mult)
@@ -284,62 +293,47 @@ def rank_program(g, core, T, topo):
 
     def stream(name):
         s, out = int(name[1]), name[0] == "f"
-        wn, w0, cand, split = ("xw", 0, "cf", SPLITF) if out else (("ya", "yb")[s % 2], YO, "cb", SPLITB)
+        wn, w0, cand = ("xw", 0, "cf") if out else (("ya", "yb")[s % 2], YO, "cb")
         ot = ("yb", "ya")[s % 2]
-        win, off = (wn, w0, w0 + PL), "c16_%d" % s
+        win, off, xm = (wn, w0, w0 + PL), "c16_%d" % s, "xm%d" % s
 
-        def gs(c):
-            k, j, n = 64 * c, 1024 * c, split[c]
-            gat("s", (cand, j + 16 * n, j + 1024), win, (off, k + n, k + 64))
+        def gs(a, b):
+            gat("s", (cand, 16 * a, 16 * b), win, (off, a, b))
 
-        def gv(c):
-            k, j, n = 64 * c, 1024 * c, split[c]
-            gat("v", (cand, j, j + 16 * n), win, (off, k, k + n))
-
-        def G(c):
-            gs(c)
-            gv(c)
+        def gv(a, b):
+            gat("v", (cand, 16 * a, 16 * b), win, (off, a, b))
 
         def X(c):
-            ps, hf = "psd%d" % (c % 2), c // 2
-            for b in range(2):
-                q = (2 * c + b) % 4
-                mm((ps, 512 * b, 512 * b + 512), ("xT%d" % s, 128 * hf, 128 * hf + 128), ("R", 512 * q, 512 * q + 512), True, False)
-            for b in range(2):
-                j = 1024 * c + 512 * b
-                mm((ps, 512 * b, 512 * b + 512), ("ident",), (cand, j, j + 512), False, True)
-
-        def A(c):
-            act(("ab%d" % (c % 3),), ("psd%d" % (c % 2),), AF.Abs)
+            for i in range(16):
+                k = 64 * (i % 8)
+                sums(("pd%d" % (2 * (c % 2) + i // 8), k, k + 64),
+                     [(("dN",), (xm, 64 * c, 64 * c + 64)), (("dS",), (cand, 1024 * c + i, 1024 * c + 1024, 16))])
 
         def L(c):
-            o, i = ("nr%d" % (c % 3),), ("ab%d" % (c % 3),)
-            op("v", lambda: g.vector.tensor_scalar(ap(o), ap(i), ap(("tlb",)), None, OP.is_le), [i, ("tlb",)], [o])
-
-        def cn(c, at=0):
-            k = at + 64 * (c // 2)
-            return ("cnt%d" % (c % 2), k, k + 64)
+            for b in (2 * (c % 2), 2 * (c % 2) + 1):
+                ts(("nr%d" % b,), ("pd%d" % b,), RND, OP.add, RND, OP.not_equal)
 
         def C(c):
-            sums(cn(c), [(cmat(i), ("nr%d" % (c % 3), i, 1024, 16)) for i in range(16)])
+            k = 64 * (c % 2)
+            sums(("cnt%d" % (c // 2), k, k + 64),
+                 [(cmat(i), ("nr%d" % (2 * (c % 2) + i // 8), 64 * (i % 8), 64 * (i % 8) + 64)) for i in range(16)])
 
-        def Pt(c):
-            r = (64 * c, 64 * c + 64)
+        def Pt(h):
+            r, cn = (128 * h, 128 * h + 128), ("cnt%d" % h, 0, 128)
             if out:
-                m = cn(c, 256)
-                ts(m, cn(c), 8.5, OP.is_lt, 30000.0, OP.mult)
+                m = ("cnt%d" % h, 128, 256)
+                tt(m, cn, ("vt",) + r, OP.max)
                 tt(m, m, ("trash",), OP.min)
-                tt(m, m, ("vt",) + r, OP.max)
-                tc("v", ("vo",) + r, m)
+                ts(("vo",) + r, m, -FAR, OP.add)
             else:
-                ts(("mt",) + r, cn(c), 8.5, OP.is_ge)
+                ts(("mt",) + r, cn, FAR, OP.is_lt)
 
         def S(a, b):
-            w, o, i = ("w2",), ("vo", 16 * a, 16 * b), ("cst", 0, 256 * (b - a))
+            w, o, i = ("w2",), ("vo", a, b), ("cst", 0, 16 * (b - a))
             op("s", lambda: g.scalar.activation(ap(w).indirect(ap(o)), ap(i), AF.Sigmoid), [o, i], [w])
 
         def V(a, b):
-            sca(("w1",), ("vo", 16 * a, 16 * b), ("ones", 0, 256 * (b - a)))
+            sca(("w1",), ("vo", a, b), ("ones", 0, 16 * (b - a)))
 
         def F():
             tc("s", ("c2b",), ("w2", 2 * P, ST))
@@ -349,12 +343,12 @@ def rank_program(g, core, T, topo):
             send("f%d" % s, "fsend", "L%d" % s, 0, -1)
 
         def N(c):
-            i, o = ("cb", 1024 * c, 1024 * c + 1024), ("scn", 1024 * c, 1024 * c + 1024)
-            op("v", lambda: g.vector.tensor_tensor_scan(ap(o), ap(("d0",)), ap(i), 191.0, OP.max, OP.min), [i, ("d0",)], [o])
+            scan(("scn", 1024 * c, 1024 * c + 1024), ("d0",), ("cb", 1024 * c, 1024 * c + 1024), 191.0, OP.max, OP.min)
 
-        def H():
-            sums(("psB", 0, 256), [(("hI",), ("xm%d" % s,)), (("qI",), ("ones", 0, 256)), (("hI",), ("scn", 15, 4096, 16))])
-            tc("v", ("hi",), ("psB", 0, 256))
+        def H(k):
+            r = (128 * k, 128 * k + 128)
+            sums(("psB",) + r, [(("hI",), (xm,) + r), (("qI",), ("ones",) + r), (("hI",), ("scn", 2048 * k + 15, 2048 * k + 2048, 16))])
+            tc("v", ("hi",) + r, ("psB",) + r)
 
         def Bm(k):
             mm(("psA", 128 * k, 128 * k + 128), ("B",), ("mt", 128 * k, 128 * k + 128), True, True)
@@ -380,32 +374,32 @@ def rank_program(g, core, T, topo):
             if s == 2:
                 dma("y", "cy", [(ap((wn,) + r), ap((ot,) + r))], [(ot,) + r], [(wn,) + r])
 
-        def Tk():
-            tc("s", ("xT%d" % s,), ("psA", 0, 256))
-
         def ck():
-            offsets(s, 128, 256)
+            offsets(s, 64, 256)
+
+        def marks():
+            ts(("xi",), ("comp", 0, CAP), 255, OP.bitwise_and)
+            tc("v", (xm,), ("xi",))
 
         def Q():
-            ts(("vt",), ("comp", 0, CAP), 8, OP.arith_shift_right)
+            ts(("vt",), ("comp", 0, CAP), 1.0 / 256, OP.mult, FAR - 0.375, OP.add)
 
         def R():
-            w, o, i = ("w1", 0, 2 * P), ("tmpR",), ("L2", 0, NB)
-            op("v", lambda: g.vector.tensor_tensor(ap(o), ap(w).indirect(ap(("snd2",))), ap(i), OP.add), [w, i, ("snd2",)], [o])
-            sca(w, ("snd2",), o)
-            dma("y", "bl1", [(T.w1blk[b::16, :], T.w1[b::16, 672 * b:672 * b + 672]) for b in range(16)], [w], [("w1blk",)])
+            sca(("w3",), ("snd16",), ("L2", 0, NB))
+            dma("y", "bl3", blocks("w3blk", "w3", FB), [("w3",)], [("w3blk",)])
 
         def M():
             gat("s", ("memrep", BS * s, BS * s + BS), ("mw",), ("sb16_%d" % s,))
             if s == 2:
-                dma("y", "bl2", [(T.w2blk[b::16, :], T.w2[b::16, 672 * b:672 * b + 672]) for b in range(16)], [("w2", 0, 2 * P)], [("w2blk",)])
-                dma("y", "blm", [(T.memblk[b::16, 0:min(336, 1536 - 336 * b)], T.memrep[b::16, 336 * b:min(1536, 336 * b + 336)])
+                dma("y", "bl2", blocks("w2blk", "w2", 2 * FB), [("w2", 0, 2 * P)], [("w2blk",)])
+                dma("y", "bl1", blocks("w1blk", "w1", 2 * FB), [("w1", 0, 2 * P)], [("w1blk",)])
+                dma("y", "blm", [(T.memblk[b::16, 0:min(FB, 1536 - FB * b)], T.memrep[b::16, FB * b:min(1536, FB * b + FB)])
                                  for b in range(5)], [("memrep",)], [("memblk",)])
 
         def W():
             tc("s", ("w2bb",), ("w2blk",))
-        return {"G": G, "g": gs, "v": gv, "X": X, "A": A, "L": L, "C": C, "P": Pt, "S": S, "V": V, "F": F, "N": N, "H": H,
-                "B": Bm, "D": D, "U": U, "Y": Y, "T": Tk, "c": ck, "Q": Q, "R": R, "M": M, "W": W}
+        return {"s": gs, "v": gv, "X": X, "L": L, "C": C, "P": Pt, "S": S, "V": V, "F": F, "N": N, "H": H,
+                "B": Bm, "D": D, "U": U, "Y": Y, "m": marks, "c": ck, "Q": Q, "R": R, "M": M, "W": W}
 
     streams = {n: stream(n) for n in ("f0", "f1", "f2", "b2", "b1", "b0")}
 
@@ -413,114 +407,118 @@ def rank_program(g, core, T, topo):
         for part in SCHED[key].split(";"):
             words = part.split()
             for w in words[1:]:
+                TAG[0] = words[0] + w
                 streams[words[0]][w[0]](*[int(a) for a in w[1:].split("-") if a])
+        TAG[0] = ""
 
     h = P // 2
     dma("y", "xa", [(T.xw[:, 0:h], T.x[:, 0:h])], [], [("xw", 0, h)])
     dma("s", "snd", [(T.snd32[:, :], T.snd[:, :])], [], [("snd32",)])
     dma("s", "xb", [(T.xw[:, h:P], T.x[:, h:P])], [], [("xw", h, P)])
-    fill(("sdrep",), 0.0)
     fill(("ones",), 1.0)
-    fill(("neg",), -1.0)
+    fill(("sdrep",), 0.0)
     fill(("sdblk",), 0.0)
     dma("y", "sd", [(T.sdrep[0::16, :], T.sd[:, :])], [], [("sdrep",)])
     dma("y", "cd0", [(T.cdt[:, 0:BS], T.cd[:, 0:BS])], [], [("cdt", 0, BS)])
     dma("y", "tl", [(T.tlb[:, :], T.tl[:, :])], [], [("tlb",)])
-    dma("y", "sk", [(T.sdblk[0::16, :], T.sd[:, 0:336]), (T.sdblk[1::16, 0:BS - 336], T.sd[:, 336:BS])], [], [("sdblk",)])
-    dma("y", "cd1", [(T.cdt[:, BS:3 * BS], T.cd[:, BS:3 * BS])], [], [("cdt", BS, 3 * BS)])
 
     sel(("B",), ("ones", 0, 128), [[-16, 8], [0, 16]], OP.is_ge, 0.0, 0, 1)
     sel(("B",), ("B",), [[16, 8], [0, 16]], OP.is_ge, 0.0, 15, -1)
-    iota(("itp",), [[0, 64]], 0, 1)
+    iota(("itp",), [[0, 128]], 0, 1)
     iota(("it3",), [[16, 32]], BS, 0)
-    sel(("A1",), ("neg",), [[16, 8], [0, 16]], OP.is_ge, 0.0, 15, -1)
-    sel(("A1",), ("A1",), [[-1, 128]], OP.is_gt, 0.0, 0, 1)
-    sel(("A1",), ("A1",), [[-1, 128]], OP.not_equal, -(BIG + 1), 0, 1)
+    sel(("A",), ("B",), [[1, 128]], OP.is_gt, 0.0, 0, -1)
+    sel(("A",), ("A",), [[-1, 128]], OP.not_equal, -BIG, 0, 1)
     sel(("ident",), ("ones", 0, 128), [[-1, 128]], OP.is_equal, 0.0, 0, 1)
-    iota(("it2",), [[16, 64]], ST, 0)
+    iota(("it2",), [[0, 2], [16, 64]], ST + int(FAR), 0)
+    iota(("io384",), [[1, NB]], -NB // 2, 0)
 
     act(("warm",), ("ones", 0, 8), AF.Sigmoid)
-    for a in (0, 1024):
-        act(("R", a, a + 1024), ("ones",), AF.Copy, scale=-1.0)
-    for a in range(0, ZS, 1024):
-        act(("w2", a, a + 1024), ("ones",), AF.Copy, scale=0.0)
-
+    act(("zf",), ("ones", 0, 2 * FB), AF.Copy, scale=0.0)
+    for a, b in ((1024, 2048), (2048, 3072), (2 * P, ST)):
+        act(("w2", a, b), ("ones", 0, b - a), AF.Copy, scale=0.0)
+    act(("cst",), ("ones",), AF.Copy, scale=30.0)
     fill(("C",), 0.0)
-    fill(("w1", 0, 3072), 0.0)
+    fill(("zb",), 0.0)
+    fill(("w1", 1024, 3072), 0.0)
+    fill(("w1", 2 * P, ST), 0.0)
     for q in range(8):
-        tc("v", ("C", 16 * q, 16 * q + 129 * 15 + 1, 129), ("B", 16 * q, 16 * q + 16))
+        ts(("C", 16 * q, 16 * q + 129 * 15 + 1, 129), ("B", 16 * q, 16 * q + 16), CS, OP.mult)
     fill(("one32",), 1.0)
+    fill(("flw", 0, 1), 0.0)
     ts(("itp",), ("itp",), 15, OP.bitwise_and)
     tt(("t512",), ("it3",), ("itp", 0, 32), OP.add)
+    tt(("trash",), ("it2",), ("itp",), OP.add)
+    ts(("nA",), ("A",), -1.0, OP.mult)
     fill(("comp", 0, CAP), 255)
+    fill(("bw", BS, 3 * BS), float(NB // 2))
     tc("v", ("snd16",), ("snd32",))
-    fill(("w1", 3072, ZV), 0.0)
+    for s in range(3):
+        ts(("vs%d" % s,), ("t512",), float(512 * s - 256), OP.add)
+    fill(("L0", NB, 400), 0.0)
+    fill(("L1", NB, 400), 0.0)
+    ts(("hI",), ("ident",), 0.5, OP.mult)
+    ts(("qI",), ("ident",), -0.25, OP.mult)
+    fill(("d0",), 0.0)
+    fill(("d0", 0, 1024, 16), 191.0)
+    sca(("bw",), ("snd16",), ("io384",))
 
     gat("v", ("xsend",), ("xw", 0, P), ("snd16",))
     send("x", "xsend", "xw", P, 1)
-    sel(("R",), ("R",), [[-1, 128], [0, 16]], OP.is_equal, 0.0, 0, 1)
-    iota(("cst",), [[0, 1024]], 30, 0)
-    iota(("io384",), [[1, NB]], -NB // 2, 0)
-    iota(("bw",), [[0, P]], NB // 2, 0)
     sums(("psA", 0, 32), [(cmat(r), ("sdrep", r, BS, 16)) for r in range(16)])
     pack(0)
     lists(0)
-    streams["f0"]["Q"]()
-    tt(("trash",), ("it2",), ("itp",), OP.add)
+    ts(("tlf",), ("tlb",), 2.0, OP.mult, 1.0, OP.add)
+    op("v", lambda: g.vector.reciprocal(ap(("rec",)), ap(("tlf",))), [("tlf",)], [("rec",)])
+    ts(("dS",), ("ident",), ("rec",), OP.mult)
+    ts(("dN",), ("dS",), -1.0, OP.mult)
+    slots(0)
     need("y", [("rs_x", total["rs_x"])])
-    dma("y", "zz", [(T.w2[:, ZS:ST], T.w2[:, 0:ST - ZS])], [("w2", 0, ST - ZS)], [("w2", ZS, ST)])
-    dma("y", "zv", [(T.w1[:, ZV:ST], T.w1[:, 0:ST - ZV])], [("w1", 0, ST - ZV)], [("w1", ZV, ST)])
+    dma("y", "z2", [(i, T.zf[b::16, :]) for b, (o, i) in enumerate(blocks("w2blk", "w2", 2 * FB))], [("zf",)], [("w2", 0, 2 * P)])
+    dma("y", "z1", [(i, T.zb[b::16, :]) for b, (o, i) in enumerate(blocks("w1blk", "w1", 2 * FB))], [("zb",)], [("w1", 0, 2 * P)])
+    dma("y", "cd1", [(T.cdt[:, BS:3 * BS], T.cd[:, BS:3 * BS])], [], [("cdt", BS, 3 * BS)])
     dma("y", "ya", [(T.ya[:, YO:YO + P], T.y0[:, :])], [], [("ya", YO, YO + P)])
     dma("y", "yb", [(T.yb[:, YO:YO + P], T.y0[:, :])], [], [("yb", YO, YO + P)])
+    dma("y", "sk", [(T.sdblk[0::16, :], T.sd[:, 0:FB]), (T.sdblk[1::16, 0:BS - FB], T.sd[:, FB:BS])], [], [("sdblk",)])
+    dma("y", "z3", [(i, T.zb[b::16, 0:FB]) for b, (o, i) in enumerate(blocks("w3blk", "w3", FB))], [("zb",)], [("w3",)])
 
     play("out0")
-    own_flags(1)
-    for s in range(3):
-        ts(("vs%d" % s,), ("t512",), float(512 * s - 256), OP.add)
-    pack(1)
-    sca(("bw",), ("snd16",), ("io384",))
     sums(("psB", 0, 64), [(cmat(r), ("bw", BS + r, 3 * BS, 16)) for r in range(16)])
-    slots(0)
-    ts(("binv",), ("psB", 0, 64), 1.0 / 16, OP.mult, float(NB // 2), OP.add)
-    fill(("L0", NB, 400), 0.0)
+    ts(("binv",), ("psB", 0, 64), 1.0 / (16 * CS), OP.mult, float(NB // 2), OP.add)
+    own_flags(1)
+    pack(1)
     fill(("comp", 0, CAP), 255)
     gat("s", ("ysend",), ("ya", YO, YO + P), ("snd16",))
     their_flags(1)
     need("g", [("rs_f0", total["rs_f0"])])
     send("y", "ysend", "ya", YO + P, 1)
     lists(1)
-    streams["f1"]["Q"]()
     play("out1")
     own_flags(2)
     slots(1)
     pack(2)
     fill(("comp", 0, CAP), 255)
-    fill(("L1", NB, 400), 0.0)
-    fill(("d0",), 0.0)
-    fill(("d0", 0, 1024, 16), 191.0)
-    ts(("hI",), ("ident",), 0.5, OP.mult)
-    ts(("qI",), ("ident",), -0.25, OP.mult)
     fill(("mw", 0, CAP), 1.0)
     fill(("mw", CAP, CAP + 1536), 0.0)
     fill(("memblk",), 0.0)
-    ts(("snd2i",), ("snd32",), 2, OP.mult)
-    tc("v", ("snd2",), ("snd2i",))
     streams["f0"]["M"]()
     streams["f1"]["M"]()
     their_flags(2)
     lists(2)
-    play("back2a") if "back2a" in SCHED else slots(2)
+    play("back2a")
+    slots(2)
     play("back2")
     play("gap1")
     play("back1")
     play("gap0")
     play("back0")
-    dma("y", "o0", [(T.yv[:, 0:BS], T.yb[:, YO:YO + BS])], [("yb", YO, YO + BS)], [])
     i = ("ident",)
-    sums(("psB", 0, 336), [(i, ("sdblk",)), (i, ("w2bb", 0, 672, 2)), (i, ("w2bb", 1, 672, 2)), (i, ("w1blk", 0, 672, 2)), (i, ("w1blk", 1, 672, 2))])
-    ts(("psB", 0, 336), ("psB", 0, 336), 0.25, OP.is_gt)
-    tt(("yfb",), ("psB", 0, 336), ("memblk",), OP.add)
-    dma("s", "of", [(T.yf[:, :], T.yfb[:, :])], [("yfb",)], [])
+    sums(("psB", 0, FB), [(i, ("sdblk",)), (i, ("w2bb", 0, 2 * FB, 2)), (i, ("w2bb", 1, 2 * FB, 2)), (i, ("w1blk", 0, 2 * FB, 2)),
+                          (i, ("w1blk", 1, 2 * FB, 2)), (i, ("w3blk",))])
+    ts(("psB", 0, FB), ("psB", 0, FB), 0.25, OP.is_gt)
+    tt(("yfb",), ("psB", 0, FB), ("memblk",), OP.add)
+    dma("y", "of", [(T.yf[:, :], T.yfb[:, :])], [("yfb",)], [])
+    play("end0")
+    dma("s", "o0", [(T.yv[:, 0:BS], T.yb[:, YO:YO + BS])], [("yb", YO, YO + BS)], [])
     need("g", list(total.items()))
     for s, n in total.items():
         if s != "qg" and known["g"].get(s, 0) < n:

@@ -10,35 +10,41 @@ FAR = 7.5 * CS
 RND = 12582912.0
 YO = CAP
 FB = P // 16
+XS = 512.0
 TAG = [""]
 
-FT = (" s0-32 c s64-104 m v32-64 X0 v104-128 s128-192 X1 L0 Q C0 s192-256 L1 X2 C1 P0 X3 L2 S0-64 C2 L3 S64-128 C3 P1"
-      " S128-144 V144-200 V200-256 F")
-BT = " X0 s128-192 X1 L0 N0 C0 s192-256 L1 N1 X2 C1 X3 L2 C2 P0 N2 B0 H0 "
-BE = " N3 L3 C3 D0 H1 P1 B1 D1 U "
+FT = (" X0 v104-128 s128-192 X1 L0 C0 s192-256 L1 X2 C1 X3 P0 L2 S0-64 C2 L3 S64-128 C3 P1 S128-152 V152-200 V200-256 G F")
+BT = " s128-192 X1 L0 N0 s192-256 X2 C0 L1 N1 X3 C1 L2 N2 C2 P0 B0 H0 "
+BE = " L3 N3 C3 h0 D0 H1 h1 P1 B1 D1 U "
 SCHED = {
-    "out0": "f0" + FT,
-    "out1": "f1" + FT,
-    "back2a": "b2 s0-32 c s64-128 m v32-64",
-    "back2": "b2" + BT + "; f2 s0-64 s64-128 s128-192; b2" + BE + "Y",
-    "gap1": "f2 Q X0 s192-256 X1 L0 C0 L1 X2 C1 P0 X3 L2 S0-32 S32-56 C2 L3 C3 P1 ; b1 s0-32 v32-64 s64-128",
-    "back1": "b1" + BT + "; f2 S56-88 S88-120 ; b1" + BE + "Y",
-    "gap0": "f2 S120-176 V176-216 V216-256 F M",
-    "back0": "b0 s0-32 v32-64 s64-128" + BT + "W R N3 L3 C3 D0 H1 P1 B1 D1",
-    "end0": "b0 U",
+    "pre0": "f0 a l n c m z",
+    "out0": "f0 s0-32 s64-104 v32-64" + FT,
+    "to1": "f1 w a o r f ; f0 y M ; f1 t ; f0 Z ; f1 l n",
+    "out1": "f1 s0-32 c s64-104 m v32-64" + FT,
+    "to2": "f2 w a o r f ; f1 z M ; f2 t l n",
+    "back2": "b2 s0-40 c s64-128 m v40-64 X0 z" + BT + "; f2 s0-64 s64-128 s128-192 ; b2" + BE + "Y",
+    "gap1": "f2 X0 s192-256 X1 L0 C0 P0-0-64 X2 L1 S0-64 C1 X3 L2 C2 P0-64-128 L3 C3 P1 S64-80 ; b1 s0-32 s64-112 v32-64",
+    "back1": "b1 X0 v112-128" + BT + "; f2 S80-144 ; b1" + BE + "Y",
+    "gap0": "f2 S144-192 V192-256 G F M",
+    "back0": "b0 s0-32 v32-64 s64-112 X0 v112-128 s128-192 X1 L0 N0 s192-256 X2 C0 L1 N1 X3 C1 L2 R N2 C2 P0 B0 H0 W"
+             " L3 N3 C3 h0 D0 H1 h1 P1 B1 E D1 U e O",
 }
 
 SCRATCH = {
     "xw": ("sbuf", [128, PL], "bfloat16"),
     "ya": ("sbuf", [128, YO + PL], "bfloat16"), "yb": ("sbuf", [128, YO + PL], "bfloat16"),
-    "cdt": ("sbuf", [128, 1536], "int32"), "comp": ("sbuf", [128, 1024], "int32"),
+    "cdt": ("sbuf", [128, 1536], "int32"), "comp": ("sbuf", [128, 1024], "float32"),
+    "pc16": ("sbuf", [128, 512], "uint16"), "miss": ("sbuf", [128, 512], "float32"), "comp2": ("sbuf", [128, 1024], "float32"),
+    "orow": ("sbuf", [128, 512], "bfloat16"), "dM": ("sbuf", [128, 128], "bfloat16"),
+    "cdf": ("sbuf", [128, 512], "float32"), "kI": ("sbuf", [128, 128], "bfloat16"), "nX": ("sbuf", [128, 128], "bfloat16"),
+    "hX": ("sbuf", [128, 128], "bfloat16"), "fB": ("sbuf", [128, 128], "bfloat16"),
     "snd32": ("sbuf", [128, 24], "int32"), "snd16": ("sbuf", [128, 24], "uint16"),
-    "xi": ("sbuf", [128, 256], "int32"), "vt": ("sbuf", [128, 256], "int32"),
+    "vt": ("sbuf", [128, 256], "int32"),
     "cf": ("sbuf", [128, 4096], "bfloat16"), "cb": ("sbuf", [128, 4096], "bfloat16"),
     "scn": ("sbuf", [128, 4096], "bfloat16"),
-    "d0": ("sbuf", [128, 1024], "bfloat16"), "mt": ("sbuf", [128, 256], "bfloat16"), "hi": ("sbuf", [128, 256], "int32"),
+    "d0": ("sbuf", [128, 1024], "bfloat16"), "mt": ("sbuf", [128, 256], "bfloat16"), "hi": ("sbuf", [128, 256], "float32"),
     "vo": ("sbuf", [128, 256], "uint16"), "trash": ("sbuf", [128, 128], "float32"),
-    "w1": ("sbuf", [128, WW], "bfloat16"), "w2": ("sbuf", [128, WW], "float32"), "w3": ("sbuf", [128, P], "bfloat16"),
+    "w1": ("sbuf", [128, WW], "bfloat16"), "w2": ("sbuf", [128, WW], "float32"), "w3": ("sbuf", [128, P], "float32"),
     "zb": ("sbuf", [128, 2 * FB], "bfloat16"), "zf": ("sbuf", [128, 2 * FB], "float32"),
     "ones": ("sbuf", [128, 1024], "bfloat16"), "cst": ("sbuf", [128, 1024], "float32"),
     "C": ("sbuf", [128, 2048], "bfloat16"),
@@ -50,7 +56,7 @@ SCRATCH = {
     "L0": ("sbuf", [128, 400], "bfloat16"), "L1": ("sbuf", [128, 400], "bfloat16"), "L2": ("sbuf", [128, 400], "bfloat16"),
     "Lg": ("sbuf", [128, 512], "bfloat16"), "fsend": ("sbuf", [128, NB], "bfloat16"),
     "xsend": ("sbuf", [128, NB], "bfloat16"), "ysend": ("sbuf", [128, NB], "bfloat16"),
-    "bw": ("sbuf", [128, P], "bfloat16"), "io384": ("sbuf", [128, NB], "bfloat16"), "binv": ("sbuf", [128, 64], "uint16"),
+    "io384": ("sbuf", [128, NB], "bfloat16"), "binv": ("sbuf", [128, 64], "uint16"),
     "c2b": ("sbuf", [128, 768], "bfloat16"), "c2w": ("sbuf", [128, 1024], "bfloat16"),
     "tlb": ("sbuf", [128, 1], "bfloat16"), "tlf": ("sbuf", [128, 1], "float32"), "rec": ("sbuf", [128, 1], "float32"),
     "warm": ("sbuf", [128, 8], "float32"),
@@ -61,7 +67,8 @@ SCRATCH = {
     "mw": ("sbuf", [128, CAP + 1536], "bfloat16"), "memrep": ("sbuf", [128, 1536], "bfloat16"),
     "memblk": ("sbuf", [128, FB], "bfloat16"), "w1blk": ("sbuf", [128, 2 * FB], "bfloat16"),
     "w2blk": ("sbuf", [128, 2 * FB], "float32"), "w2bb": ("sbuf", [128, 2 * FB], "bfloat16"),
-    "w3blk": ("sbuf", [128, FB], "bfloat16"), "yfb": ("sbuf", [128, FB], "bfloat16"),
+    "L2f": ("sbuf", [128, NB], "float32"), "hr": ("sbuf", [128, 256], "float32"), "nI": ("sbuf", [128, 128], "bfloat16"),
+    "w3bb": ("sbuf", [128, FB], "bfloat16"), "w3blk": ("sbuf", [128, FB], "float32"), "yfb": ("sbuf", [128, FB], "bfloat16"),
     "cnt0": ("psum", [128, 512], "float32"), "cnt1": ("psum", [128, 512], "float32"),
     "psA": ("psum", [128, 512], "float32"), "psB": ("psum", [128, 512], "float32"),
 }
@@ -72,10 +79,11 @@ for _s in range(3):
     SCRATCH["vs%d" % _s] = ("sbuf", [128, 32], "float32")
 for _s in range(4):
     SCRATCH["nr%d" % _s] = ("sbuf", [128, 512], "bfloat16")
+    SCRATCH["ab%d" % _s] = ("sbuf", [128, 512], "bfloat16")
     SCRATCH["pd%d" % _s] = ("psum", [128, 512], "float32")
 
 _EX = ["x", "f0", "y", "f1", "b2", "f2", "b1"]
-_DM = ["snd", "xa", "xb", "tl", "sd", "cd0", "cd1", "sk", "z1", "z2", "z3", "ya", "yb", "bl1", "bl2", "bl3", "blm", "cy",
+_DM = ["snd", "xa", "xb", "tl", "sd", "cd0", "cd1", "cd2", "sk", "z1", "z2", "z3", "ya", "yb", "bl1", "bl2", "bl3", "blm", "cy",
        "o2", "o1", "o0", "of"]
 SEMAPHORES = ["qv", "qs", "qt", "qg"] + ["ls_" + e for e in _EX] + ["rs_" + e for e in _EX] + ["d_" + d for d in _DM]
 
@@ -249,15 +257,19 @@ def rank_program(g, core, T, topo):
         return ("C", 128 * r, 128 * r + 128)
 
     def blocks(blk, win, n):
-        return [(T[blk][b::16, :], T[win][b::16, n * b:n * b + n]) for b in range(16)]
+        return T[blk][:, 0:n], T[win][0::16, 0:16 * n]
 
     def pack(s):
-        r = ("cdt", BS * s, BS * s + BS)
-        ts(r, r, 256, OP.mult)
-        tt(r, r, ("xw", BS * s, BS * s + BS), OP.add)
+        mm(("psB",), ("kI",), ("xw", BS * s, BS * s + BS), True, True)
+        tt(("cdf",), ("cdt", BS * s, BS * s + BS), ("psB",), OP.add)
 
     def offsets(s, a, b):
-        ts(("c16_%d" % s, a, b), ("comp", a, b), 1.0 / 512, OP.mult, -0.44, OP.add)
+        ts(("c16_%d" % s, a, b), ("comp", a, b), 0.5, OP.mult, -0.375, OP.add)
+
+    def sfill(o, c):
+        n, a, b = reg(o)
+        for k in range(a, b, 1024):
+            act((n, k, min(b, k + 1024)), ("ones", 0, min(b, k + 1024) - k), AF.Copy, scale=c)
 
     def lists(s):
         now, was = ("flw", 1, 33), ("flw", 0, 32)
@@ -266,7 +278,9 @@ def rank_program(g, core, T, topo):
         scan(("pp",), ("one32",), ("psB", 0, 32), BIG, OP.mult, OP.add)
         tt(("sl",), ("pp",), ("t512",), OP.min)
         tc("v", ("sl16",), ("sl",))
-        sca(("comp",), ("sl16",), ("cdt", BS * s, BS * s + BS))
+
+    def compact(s):
+        sca(("comp",), ("sl16",), ("cdf",))
         offsets(s, 0, 64)
 
     def slots(s):
@@ -275,39 +289,84 @@ def rank_program(g, core, T, topo):
         tt(("zz",), ("zz",), ("vs%d" % s,), OP.min)
         tc("v", ("sb16_%d" % s,), ("zz",))
 
-    def own_flags(s):
-        a = 2 * BS * s
-        tc("s", ("c2w",), ("w2", a, a + 1024))
-        for n, lo, hi in (("w1", a, a + 1024), ("c2w", 0, 1024)):
-            for r in range(16):
-                for b in range(2):
-                    mm(("psA", 0, 32), cmat(r), (n, lo + 2 * r + b, hi, 32), n == "w1" and r + b == 0, False)
-
-    def their_flags(s):
-        k = 32 * (s - 1)
-        w = ("L%d" % (s - 1),)
-        gat("s", ("Lg", 256, 512), w, ("binv", k + 16, k + 32))
-        gat("v", ("Lg", 0, 256), w, ("binv", k, k + 16))
-        for r in range(16):
-            mm(("psA", 0, 32), cmat(r), ("Lg", r, 512, 16), False, r == 15)
-
     def stream(name):
-        s, out = int(name[1]), name[0] == "f"
+        s, out, ahead = int(name[1]), name[0] == "f", name[0] == "p"
         wn, w0, cand = ("xw", 0, "cf") if out else (("ya", "yb")[s % 2], YO, "cb")
         ot = ("yb", "ya")[s % 2]
-        win, off, xm = (wn, w0, w0 + PL), "c16_%d" % s, "xm%d" % s
+        off, o0, xm, x0, negs = "c16_%d" % s, 0, "xm%d" % s, 0, ("dN", "nX")
+        if ahead:
+            wn, w0, off, o0, xm, x0, negs = "xw", 0, "pc16", CAP * s, "xw", 2 * BS + CAP * s, ("dM", "nI")
+        win = (wn, w0, w0 + PL)
+        dead, far = {}, {}
+
+        def wide():
+            tc("s", ("c2w",), ("w2", 2 * BS * s, 2 * BS * s + 1024))
+
+        def own():
+            a, i = 2 * BS * s, ("ident",)
+            sums(("psA",), [(i, ("w1", a, a + 1024, 2)), (i, ("w1", a + 1, a + 1024, 2)), (i, ("c2w", 0, 1024, 2)), (i, ("c2w", 1, 1024, 2))])
+
+        def row():
+            tc("s", ("orow",), ("psA",))
+            for r in range(16):
+                mm(("psA", 0, 32), cmat(r), ("orow", r, 512, 16), r == 0, False)
+
+        def theirs():
+            w, k = ("L%d" % (s - 1),), 32 * s - 32
+            gat("s", ("Lg", 256, 512), w, ("binv", k + 16, k + 32))
+            gat("v", ("Lg", 0, 256), w, ("binv", k, k + 16))
+            for r in range(16):
+                mm(("psA", 0, 32), cmat(r), ("Lg", r, 512, 16), False, r == 15)
+
+        def first_y():
+            gat("s", ("ysend",), ("ya", YO, YO + P), ("snd16",))
+
+        def send_y():
+            need("g", [("rs_f0", total["rs_f0"])])
+            send("y", "ysend", "ya", YO + P, 1)
+
+        def places():
+            ts(("pc16",), ("cdt", 2 * BS, 3 * BS), 0.5, OP.mult, -0.25, OP.add)
+
+        def keep(h):
+            act(("miss", o0 + 128 * h, o0 + 128 * h + 128), ("cnt%d" % h, 0, 128), AF.Relu)
+
+        def misses():
+            w, o, i = ("comp2",), ("sl16",), ("miss",)
+            op("s", lambda: g.scalar.activation(ap(w).indirect(ap(o)), ap(i), AF.Tanh), [o, i], [w])
+
+        def Pq():
+            m = ("cnt0", 0, CAP)
+            ts(m, ("comp2", 0, CAP), CS, OP.mult)
+            tt(m, m, ("vt",), OP.max)
+            for h in range(2):
+                r = ("cnt0", 128 * h, 128 * h + 128)
+                tt(r, r, ("trash",), OP.min)
+            tc("v", ("vo",), m)
 
         def gs(a, b):
-            gat("s", (cand, 16 * a, 16 * b), win, (off, a, b))
+            gat("s", (cand, 16 * a, 16 * b), win, (off, o0 + a, o0 + b))
 
         def gv(a, b):
-            gat("v", (cand, 16 * a, 16 * b), win, (off, a, b))
+            gat("v", (cand, 16 * a, 16 * b), win, (off, o0 + a, o0 + b))
 
-        def X(c):
+        def X(c, neg=negs[0], pos="dS"):
             for i in range(16):
                 k = 64 * (i % 8)
                 sums(("pd%d" % (2 * (c % 2) + i // 8), k, k + 64),
-                     [(("dN",), (xm, 64 * c, 64 * c + 64)), (("dS",), (cand, 1024 * c + i, 1024 * c + 1024, 16))])
+                     [((neg,), (xm, x0 + 64 * c, x0 + 64 * c + 64)), ((pos,), (cand, 1024 * c + i, 1024 * c + 1024, 16))])
+
+        def Xp(c):
+            X(c, negs[1], "ident")
+
+        def A(c):
+            for b in (2 * (c % 2), 2 * (c % 2) + 1):
+                act(("ab%d" % b,), ("pd%d" % b,), AF.Abs)
+
+        def K(c):
+            for b in (2 * (c % 2), 2 * (c % 2) + 1):
+                ts(("ab%d" % b,), ("ab%d" % b,), ("tlb",), OP.is_gt)
+            far[c] = "ab%d"
 
         def L(c):
             for b in (2 * (c % 2), 2 * (c % 2) + 1):
@@ -315,28 +374,35 @@ def rank_program(g, core, T, topo):
 
         def C(c):
             k = 64 * (c % 2)
-            sums(("cnt%d" % (c // 2), k, k + 64),
-                 [(cmat(i), ("nr%d" % (2 * (c % 2) + i // 8), 64 * (i % 8), 64 * (i % 8) + 64)) for i in range(16)])
+            sums(("cnt%d" % (c // 2), k, k + 64), [(("fB",), ("ones", 0, 64))] +
+                 [(cmat(i), (far.get(c, "nr%d") % (2 * (c % 2) + i // 8), 64 * (i % 8), 64 * (i % 8) + 64)) for i in range(16)])
 
-        def Pt(h):
-            r, cn = (128 * h, 128 * h + 128), ("cnt%d" % h, 0, 128)
+        def Pt(h, a=0, b=128):
+            r, cn = (128 * h + a, 128 * h + b), ("cnt%d" % h, a, b)
             if out:
-                m = ("cnt%d" % h, 128, 256)
+                m = ("cnt%d" % h, 128 + a, 128 + b)
                 tt(m, cn, ("vt",) + r, OP.max)
-                tt(m, m, ("trash",), OP.min)
-                ts(("vo",) + r, m, -FAR, OP.add)
+                tt(m, m, ("trash", a, b), OP.min)
+                tc("v", ("vo",) + r, m)
             else:
-                ts(("mt",) + r, cn, FAR, OP.is_lt)
+                ts(("mt",) + r, cn, 0.0, OP.is_lt)
+                dead[h] = 1.5
+
+        def Ps(h):
+            act(("mt", 128 * h, 128 * h + 128), ("cnt%d" % h, 0, 128), AF.Sign, scale=-1.0)
+            dead[h] = -13.0
 
         def S(a, b):
             w, o, i = ("w2",), ("vo", a, b), ("cst", 0, 16 * (b - a))
-            op("s", lambda: g.scalar.activation(ap(w).indirect(ap(o)), ap(i), AF.Sigmoid), [o, i], [w])
+            op("s", lambda: g.scalar.activation(ap(w).indirect(ap(o)), ap(i), AF.Tanh), [o, i], [w])
 
         def V(a, b):
             sca(("w1",), ("vo", a, b), ("ones", 0, 16 * (b - a)))
 
-        def F():
+        def G():
             tc("s", ("c2b",), ("w2", 2 * P, ST))
+
+        def F():
             i = ("ident",)
             sums(("psB", 0, NB), [(i, ("c2b", 0, 768, 2)), (i, ("c2b", 1, 768, 2)), (i, ("w1", 2 * P, ST, 2)), (i, ("w1", 2 * P + 1, ST, 2))])
             tc("v", ("fsend",), ("psB", 0, NB))
@@ -347,8 +413,16 @@ def rank_program(g, core, T, topo):
 
         def H(k):
             r = (128 * k, 128 * k + 128)
-            sums(("psB",) + r, [(("hI",), (xm,) + r), (("qI",), ("ones",) + r), (("hI",), ("scn", 2048 * k + 15, 2048 * k + 2048, 16))])
-            tc("v", ("hi",) + r, ("psB",) + r)
+            sums(("psB",) + r, [(("hX",), (xm,) + r), (("qI",), ("ones",) + r), (("hI",), ("scn", 2048 * k + 15, 2048 * k + 2048, 16))])
+
+        def hv(k):
+            r = (128 * k, 128 * k + 128)
+            ts(("hi",) + r, ("psB",) + r, RND, OP.add, -RND, OP.add)
+
+        def hs(k):
+            r = (128 * k, 128 * k + 128)
+            act(("hr",) + r, ("psB",) + r, AF.Identity, bias=RND)
+            act(("hi",) + r, ("hr",) + r, AF.Identity, bias=-RND)
 
         def Bm(k):
             mm(("psA", 128 * k, 128 * k + 128), ("B",), ("mt", 128 * k, 128 * k + 128), True, True)
@@ -356,7 +430,7 @@ def rank_program(g, core, T, topo):
         def D(k):
             r = (128 * k, 128 * k + 128)
             m = ("psA", 256 + 128 * k, 384 + 128 * k)
-            ts(m, ("psA",) + r, 1.5, OP.is_ge, 255.0, OP.mult)
+            ts(m, ("psA",) + r, dead[k], OP.is_ge, 255.0, OP.mult)
             tt((wn,) + r, ("hi",) + r, m, OP.max)
 
         def U():
@@ -378,30 +452,46 @@ def rank_program(g, core, T, topo):
             offsets(s, 64, 256)
 
         def marks():
-            ts(("xi",), ("comp", 0, CAP), 255, OP.bitwise_and)
-            tc("v", (xm,), ("xi",))
-
-        def Q():
-            ts(("vt",), ("comp", 0, CAP), 1.0 / 256, OP.mult, FAR - 0.375, OP.add)
+            ts(("vt",), ("comp", 0, CAP), -0.25, OP.add)
+            tt((xm,), ("comp", 0, CAP), ("vt",), OP.subtract)
 
         def R():
-            sca(("w3",), ("snd16",), ("L2", 0, NB))
-            dma("y", "bl3", blocks("w3blk", "w3", FB), [("w3",)], [("w3blk",)])
+            w, o, i = ("w3",), ("snd16",), ("L2f",)
+            act(i, ("L2", 0, NB), AF.Copy, scale=30.0)
+            op("s", lambda: g.scalar.activation(ap(w).indirect(ap(o)), ap(i), AF.Tanh), [o, i], [w])
+            dma("y", "bl3", [blocks("w3blk", "w3", FB)], [w], [("w3blk",)])
 
         def M():
             gat("s", ("memrep", BS * s, BS * s + BS), ("mw",), ("sb16_%d" % s,))
             if s == 2:
-                dma("y", "bl2", blocks("w2blk", "w2", 2 * FB), [("w2", 0, 2 * P)], [("w2blk",)])
-                dma("y", "bl1", blocks("w1blk", "w1", 2 * FB), [("w1", 0, 2 * P)], [("w1blk",)])
+                dma("y", "bl2", [blocks("w2blk", "w2", 2 * FB)], [("w2", 0, 2 * P)], [("w2blk",)])
+                dma("y", "bl1", [blocks("w1blk", "w1", 2 * FB)], [("w1", 0, 2 * P)], [("w1blk",)])
                 dma("y", "blm", [(T.memblk[b::16, 0:min(FB, 1536 - FB * b)], T.memrep[b::16, FB * b:min(1536, FB * b + FB)])
                                  for b in range(5)], [("memrep",)], [("memblk",)])
 
         def W():
             tc("s", ("w2bb",), ("w2blk",))
-        return {"s": gs, "v": gv, "X": X, "L": L, "C": C, "P": Pt, "S": S, "V": V, "F": F, "N": N, "H": H,
-                "B": Bm, "D": D, "U": U, "Y": Y, "m": marks, "c": ck, "Q": Q, "R": R, "M": M, "W": W}
 
-    streams = {n: stream(n) for n in ("f0", "f1", "f2", "b2", "b1", "b0")}
+        def E():
+            i, o = ("ident",), ("cnt0", 0, FB)
+            tc("s", ("w3bb",), ("w3blk",))
+            sums(o, [(i, ("sdblk",)), (i, ("w2bb", 0, 2 * FB, 2)), (i, ("w2bb", 1, 2 * FB, 2)), (i, ("w1blk", 0, 2 * FB, 2)),
+                     (i, ("w1blk", 1, 2 * FB, 2)), (i, ("memblk",)), (("nI",), ("ones", 0, FB)), (i, ("w3bb",))])
+
+        def e():
+            tt(("yfb",), ("cnt0", 0, FB), ("memblk",), OP.min)
+            dma("y", "of", [(T.yf[:, :], T.yfb[:, :])], [("yfb",)], [])
+
+        def O():
+            dma("s", "o0", [(T.yv[:, 0:BS], T.yb[:, YO:YO + BS])], [("yb", YO, YO + BS)], [])
+        return {"s": gs, "v": gv, "X": X, "L": L, "C": C, "P": Pt, "S": S, "V": V, "F": F, "G": G, "N": N, "H": H,
+                "x": Xp, "A": A, "K": K, "p": Ps, "h": hv, "j": hs, "E": E, "e": e, "O": O, "z": lambda: slots(s),
+                "w": wide, "o": own, "r": row, "t": theirs, "y": first_y, "Z": send_y, "q": places, "k": keep, "u": misses,
+                "Q": Pq, "a": lambda: pack(s), "l": lambda: lists(s), "n": lambda: compact(s),
+                "f": lambda: sfill(("comp", 0, CAP), 255 / XS),
+                "B": Bm, "D": D, "U": U, "Y": Y, "m": marks, "c": ck, "R": R, "M": M, "W": W}
+
+    streams = {n: stream(n) for n in ("f0", "f1", "f2", "b2", "b1", "b0", "p0", "p1")}
 
     def play(key):
         for part in SCHED[key].split(";"):
@@ -414,111 +504,78 @@ def rank_program(g, core, T, topo):
     h = P // 2
     dma("y", "xa", [(T.xw[:, 0:h], T.x[:, 0:h])], [], [("xw", 0, h)])
     dma("s", "snd", [(T.snd32[:, :], T.snd[:, :])], [], [("snd32",)])
+    dma("s", "tl", [(T.tlb[:, :], T.tl[:, :])], [], [("tlb",)])
     dma("s", "xb", [(T.xw[:, h:P], T.x[:, h:P])], [], [("xw", h, P)])
     fill(("ones",), 1.0)
     fill(("sdrep",), 0.0)
-    fill(("sdblk",), 0.0)
     dma("y", "sd", [(T.sdrep[0::16, :], T.sd[:, :])], [], [("sdrep",)])
     dma("y", "cd0", [(T.cdt[:, 0:BS], T.cd[:, 0:BS])], [], [("cdt", 0, BS)])
-    dma("y", "tl", [(T.tlb[:, :], T.tl[:, :])], [], [("tlb",)])
 
     sel(("B",), ("ones", 0, 128), [[-16, 8], [0, 16]], OP.is_ge, 0.0, 0, 1)
     sel(("B",), ("B",), [[16, 8], [0, 16]], OP.is_ge, 0.0, 15, -1)
+    sel(("ident",), ("ones", 0, 128), [[-1, 128]], OP.is_equal, 0.0, 0, 1)
+    iota(("io384",), [[1, NB]], -NB // 2, 0)
     iota(("itp",), [[0, 128]], 0, 1)
     iota(("it3",), [[16, 32]], BS, 0)
     sel(("A",), ("B",), [[1, 128]], OP.is_gt, 0.0, 0, -1)
     sel(("A",), ("A",), [[-1, 128]], OP.not_equal, -BIG, 0, 1)
-    sel(("ident",), ("ones", 0, 128), [[-1, 128]], OP.is_equal, 0.0, 0, 1)
-    iota(("it2",), [[0, 2], [16, 64]], ST + int(FAR), 0)
-    iota(("io384",), [[1, NB]], -NB // 2, 0)
+    iota(("it2",), [[0, 2], [16, 64]], ST, 0)
 
-    act(("warm",), ("ones", 0, 8), AF.Sigmoid)
-    act(("zf",), ("ones", 0, 2 * FB), AF.Copy, scale=0.0)
-    for a, b in ((1024, 2048), (2048, 3072), (2 * P, ST)):
-        act(("w2", a, b), ("ones", 0, b - a), AF.Copy, scale=0.0)
-    act(("cst",), ("ones",), AF.Copy, scale=30.0)
     fill(("C",), 0.0)
-    fill(("zb",), 0.0)
-    fill(("w1", 1024, 3072), 0.0)
-    fill(("w1", 2 * P, ST), 0.0)
+    act(("warm",), ("ones", 0, 8), AF.Tanh)
     for q in range(8):
-        ts(("C", 16 * q, 16 * q + 129 * 15 + 1, 129), ("B", 16 * q, 16 * q + 16), CS, OP.mult)
+        act(("C", 16 * q, 16 * q + 129 * 15 + 1, 129), ("B", 16 * q, 16 * q + 16), AF.Copy, scale=CS)
+    for n, m, c in (("kI", "ident", 1.0 / XS), ("fB", "B", -FAR / 16), ("nX", "ident", -XS), ("hX", "ident", XS / 2),
+                    ("hI", "ident", 0.5), ("qI", "ident", -0.25), ("nI", "ident", -1.0), ("nA", "A", -1.0)):
+        act((n,), (m,), AF.Copy, scale=c)
+    fill(("w1", 2 * P, ST), 0.0)
+    fill(("w1", BS, 3 * BS), float(NB // 2))
     fill(("one32",), 1.0)
     fill(("flw", 0, 1), 0.0)
+    tc("v", ("snd16",), ("snd32",))
+    ts(("tlf",), ("tlb",), 2.0, OP.mult, 1.0, OP.add)
+    op("v", lambda: g.vector.reciprocal(ap(("rec",)), ap(("tlf",))), [("tlf",)], [("rec",)])
+    sca(("w1", 0, P), ("snd16",), ("io384",))
+    sums(("psB", 0, 64), [(cmat(r), ("w1", BS + r, 3 * BS, 16)) for r in range(16)])
     ts(("itp",), ("itp",), 15, OP.bitwise_and)
+    ts(("dS",), ("ident",), ("rec",), OP.mult)
     tt(("t512",), ("it3",), ("itp", 0, 32), OP.add)
     tt(("trash",), ("it2",), ("itp",), OP.add)
-    ts(("nA",), ("A",), -1.0, OP.mult)
-    fill(("comp", 0, CAP), 255)
-    fill(("bw", BS, 3 * BS), float(NB // 2))
-    tc("v", ("snd16",), ("snd32",))
+    ts(("binv",), ("psB", 0, 64), 1.0 / (16 * CS), OP.mult, float(NB // 2), OP.add)
+    act(("dN",), ("dS",), AF.Copy, scale=-XS)
+    sfill(("comp", 0, CAP), 255 / XS)
+    sfill(("zf",), 0.0)
+    sfill(("w2", 1024, 3072), 0.0)
+    sfill(("w2", 2 * P, ST), 0.0)
+    sfill(("zb",), 0.0)
+    sfill(("cst",), 30.0)
+    sfill(("sdblk",), 0.0)
+    sfill(("L0", NB, 400), 0.0)
+    sfill(("L1", NB, 400), 0.0)
+    sfill(("memblk",), 1.0)
+    sfill(("mw", 0, CAP), 2.0)
+    sfill(("mw", CAP, CAP + 1536), 1.0)
     for s in range(3):
         ts(("vs%d" % s,), ("t512",), float(512 * s - 256), OP.add)
-    fill(("L0", NB, 400), 0.0)
-    fill(("L1", NB, 400), 0.0)
-    ts(("hI",), ("ident",), 0.5, OP.mult)
-    ts(("qI",), ("ident",), -0.25, OP.mult)
     fill(("d0",), 0.0)
     fill(("d0", 0, 1024, 16), 191.0)
-    sca(("bw",), ("snd16",), ("io384",))
 
     gat("v", ("xsend",), ("xw", 0, P), ("snd16",))
     send("x", "xsend", "xw", P, 1)
     sums(("psA", 0, 32), [(cmat(r), ("sdrep", r, BS, 16)) for r in range(16)])
-    pack(0)
-    lists(0)
-    ts(("tlf",), ("tlb",), 2.0, OP.mult, 1.0, OP.add)
-    op("v", lambda: g.vector.reciprocal(ap(("rec",)), ap(("tlf",))), [("tlf",)], [("rec",)])
-    ts(("dS",), ("ident",), ("rec",), OP.mult)
-    ts(("dN",), ("dS",), -1.0, OP.mult)
-    slots(0)
+    play("pre0")
+    fill(("w1", 1024, 3072), 0.0)
     need("y", [("rs_x", total["rs_x"])])
-    dma("y", "z2", [(i, T.zf[b::16, :]) for b, (o, i) in enumerate(blocks("w2blk", "w2", 2 * FB))], [("zf",)], [("w2", 0, 2 * P)])
-    dma("y", "z1", [(i, T.zb[b::16, :]) for b, (o, i) in enumerate(blocks("w1blk", "w1", 2 * FB))], [("zb",)], [("w1", 0, 2 * P)])
+    dma("y", "z2", [blocks("zf", "w2", 2 * FB)[::-1]], [("zf",)], [("w2", 0, 2 * P)])
+    dma("y", "z1", [blocks("zb", "w1", 2 * FB)[::-1]], [("zb",)], [("w1", 0, 2 * P)])
     dma("y", "cd1", [(T.cdt[:, BS:3 * BS], T.cd[:, BS:3 * BS])], [], [("cdt", BS, 3 * BS)])
     dma("y", "ya", [(T.ya[:, YO:YO + P], T.y0[:, :])], [], [("ya", YO, YO + P)])
     dma("y", "yb", [(T.yb[:, YO:YO + P], T.y0[:, :])], [], [("yb", YO, YO + P)])
     dma("y", "sk", [(T.sdblk[0::16, :], T.sd[:, 0:FB]), (T.sdblk[1::16, 0:BS - FB], T.sd[:, FB:BS])], [], [("sdblk",)])
-    dma("y", "z3", [(i, T.zb[b::16, 0:FB]) for b, (o, i) in enumerate(blocks("w3blk", "w3", FB))], [("zb",)], [("w3",)])
+    dma("y", "z3", [blocks("zf", "w3", FB)[::-1]], [("zf",)], [("w3",)])
 
-    play("out0")
-    sums(("psB", 0, 64), [(cmat(r), ("bw", BS + r, 3 * BS, 16)) for r in range(16)])
-    ts(("binv",), ("psB", 0, 64), 1.0 / (16 * CS), OP.mult, float(NB // 2), OP.add)
-    own_flags(1)
-    pack(1)
-    fill(("comp", 0, CAP), 255)
-    gat("s", ("ysend",), ("ya", YO, YO + P), ("snd16",))
-    their_flags(1)
-    need("g", [("rs_f0", total["rs_f0"])])
-    send("y", "ysend", "ya", YO + P, 1)
-    lists(1)
-    play("out1")
-    own_flags(2)
-    slots(1)
-    pack(2)
-    fill(("comp", 0, CAP), 255)
-    fill(("mw", 0, CAP), 1.0)
-    fill(("mw", CAP, CAP + 1536), 0.0)
-    fill(("memblk",), 0.0)
-    streams["f0"]["M"]()
-    streams["f1"]["M"]()
-    their_flags(2)
-    lists(2)
-    play("back2a")
-    slots(2)
-    play("back2")
-    play("gap1")
-    play("back1")
-    play("gap0")
-    play("back0")
-    i = ("ident",)
-    sums(("psB", 0, FB), [(i, ("sdblk",)), (i, ("w2bb", 0, 2 * FB, 2)), (i, ("w2bb", 1, 2 * FB, 2)), (i, ("w1blk", 0, 2 * FB, 2)),
-                          (i, ("w1blk", 1, 2 * FB, 2)), (i, ("w3blk",))])
-    ts(("psB", 0, FB), ("psB", 0, FB), 0.25, OP.is_gt)
-    tt(("yfb",), ("psB", 0, FB), ("memblk",), OP.add)
-    dma("y", "of", [(T.yf[:, :], T.yfb[:, :])], [("yfb",)], [])
-    play("end0")
-    dma("s", "o0", [(T.yv[:, 0:BS], T.yb[:, YO:YO + BS])], [("yb", YO, YO + BS)], [])
+    for key in ("out0", "to1", "out1", "to2", "back2", "gap1", "back1", "gap0", "back0"):
+        play(key)
     need("g", list(total.items()))
     for s, n in total.items():
         if s != "qg" and known["g"].get(s, 0) < n:

@@ -13,36 +13,35 @@ FB = P // 16
 XS = 512.0
 TAG = [""]
 
-FT = (" X0 v104-128 s128-192 X1 L0 C0 s192-256 L1 X2 C1 X3 P0 L2 S0-64 C2 L3 S64-128 C3 P1 S128-152 V152-200 V200-256 G F")
-BT = " s128-192 X1 L0 N0 s192-256 X2 C0 L1 N1 X3 C1 L2 N2 C2 P0 B0 H0 "
-BE = " L3 N3 C3 h0 D0 H1 h1 P1 B1 D1 U "
+FT = (" s64-104 X0 v104-128 s128-192 X1 K0 C0 s192-256 L1 P0-64 X2 S0-64 C1 X3 L2 P64-128 C2 K3 S64-128 C3 P128-256"
+      " S128-152 V152-216 V216-256 G F")
+BT = " s128-192 X1 K0 s192-256 X2 C0 L1 N0-2 X3 C1 L2 N2-3 C2 "
+BE = " K3 N3-4 C3 H P h "
 SCHED = {
-    "pre0": "f0 a l n c m z",
-    "out0": "f0 s0-32 s64-104 v32-64" + FT,
-    "to1": "f1 w a o r f ; f0 y M ; f1 t ; f0 Z ; f1 l n",
-    "out1": "f1 s0-32 c s64-104 m v32-64" + FT,
+    "pre0": "f0 a l n c m",
+    "out0": "f0 s0-32 v32-64" + FT,
+    "to1": "f1 w a o r f ; f0 z y M ; f1 t ; f0 Z ; f1 l n",
+    "out1": "f1 s0-32 c m v32-64" + FT,
     "to2": "f2 w a o r f ; f1 z M ; f2 t l n",
-    "back2": "b2 s0-40 c s64-128 m v40-64 X0 z" + BT + "; f2 s0-64 s64-128 s128-192 ; b2" + BE + "Y",
-    "gap1": "f2 X0 s192-256 X1 L0 C0 P0-0-64 X2 L1 S0-64 C1 X3 L2 C2 P0-64-128 L3 C3 P1 S64-80 ; b1 s0-32 s64-112 v32-64",
-    "back1": "b1 X0 v112-128" + BT + "; f2 S80-144 ; b1" + BE + "Y",
+    "back2": "b2 s0-40 c s64-128 m v40-64 X0 z" + BT + "; f2 s0-64 s64-128 s128-192 ; b2" + BE + "D U Y",
+    "gap1": "f2 X0 s192-256 X1 L0 C0 L1 X2 P0-64 S0-64 C1 X3 L2 C2 K3 P64-128 C3 P128-256 ; b1 s0-32 s64-112 v32-64",
+    "back1": "b1 X0 v112-128" + BT + "; f2 S64-128 S128-144 ; b1" + BE + "D U Y",
     "gap0": "f2 S144-192 V192-256 G F M",
-    "back0": "b0 s0-32 v32-64 s64-112 X0 v112-128 s128-192 X1 L0 N0 s192-256 X2 C0 L1 N1 X3 C1 L2 R N2 C2 P0 B0 H0 W"
-             " L3 N3 C3 h0 D0 H1 h1 P1 B1 E D1 U e O",
+    "back0": "b0 s0-32 v32-64 s64-112 X0 v112-128" + BT + "R W" + BE + "E D U e O",
 }
 
 SCRATCH = {
     "xw": ("sbuf", [128, PL], "bfloat16"),
     "ya": ("sbuf", [128, YO + PL], "bfloat16"), "yb": ("sbuf", [128, YO + PL], "bfloat16"),
     "cdt": ("sbuf", [128, 1536], "int32"), "comp": ("sbuf", [128, 1024], "float32"),
-    "pc16": ("sbuf", [128, 512], "uint16"), "miss": ("sbuf", [128, 512], "float32"), "comp2": ("sbuf", [128, 1024], "float32"),
-    "orow": ("sbuf", [128, 512], "bfloat16"), "dM": ("sbuf", [128, 128], "bfloat16"),
-    "cdf": ("sbuf", [128, 512], "float32"), "kI": ("sbuf", [128, 128], "bfloat16"), "nX": ("sbuf", [128, 128], "bfloat16"),
+    "orow": ("sbuf", [128, 512], "bfloat16"),
+    "cdf": ("sbuf", [128, 512], "float32"), "kI": ("sbuf", [128, 128], "bfloat16"),
     "hX": ("sbuf", [128, 128], "bfloat16"), "fB": ("sbuf", [128, 128], "bfloat16"),
     "snd32": ("sbuf", [128, 24], "int32"), "snd16": ("sbuf", [128, 24], "uint16"),
     "vt": ("sbuf", [128, 256], "int32"),
     "cf": ("sbuf", [128, 4096], "bfloat16"), "cb": ("sbuf", [128, 4096], "bfloat16"),
     "scn": ("sbuf", [128, 4096], "bfloat16"),
-    "d0": ("sbuf", [128, 1024], "bfloat16"), "mt": ("sbuf", [128, 256], "bfloat16"), "hi": ("sbuf", [128, 256], "float32"),
+    "d0": ("sbuf", [128, 2048], "bfloat16"), "mt": ("sbuf", [128, 256], "bfloat16"), "hi": ("sbuf", [128, 256], "float32"),
     "vo": ("sbuf", [128, 256], "uint16"), "trash": ("sbuf", [128, 128], "float32"),
     "w1": ("sbuf", [128, WW], "bfloat16"), "w2": ("sbuf", [128, WW], "float32"), "w3": ("sbuf", [128, P], "float32"),
     "zb": ("sbuf", [128, 2 * FB], "bfloat16"), "zf": ("sbuf", [128, 2 * FB], "float32"),
@@ -67,9 +66,9 @@ SCRATCH = {
     "mw": ("sbuf", [128, CAP + 1536], "bfloat16"), "memrep": ("sbuf", [128, 1536], "bfloat16"),
     "memblk": ("sbuf", [128, FB], "bfloat16"), "w1blk": ("sbuf", [128, 2 * FB], "bfloat16"),
     "w2blk": ("sbuf", [128, 2 * FB], "float32"), "w2bb": ("sbuf", [128, 2 * FB], "bfloat16"),
-    "L2f": ("sbuf", [128, NB], "float32"), "hr": ("sbuf", [128, 256], "float32"), "nI": ("sbuf", [128, 128], "bfloat16"),
+    "L2f": ("sbuf", [128, NB], "float32"), "nI": ("sbuf", [128, 128], "bfloat16"),
     "w3bb": ("sbuf", [128, FB], "bfloat16"), "w3blk": ("sbuf", [128, FB], "float32"), "yfb": ("sbuf", [128, FB], "bfloat16"),
-    "cnt0": ("psum", [128, 512], "float32"), "cnt1": ("psum", [128, 512], "float32"),
+    "nr": ("sbuf", [128, 2048], "bfloat16"), "pd": ("psum", [128, 2048], "float32"), "cnt": ("psum", [128, 1024], "float32"),
     "psA": ("psum", [128, 512], "float32"), "psB": ("psum", [128, 512], "float32"),
 }
 for _s in range(3):
@@ -77,10 +76,6 @@ for _s in range(3):
     SCRATCH["xm%d" % _s] = ("sbuf", [128, 256], "bfloat16")
     SCRATCH["sb16_%d" % _s] = ("sbuf", [128, 32], "uint16")
     SCRATCH["vs%d" % _s] = ("sbuf", [128, 32], "float32")
-for _s in range(4):
-    SCRATCH["nr%d" % _s] = ("sbuf", [128, 512], "bfloat16")
-    SCRATCH["ab%d" % _s] = ("sbuf", [128, 512], "bfloat16")
-    SCRATCH["pd%d" % _s] = ("psum", [128, 512], "float32")
 
 _EX = ["x", "f0", "y", "f1", "b2", "f2", "b1"]
 _DM = ["snd", "xa", "xb", "tl", "sd", "cd0", "cd1", "cd2", "sk", "z1", "z2", "z3", "ya", "yb", "bl1", "bl2", "bl3", "blm", "cy",
@@ -108,6 +103,9 @@ def rank_program(g, core, T, topo):
     def is_ps(n):
         return SCRATCH[n][0] == "psum"
 
+    def banks(a, b):
+        return a // 512 * 512, -(-b // 512) * 512
+
     def ap(r):
         n, a, b = reg(r)
         if len(r) > 3:
@@ -134,7 +132,7 @@ def rank_program(g, core, T, topo):
         for r, w in [(r, is_ps(r[0])) for r in R] + [(r, True) for r in W]:
             n, a, b = reg(r)
             if is_ps(n):
-                a, b = 0, width(n)
+                a, b = banks(a, b)
             for c0, c1, iw, qq, ev in recs.get(n, []):
                 if c0 < b and a < c1 and (w or iw) and not (q == "t" and qq == "t"):
                     evs.append(ev)
@@ -144,15 +142,16 @@ def rank_program(g, core, T, topo):
         for r in W:
             n, a, b = reg(r)
             if is_ps(n):
-                a, b = 0, width(n)
-                recs[n] = [e for e in recs.get(n, []) if q == "t" and e[3] == "t"]
+                a, b = banks(a, b)
+                recs[n] = [e for e in recs.get(n, []) if not (a <= e[0] and e[1] <= b)]
             elif len(r) <= 3:
                 recs[n] = [e for e in recs.get(n, []) if not (a <= e[0] and e[1] <= b)]
             recs.setdefault(n, []).append((a, b, True, q, ev))
         for r in R:
             n, a, b = reg(r)
             if is_ps(n):
-                recs[n] = [(0, width(n), True, q, ev)]
+                a, b = banks(a, b)
+                recs[n] = [e for e in recs.get(n, []) if not (a <= e[0] and e[1] <= b)] + [(a, b, True, q, ev)]
             else:
                 recs.setdefault(n, []).append((a, b, False, q, ev))
 
@@ -290,14 +289,10 @@ def rank_program(g, core, T, topo):
         tc("v", ("sb16_%d" % s,), ("zz",))
 
     def stream(name):
-        s, out, ahead = int(name[1]), name[0] == "f", name[0] == "p"
+        s, out = int(name[1]), name[0] == "f"
         wn, w0, cand = ("xw", 0, "cf") if out else (("ya", "yb")[s % 2], YO, "cb")
         ot = ("yb", "ya")[s % 2]
-        off, o0, xm, x0, negs = "c16_%d" % s, 0, "xm%d" % s, 0, ("dN", "nX")
-        if ahead:
-            wn, w0, off, o0, xm, x0, negs = "xw", 0, "pc16", CAP * s, "xw", 2 * BS + CAP * s, ("dM", "nI")
-        win = (wn, w0, w0 + PL)
-        dead, far = {}, {}
+        win, off, xm = (wn, w0, w0 + PL), "c16_%d" % s, "xm%d" % s
 
         def wide():
             tc("s", ("c2w",), ("w2", 2 * BS * s, 2 * BS * s + 1024))
@@ -325,72 +320,39 @@ def rank_program(g, core, T, topo):
             need("g", [("rs_f0", total["rs_f0"])])
             send("y", "ysend", "ya", YO + P, 1)
 
-        def places():
-            ts(("pc16",), ("cdt", 2 * BS, 3 * BS), 0.5, OP.mult, -0.25, OP.add)
-
-        def keep(h):
-            act(("miss", o0 + 128 * h, o0 + 128 * h + 128), ("cnt%d" % h, 0, 128), AF.Relu)
-
-        def misses():
-            w, o, i = ("comp2",), ("sl16",), ("miss",)
-            op("s", lambda: g.scalar.activation(ap(w).indirect(ap(o)), ap(i), AF.Tanh), [o, i], [w])
-
-        def Pq():
-            m = ("cnt0", 0, CAP)
-            ts(m, ("comp2", 0, CAP), CS, OP.mult)
-            tt(m, m, ("vt",), OP.max)
-            for h in range(2):
-                r = ("cnt0", 128 * h, 128 * h + 128)
-                tt(r, r, ("trash",), OP.min)
-            tc("v", ("vo",), m)
-
         def gs(a, b):
-            gat("s", (cand, 16 * a, 16 * b), win, (off, o0 + a, o0 + b))
+            gat("s", (cand, 16 * a, 16 * b), win, (off, a, b))
 
         def gv(a, b):
-            gat("v", (cand, 16 * a, 16 * b), win, (off, o0 + a, o0 + b))
+            gat("v", (cand, 16 * a, 16 * b), win, (off, a, b))
 
-        def X(c, neg=negs[0], pos="dS"):
+        def X(c):
             for i in range(16):
-                k = 64 * (i % 8)
-                sums(("pd%d" % (2 * (c % 2) + i // 8), k, k + 64),
-                     [((neg,), (xm, x0 + 64 * c, x0 + 64 * c + 64)), ((pos,), (cand, 1024 * c + i, 1024 * c + 1024, 16))])
+                k = 1024 * (c % 2) + 64 * i
+                sums(("pd", k, k + 64), [(("dN",), (xm, 64 * c, 64 * c + 64)), (("dS",), (cand, 1024 * c + i, 1024 * c + 1024, 16))])
 
-        def Xp(c):
-            X(c, negs[1], "ident")
+        def L(c, n=1024):
+            for k in range(1024 * (c % 2), 1024 * (c % 2) + 1024, n):
+                ts(("nr", k, k + n), ("pd", k, k + n), RND, OP.add, RND, OP.not_equal)
 
-        def A(c):
-            for b in (2 * (c % 2), 2 * (c % 2) + 1):
-                act(("ab%d" % b,), ("pd%d" % b,), AF.Abs)
-
-        def K(c):
-            for b in (2 * (c % 2), 2 * (c % 2) + 1):
-                ts(("ab%d" % b,), ("ab%d" % b,), ("tlb",), OP.is_gt)
-            far[c] = "ab%d"
-
-        def L(c):
-            for b in (2 * (c % 2), 2 * (c % 2) + 1):
-                ts(("nr%d" % b,), ("pd%d" % b,), RND, OP.add, RND, OP.not_equal)
+        def cnt(a, b):
+            k = a + (384 if out and a >= 128 else 0)
+            return ("cnt", k, k + b - a)
 
         def C(c):
-            k = 64 * (c % 2)
-            sums(("cnt%d" % (c // 2), k, k + 64), [(("fB",), ("ones", 0, 64))] +
-                 [(cmat(i), (far.get(c, "nr%d") % (2 * (c % 2) + i // 8), 64 * (i % 8), 64 * (i % 8) + 64)) for i in range(16)])
+            k = 1024 * (c % 2)
+            sums(cnt(64 * c, 64 * c + 64), [(("fB",), ("ones", 0, 64))] + [(cmat(i), ("nr", k + 64 * i, k + 64 * i + 64)) for i in range(16)])
 
-        def Pt(h, a=0, b=128):
-            r, cn = (128 * h + a, 128 * h + b), ("cnt%d" % h, a, b)
+        def Pt(a=0, b=CAP):
+            cn = cnt(a, b)
             if out:
-                m = ("cnt%d" % h, 128 + a, 128 + b)
-                tt(m, cn, ("vt",) + r, OP.max)
-                tt(m, m, ("trash", a, b), OP.min)
-                tc("v", ("vo",) + r, m)
+                m = ("cnt", cn[1] + 128, cn[2] + 128)
+                tt(m, cn, ("vt", a, b), OP.max)
+                tt(m, m, ("trash", a % 128, a % 128 + b - a), OP.min)
+                tc("v", ("vo", a, b), m)
             else:
-                ts(("mt",) + r, cn, 0.0, OP.is_lt)
-                dead[h] = 1.5
-
-        def Ps(h):
-            act(("mt", 128 * h, 128 * h + 128), ("cnt%d" % h, 0, 128), AF.Sign, scale=-1.0)
-            dead[h] = -13.0
+                ts(("mt", a, b), cn, 0.0, OP.is_lt)
+                mm(("psA", a, b), ("B",), ("mt", a, b), True, True)
 
         def S(a, b):
             w, o, i = ("w2",), ("vo", a, b), ("cst", 0, 16 * (b - a))
@@ -408,30 +370,20 @@ def rank_program(g, core, T, topo):
             tc("v", ("fsend",), ("psB", 0, NB))
             send("f%d" % s, "fsend", "L%d" % s, 0, -1)
 
-        def N(c):
-            scan(("scn", 1024 * c, 1024 * c + 1024), ("d0",), ("cb", 1024 * c, 1024 * c + 1024), 191.0, OP.max, OP.min)
+        def N(a, b):
+            r = (1024 * a, 1024 * b)
+            scan(("scn",) + r, ("d0", 0, r[1] - r[0]), ("cb",) + r, 191.0, OP.max, OP.min)
 
-        def H(k):
-            r = (128 * k, 128 * k + 128)
-            sums(("psB",) + r, [(("hX",), (xm,) + r), (("qI",), ("ones",) + r), (("hI",), ("scn", 2048 * k + 15, 2048 * k + 2048, 16))])
+        def H(a=0, b=CAP):
+            sums(("psB", a, b), [(("hX",), (xm, a, b)), (("qI",), ("ones", a, b)), (("hI",), ("scn", 16 * a + 15, 16 * b, 16))])
 
-        def hv(k):
-            r = (128 * k, 128 * k + 128)
-            ts(("hi",) + r, ("psB",) + r, RND, OP.add, -RND, OP.add)
+        def hv(a=0, b=CAP):
+            ts(("hi", a, b), ("psB", a, b), RND, OP.add, -RND, OP.add)
 
-        def hs(k):
-            r = (128 * k, 128 * k + 128)
-            act(("hr",) + r, ("psB",) + r, AF.Identity, bias=RND)
-            act(("hi",) + r, ("hr",) + r, AF.Identity, bias=-RND)
-
-        def Bm(k):
-            mm(("psA", 128 * k, 128 * k + 128), ("B",), ("mt", 128 * k, 128 * k + 128), True, True)
-
-        def D(k):
-            r = (128 * k, 128 * k + 128)
-            m = ("psA", 256 + 128 * k, 384 + 128 * k)
-            ts(m, ("psA",) + r, dead[k], OP.is_ge, 255.0, OP.mult)
-            tt((wn,) + r, ("hi",) + r, m, OP.max)
+        def D(a=0, b=CAP):
+            m = ("psA", CAP + a, CAP + b)
+            ts(m, ("psA", a, b), 1.5, OP.is_ge, 255.0, OP.mult)
+            tt((wn, a, b), ("hi", a, b), m, OP.max)
 
         def U():
             a = YO + BS * s
@@ -473,25 +425,24 @@ def rank_program(g, core, T, topo):
             tc("s", ("w2bb",), ("w2blk",))
 
         def E():
-            i, o = ("ident",), ("cnt0", 0, FB)
+            i, o = ("ident",), ("cnt", 512, 512 + FB)
             tc("s", ("w3bb",), ("w3blk",))
             sums(o, [(i, ("sdblk",)), (i, ("w2bb", 0, 2 * FB, 2)), (i, ("w2bb", 1, 2 * FB, 2)), (i, ("w1blk", 0, 2 * FB, 2)),
                      (i, ("w1blk", 1, 2 * FB, 2)), (i, ("memblk",)), (("nI",), ("ones", 0, FB)), (i, ("w3bb",))])
 
         def e():
-            tt(("yfb",), ("cnt0", 0, FB), ("memblk",), OP.min)
+            tt(("yfb",), ("cnt", 512, 512 + FB), ("memblk",), OP.min)
             dma("y", "of", [(T.yf[:, :], T.yfb[:, :])], [("yfb",)], [])
 
         def O():
             dma("s", "o0", [(T.yv[:, 0:BS], T.yb[:, YO:YO + BS])], [("yb", YO, YO + BS)], [])
         return {"s": gs, "v": gv, "X": X, "L": L, "C": C, "P": Pt, "S": S, "V": V, "F": F, "G": G, "N": N, "H": H,
-                "x": Xp, "A": A, "K": K, "p": Ps, "h": hv, "j": hs, "E": E, "e": e, "O": O, "z": lambda: slots(s),
-                "w": wide, "o": own, "r": row, "t": theirs, "y": first_y, "Z": send_y, "q": places, "k": keep, "u": misses,
-                "Q": Pq, "a": lambda: pack(s), "l": lambda: lists(s), "n": lambda: compact(s),
-                "f": lambda: sfill(("comp", 0, CAP), 255 / XS),
-                "B": Bm, "D": D, "U": U, "Y": Y, "m": marks, "c": ck, "R": R, "M": M, "W": W}
+                "K": lambda c: L(c, 512), "h": hv, "E": E, "e": e, "O": O, "z": lambda: slots(s),
+                "w": wide, "o": own, "r": row, "t": theirs, "y": first_y, "Z": send_y,
+                "a": lambda: pack(s), "l": lambda: lists(s), "n": lambda: compact(s),
+                "f": lambda: sfill(("comp", 0, CAP), 255 / XS), "D": D, "U": U, "Y": Y, "m": marks, "c": ck, "R": R, "M": M, "W": W}
 
-    streams = {n: stream(n) for n in ("f0", "f1", "f2", "b2", "b1", "b0", "p0", "p1")}
+    streams = {n: stream(n) for n in ("f0", "f1", "f2", "b2", "b1", "b0")}
 
     def play(key):
         for part in SCHED[key].split(";"):
@@ -525,7 +476,7 @@ def rank_program(g, core, T, topo):
     act(("warm",), ("ones", 0, 8), AF.Tanh)
     for q in range(8):
         act(("C", 16 * q, 16 * q + 129 * 15 + 1, 129), ("B", 16 * q, 16 * q + 16), AF.Copy, scale=CS)
-    for n, m, c in (("kI", "ident", 1.0 / XS), ("fB", "B", -FAR / 16), ("nX", "ident", -XS), ("hX", "ident", XS / 2),
+    for n, m, c in (("kI", "ident", 1.0 / XS), ("fB", "B", -FAR / 16), ("hX", "ident", XS / 2),
                     ("hI", "ident", 0.5), ("qI", "ident", -0.25), ("nI", "ident", -1.0), ("nA", "A", -1.0)):
         act((n,), (m,), AF.Copy, scale=c)
     fill(("w1", 2 * P, ST), 0.0)
@@ -544,27 +495,22 @@ def rank_program(g, core, T, topo):
     ts(("binv",), ("psB", 0, 64), 1.0 / (16 * CS), OP.mult, float(NB // 2), OP.add)
     act(("dN",), ("dS",), AF.Copy, scale=-XS)
     sfill(("comp", 0, CAP), 255 / XS)
+    for s in range(3):
+        ts(("vs%d" % s,), ("t512",), float(512 * s - 256), OP.add)
+
+    gat("s", ("xsend", 192, NB), ("xw", 0, P), ("snd16", 12, 24))
+    gat("v", ("xsend", 0, 192), ("xw", 0, P), ("snd16", 0, 12))
+    send("x", "xsend", "xw", P, 1)
     sfill(("zf",), 0.0)
     sfill(("w2", 1024, 3072), 0.0)
     sfill(("w2", 2 * P, ST), 0.0)
-    sfill(("zb",), 0.0)
-    sfill(("cst",), 30.0)
-    sfill(("sdblk",), 0.0)
-    sfill(("L0", NB, 400), 0.0)
-    sfill(("L1", NB, 400), 0.0)
-    sfill(("memblk",), 1.0)
-    sfill(("mw", 0, CAP), 2.0)
-    sfill(("mw", CAP, CAP + 1536), 1.0)
-    for s in range(3):
-        ts(("vs%d" % s,), ("t512",), float(512 * s - 256), OP.add)
-    fill(("d0",), 0.0)
-    fill(("d0", 0, 1024, 16), 191.0)
-
-    gat("v", ("xsend",), ("xw", 0, P), ("snd16",))
-    send("x", "xsend", "xw", P, 1)
+    for r, c in ((("zb",), 0), (("cst",), 30), (("sdblk",), 0), (("L0", NB, 400), 0), (("L1", NB, 400), 0), (("memblk",), 1),
+                 (("mw", 0, CAP), 2), (("mw", CAP, CAP + 1536), 1)):
+        iota(r, [[0, reg(r)[2] - reg(r)[1]]], c, 0)
+    iota(("d0",), [[0, 128], [-200, 16]], 191, 0)
     sums(("psA", 0, 32), [(cmat(r), ("sdrep", r, BS, 16)) for r in range(16)])
-    play("pre0")
     fill(("w1", 1024, 3072), 0.0)
+    play("pre0")
     need("y", [("rs_x", total["rs_x"])])
     dma("y", "z2", [blocks("zf", "w2", 2 * FB)[::-1]], [("zf",)], [("w2", 0, 2 * P)])
     dma("y", "z1", [blocks("zb", "w1", 2 * FB)[::-1]], [("zb",)], [("w1", 0, 2 * P)])

@@ -3,8 +3,8 @@ from concourse.mybir import AluOpType as OP, ActivationFunctionType as AF
 
 P, PL, NB, BS, CAP, BK = 5376, 5760, 384, 512, 256, 128
 ST = 2 * PL
-WW = ST + 1024
-BIG = 1024.0
+WW = ST + 2176
+BIG = 2048.0
 CS = 32768.0
 FAR = 7.5 * CS
 RND = 12582912.0
@@ -13,60 +13,61 @@ FB = P // 16
 XS = 512.0
 TAG = [""]
 
-FT = (" s64-104 X0 v104-128 s128-192 X1 K0 C0 s192-256 L1 P0-64 X2 S0-64 C1 X3 L2 P64-128 C2 K3 S64-128 C3 P128-256"
-      " S128-152 V152-216 V216-256 G F")
-BT = " s128-192 X1 K0 s192-256 X2 C0 L1 N0-2 X3 C1 L2 N2-3 C2 "
+FT = (" s128-192 X1 K0 C0 s192-256 K1 P0-64 X2 S0-64 C1 X3 L2 P64-128 C2 K3 S80-128 V64-80 C3 P128-256"
+      " S128-164 V164-256 G F")
+BS_ = " s0-32 v32-64 s64-92 X0 v92-128"
+BT = " s128-192 X1 K0 s192-256 X2 C0 N0-2 L1 X3 C1 L2 N2-3 C2 "
 BE = " K3 N3-4 C3 H P h "
+LAST = (128, 128, 128)
 SCHED = {
-    "pre0": "f0 a l n c m",
-    "out0": "f0 s0-32 v32-64" + FT,
-    "to1": "f1 w a o r f ; f0 z y M ; f1 t ; f0 Z ; f1 l n",
-    "out1": "f1 s0-32 c m v32-64" + FT,
-    "to2": "f2 w a o r f ; f1 z M ; f2 t l n",
-    "back2": "b2 s0-40 c s64-128 m v40-64 X0 z" + BT + "; f2 s0-64 s64-128 s128-192 ; b2" + BE + "D U Y",
-    "gap1": "f2 X0 s192-256 X1 L0 C0 L1 X2 P0-64 S0-64 C1 X3 L2 C2 K3 P64-128 C3 P128-256 ; b1 s0-32 s64-112 v32-64",
-    "back1": "b1 X0 v112-128" + BT + "; f2 S64-128 S128-144 ; b1" + BE + "D U Y",
-    "gap0": "f2 S144-192 V192-256 G F M",
-    "back0": "b0 s0-32 v32-64 s64-112 X0 v112-128" + BT + "R W" + BE + "E D U e O",
+    "pre0": "f0 l a A n c m",
+    "out0": "f0 s0-32 v32-64 s64-88 X0 v88-128" + FT,
+    "to1": "f1 w o a f ; f0 z y ; f1 t A b ; f0 Z ; f1 l n",
+    "out1": "f1 s0-56 c m v56-64 X0 v64-112 s112-128" + FT,
+    "to2": "f2 w o a f ; f0 M ; f1 z M ; f2 t A l n",
+    "back2": "b2 s0-56 c m v56-64 X0 v64-96 s96-128 z" + BT + "; f2 s0-64 s64-128 s128-192 ; b2" + BE + "D U12 Y0 O",
+    "gap1": "f2 X0 s192-256 X1 L0 C0 L1 X2 P0-64 S0-64 C1 X3 L2 C2 K3 P64-128 C3 P128-256",
+    "back1": "b1" + BS_ + BT + "; f2 S64-128 S128-142 ; b1" + BE + "D U Y",
+    "gap0": "f2 S142-192 V192-256 G F B",
+    "back0": "b0" + BS_ + BT + "R ; f2 M ; b1 O ; b0 W" + BE + "E D U e O",
 }
 
 SCRATCH = {
     "xw": ("sbuf", [128, PL], "bfloat16"),
     "ya": ("sbuf", [128, YO + PL], "bfloat16"), "yb": ("sbuf", [128, YO + PL], "bfloat16"),
-    "cdt": ("sbuf", [128, 1536], "int32"), "comp": ("sbuf", [128, 1024], "float32"),
-    "orow": ("sbuf", [128, 512], "bfloat16"),
+    "cdt": ("sbuf", [128, 1536], "int32"), "comp": ("sbuf", [128, 1152], "float32"),
+    "c2b": ("sbuf", [128, 2 * NB], "bfloat16"), "L2f": ("sbuf", [128, NB], "float32"),
     "cdf": ("sbuf", [128, 512], "float32"), "kI": ("sbuf", [128, 128], "bfloat16"),
     "hX": ("sbuf", [128, 128], "bfloat16"), "fB": ("sbuf", [128, 128], "bfloat16"),
     "snd32": ("sbuf", [128, 24], "int32"), "snd16": ("sbuf", [128, 24], "uint16"),
-    "vt": ("sbuf", [128, 256], "int32"),
     "cf": ("sbuf", [128, 4096], "bfloat16"), "cb": ("sbuf", [128, 4096], "bfloat16"),
     "scn": ("sbuf", [128, 4096], "bfloat16"),
     "d0": ("sbuf", [128, 2048], "bfloat16"), "mt": ("sbuf", [128, 256], "bfloat16"), "hi": ("sbuf", [128, 256], "float32"),
     "vo": ("sbuf", [128, 256], "uint16"), "trash": ("sbuf", [128, 128], "float32"),
     "w1": ("sbuf", [128, WW], "bfloat16"), "w2": ("sbuf", [128, WW], "float32"), "w3": ("sbuf", [128, P], "float32"),
-    "zb": ("sbuf", [128, 2 * FB], "bfloat16"), "zf": ("sbuf", [128, 2 * FB], "float32"),
-    "ones": ("sbuf", [128, 1024], "bfloat16"), "cst": ("sbuf", [128, 1024], "float32"),
+    "zb": ("sbuf", [128, 480], "bfloat16"), "zf": ("sbuf", [128, 480], "float32"),
+    "ones": ("sbuf", [128, 1536], "bfloat16"), "cst": ("sbuf", [128, 1024], "float32"),
     "C": ("sbuf", [128, 2048], "bfloat16"),
     "ident": ("sbuf", [128, 128], "bfloat16"), "B": ("sbuf", [128, 128], "bfloat16"),
     "A": ("sbuf", [128, 128], "bfloat16"), "nA": ("sbuf", [128, 128], "bfloat16"),
     "dS": ("sbuf", [128, 128], "bfloat16"), "dN": ("sbuf", [128, 128], "bfloat16"),
     "hI": ("sbuf", [128, 128], "bfloat16"), "qI": ("sbuf", [128, 128], "bfloat16"),
     "sdrep": ("sbuf", [128, 512], "bfloat16"), "sdblk": ("sbuf", [128, FB], "bfloat16"),
-    "L0": ("sbuf", [128, 400], "bfloat16"), "L1": ("sbuf", [128, 400], "bfloat16"), "L2": ("sbuf", [128, 400], "bfloat16"),
+    "L0": ("sbuf", [128, 400], "bfloat16"), "L1": ("sbuf", [128, 400], "bfloat16"), "L2": ("sbuf", [128, NB], "bfloat16"),
     "Lg": ("sbuf", [128, 512], "bfloat16"), "fsend": ("sbuf", [128, NB], "bfloat16"),
     "xsend": ("sbuf", [128, NB], "bfloat16"), "ysend": ("sbuf", [128, NB], "bfloat16"),
     "io384": ("sbuf", [128, NB], "bfloat16"), "binv": ("sbuf", [128, 64], "uint16"),
-    "c2b": ("sbuf", [128, 768], "bfloat16"), "c2w": ("sbuf", [128, 1024], "bfloat16"),
+    "c2w": ("sbuf", [128, 1024], "bfloat16"),
     "tlb": ("sbuf", [128, 1], "bfloat16"), "tlf": ("sbuf", [128, 1], "float32"), "rec": ("sbuf", [128, 1], "float32"),
     "warm": ("sbuf", [128, 8], "float32"),
     "flw": ("sbuf", [128, 33], "bfloat16"), "one32": ("sbuf", [128, 32], "float32"),
     "pp": ("sbuf", [128, 32], "float32"), "sl": ("sbuf", [128, 32], "float32"), "sl16": ("sbuf", [128, 32], "uint16"),
     "zz": ("sbuf", [128, 32], "float32"), "t512": ("sbuf", [128, 32], "float32"),
-    "itp": ("sbuf", [128, 128], "int32"), "it2": ("sbuf", [128, 128], "int32"), "it3": ("sbuf", [128, 32], "int32"),
+    "itp": ("sbuf", [128, 1], "int32"), "g16": ("sbuf", [128, 1], "float32"),
     "mw": ("sbuf", [128, CAP + 1536], "bfloat16"), "memrep": ("sbuf", [128, 1536], "bfloat16"),
     "memblk": ("sbuf", [128, FB], "bfloat16"), "w1blk": ("sbuf", [128, 2 * FB], "bfloat16"),
     "w2blk": ("sbuf", [128, 2 * FB], "float32"), "w2bb": ("sbuf", [128, 2 * FB], "bfloat16"),
-    "L2f": ("sbuf", [128, NB], "float32"), "nI": ("sbuf", [128, 128], "bfloat16"),
+    "nI": ("sbuf", [128, 128], "bfloat16"),
     "w3bb": ("sbuf", [128, FB], "bfloat16"), "w3blk": ("sbuf", [128, FB], "float32"), "yfb": ("sbuf", [128, FB], "bfloat16"),
     "nr": ("sbuf", [128, 2048], "bfloat16"), "pd": ("psum", [128, 2048], "float32"), "cnt": ("psum", [128, 1024], "float32"),
     "psA": ("psum", [128, 512], "float32"), "psB": ("psum", [128, 512], "float32"),
@@ -234,10 +235,10 @@ def rank_program(g, core, T, topo):
             n = len(es) // 4
             a, b = topo.chip(core), topo.chip(to)
             if topo.mates(a, b) or topo.same_plane(a, b):
-                mine = es[at:at + n]
+                mine = es[0::2][at:at + n]
                 at += n
             else:
-                mine = es[2 * n:]
+                mine = es[1::2]
             rid, pid, _ = topo.addr(to)
             c0 = col + (d - 1) * BK
             trs.append(RemoteDMATransfer(dst_ids=[DstId(rid=rid, pnc=pid)], dma_engine_mask=sum(1 << e for e in mine),
@@ -249,8 +250,11 @@ def rank_program(g, core, T, topo):
         total["rs_" + name] = cnt
         ev = ("rs_" + name, cnt)
         clock[ev] = {"rs_" + name: cnt}
-        recs[dst] = [e for e in recs.get(dst, []) if not (col <= e[0] and e[1] <= col + NB)]
-        recs[dst].append((col, col + NB, True, "r", ev))
+        recs[dst] = [e for e in recs.get(dst, []) if not (col <= e[0] and e[1] <= col + 3 * BK)]
+        recs[dst].append((col, col + 3 * BK, True, "r", ev))
+
+    def landed(name):
+        need("y", [("rs_" + name, total["rs_" + name])])
 
     def cmat(r):
         return ("C", 128 * r, 128 * r + 128)
@@ -259,7 +263,6 @@ def rank_program(g, core, T, topo):
         return T[blk][:, 0:n], T[win][0::16, 0:16 * n]
 
     def pack(s):
-        mm(("psB",), ("kI",), ("xw", BS * s, BS * s + BS), True, True)
         tt(("cdf",), ("cdt", BS * s, BS * s + BS), ("psB",), OP.add)
 
     def offsets(s, a, b):
@@ -267,8 +270,11 @@ def rank_program(g, core, T, topo):
 
     def sfill(o, c):
         n, a, b = reg(o)
-        for k in range(a, b, 1024):
-            act((n, k, min(b, k + 1024)), ("ones", 0, min(b, k + 1024) - k), AF.Copy, scale=c)
+        act(o, ("ones" if c else "C", 0, b - a), AF.Copy, scale=c)
+
+    def scaled(mats):
+        for n, m, c in mats:
+            act((n,), (m,), AF.Copy, scale=c)
 
     def lists(s):
         now, was = ("flw", 1, 33), ("flw", 0, 32)
@@ -279,12 +285,17 @@ def rank_program(g, core, T, topo):
         tc("v", ("sl16",), ("sl",))
 
     def compact(s):
+        act(("zz",), ("pp",), AF.Identity, scale=8192.0, bias=-255.0 * 8192)
         sca(("comp",), ("sl16",), ("cdf",))
         offsets(s, 0, 64)
 
     def slots(s):
-        ts(("zz",), ("pp",), 255.5, OP.is_gt, 8192.0, OP.mult)
-        tt(("zz",), ("pp",), ("zz",), OP.add)
+        if s == 0:
+            ts(("itp",), ("itp",), 112, OP.bitwise_and)
+            tc("v", ("g16",), ("itp",))
+            for k in range(3):
+                ts(("vs%d" % k,), ("t512",), ("g16",), OP.subtract, float(BS * k - CAP), OP.add)
+        tt(("zz",), ("pp",), ("zz",), OP.max)
         tt(("zz",), ("zz",), ("vs%d" % s,), OP.min)
         tc("v", ("sb16_%d" % s,), ("zz",))
 
@@ -298,13 +309,9 @@ def rank_program(g, core, T, topo):
             tc("s", ("c2w",), ("w2", 2 * BS * s, 2 * BS * s + 1024))
 
         def own():
-            a, i = 2 * BS * s, ("ident",)
-            sums(("psA",), [(i, ("w1", a, a + 1024, 2)), (i, ("w1", a + 1, a + 1024, 2)), (i, ("c2w", 0, 1024, 2)), (i, ("c2w", 1, 1024, 2))])
-
-        def row():
-            tc("s", ("orow",), ("psA",))
-            for r in range(16):
-                mm(("psA", 0, 32), cmat(r), ("orow", r, 512, 16), r == 0, False)
+            for n, a in (("w1", 2 * BS * s), ("c2w", 0)):
+                for k in range(32):
+                    mm(("psA", 0, 32), cmat(k // 2), (n, a + k, a + 1024, 32), n == "w1" and k == 0, False)
 
         def theirs():
             w, k = ("L%d" % (s - 1),), 32 * s - 32
@@ -319,6 +326,14 @@ def rank_program(g, core, T, topo):
         def send_y():
             need("g", [("rs_f0", total["rs_f0"])])
             send("y", "ysend", "ya", YO + P, 1)
+            iota(("mw", 0, CAP), [[0, CAP]], 2, 0)
+            iota(("mw", CAP, CAP + 3 * BS), [[0, 3 * BS]], 1, 0)
+            iota(("d0",), [[0, 128], [-200, 16]], 191, 0)
+            landed("y")
+            dma("y", "cd2", [(T.cdt[:, 2 * BS:3 * BS], T.cd[:, 2 * BS:3 * BS])], [], [("cdt", 2 * BS, 3 * BS)])
+            dma("y", "yb", [(T.yb[:, YO:YO + P], T.y0[:, :])], [], [("yb", YO, YO + P)])
+            dma("y", "sk", [(T.sdblk[0::16, :], T.sd[:, 0:FB]), (T.sdblk[1::16, 0:BS - FB], T.sd[:, FB:BS])], [], [("sdblk",)])
+            dma("y", "z3", [blocks("zf", "w3", FB)[::-1]], [("zf",)], [("w3",)])
 
         def gs(a, b):
             gat("s", (cand, 16 * a, 16 * b), win, (off, a, b))
@@ -336,22 +351,22 @@ def rank_program(g, core, T, topo):
                 ts(("nr", k, k + n), ("pd", k, k + n), RND, OP.add, RND, OP.not_equal)
 
         def cnt(a, b):
-            k = a + (384 if out and a >= 128 else 0)
+            k = a + (512 - LAST[s] if out and a >= LAST[s] else 0)
             return ("cnt", k, k + b - a)
 
         def C(c):
             k = 1024 * (c % 2)
-            sums(cnt(64 * c, 64 * c + 64), [(("fB",), ("ones", 0, 64))] + [(cmat(i), ("nr", k + 64 * i, k + 64 * i + 64)) for i in range(16)])
+            sums(cnt(64 * c, 64 * c + 64), [(("fB",), ("ones", 0, 64))] * out + [(cmat(i), ("nr", k + 64 * i, k + 64 * i + 64)) for i in range(16)])
 
         def Pt(a=0, b=CAP):
             cn = cnt(a, b)
             if out:
-                m = ("cnt", cn[1] + 128, cn[2] + 128)
-                tt(m, cn, ("vt", a, b), OP.max)
+                m = ("cnt", cn[1] + 256, cn[2] + 256)
+                tt(m, cn, ("comp", a, b), OP.max)
                 tt(m, m, ("trash", a % 128, a % 128 + b - a), OP.min)
                 tc("v", ("vo", a, b), m)
             else:
-                ts(("mt", a, b), cn, 0.0, OP.is_lt)
+                ts(("mt", a, b), cn, FAR, OP.is_lt)
                 mm(("psA", a, b), ("B",), ("mt", a, b), True, True)
 
         def S(a, b):
@@ -363,11 +378,15 @@ def rank_program(g, core, T, topo):
 
         def G():
             tc("s", ("c2b",), ("w2", 2 * P, ST))
+            for k, ps in enumerate(("psA", "psB")):
+                for b in range(2):
+                    mm((ps, 0, NB // 2), ("ident",), ("c2b", NB * k + b, NB * k + NB, 2), b == 0, False)
 
         def F():
-            i = ("ident",)
-            sums(("psB", 0, NB), [(i, ("c2b", 0, 768, 2)), (i, ("c2b", 1, 768, 2)), (i, ("w1", 2 * P, ST, 2)), (i, ("w1", 2 * P + 1, ST, 2))])
-            tc("v", ("fsend",), ("psB", 0, NB))
+            for k, ps in enumerate(("psA", "psB")):
+                for b in range(2):
+                    mm((ps, 0, NB // 2), ("ident",), ("w1", 2 * P + NB * k + b, 2 * P + NB * k + NB, 2), False, b == 1)
+                tc("sv"[k] if s < 2 else "v", ("fsend", NB // 2 * k, NB // 2 * (k + 1)), (ps, 0, NB // 2))
             send("f%d" % s, "fsend", "L%d" % s, 0, -1)
 
         def N(a, b):
@@ -385,41 +404,54 @@ def rank_program(g, core, T, topo):
             ts(m, ("psA", a, b), 1.5, OP.is_ge, 255.0, OP.mult)
             tt((wn, a, b), ("hi", a, b), m, OP.max)
 
-        def U():
-            a = YO + BS * s
-            gat("s", (ot, a + 256, a + 512), (wn, 0, YO + P), ("sb16_%d" % s, 16, 32))
-            gat("v", (ot, a, a + 256), (wn, 0, YO + P), ("sb16_%d" % s, 0, 16))
+        def O():
+            r = (ot, YO + BS * s, YO + BS * s + BS)
+            if s:
+                landed("b%d" % s)
+            dma("s" if s == 0 else "y", "o%d" % s, [(T.yv[:, BS * s:BS * s + BS], ap(r))], [r], [])
 
-        def Y():
+        def U(k=16):
+            a = YO + BS * s
+            if k < 32:
+                gat("s", (ot, a + 16 * k, a + 512), (wn, 0, YO + P), ("sb16_%d" % s, k, 32))
+            if k:
+                gat("v", (ot, a, a + 16 * k), (wn, 0, YO + P), ("sb16_%d" % s, 0, k))
+
+        def Y(k=12):
             w = (ot, YO, YO + P)
-            gat("s", ("ysend", 192, 384), w, ("snd16", 12, 24))
-            gat("v", ("ysend", 0, 192), w, ("snd16", 0, 12))
+            if k < 24:
+                gat("s", ("ysend", 16 * k, 384), w, ("snd16", k, 24))
+            if k:
+                gat("v", ("ysend", 0, 16 * k), w, ("snd16", 0, k))
             send("b%d" % s, "ysend", ot, YO + P, 1)
             r = (YO + BS * s, YO + BS * s + BS)
-            dma("y", "o%d" % s, [(T.yv[:, BS * s:BS * s + BS], ap((ot,) + r))], [(ot,) + r], [])
             if s == 2:
+                landed("b2")
                 dma("y", "cy", [(ap((wn,) + r), ap((ot,) + r))], [(ot,) + r], [(wn,) + r])
 
         def ck():
             offsets(s, 64, 256)
 
-        def marks():
-            ts(("vt",), ("comp", 0, CAP), -0.25, OP.add)
-            tt((xm,), ("comp", 0, CAP), ("vt",), OP.subtract)
+        def marks(a=0, b=CAP):
+            r = ("psA", CAP + a, CAP + b)
+            ts(r, ("comp", a, b), RND, OP.add, -RND, OP.add)
+            tt((xm, a, b), ("comp", a, b), r, OP.subtract)
 
         def R():
             w, o, i = ("w3",), ("snd16",), ("L2f",)
-            act(i, ("L2", 0, NB), AF.Copy, scale=30.0)
+            act(i, ("L2",), AF.Copy, scale=30.0)
             op("s", lambda: g.scalar.activation(ap(w).indirect(ap(o)), ap(i), AF.Tanh), [o, i], [w])
             dma("y", "bl3", [blocks("w3blk", "w3", FB)], [w], [("w3blk",)])
 
         def M():
             gat("s", ("memrep", BS * s, BS * s + BS), ("mw",), ("sb16_%d" % s,))
             if s == 2:
-                dma("y", "bl2", [blocks("w2blk", "w2", 2 * FB)], [("w2", 0, 2 * P)], [("w2blk",)])
-                dma("y", "bl1", [blocks("w1blk", "w1", 2 * FB)], [("w1", 0, 2 * P)], [("w1blk",)])
                 dma("y", "blm", [(T.memblk[b::16, 0:min(FB, 1536 - FB * b)], T.memrep[b::16, FB * b:min(1536, FB * b + FB)])
                                  for b in range(5)], [("memrep",)], [("memblk",)])
+
+        def own_blocks():
+            dma("y", "bl2", [blocks("w2blk", "w2", 2 * FB)], [("w2", 0, 2 * P)], [("w2blk",)])
+            dma("y", "bl1", [blocks("w1blk", "w1", 2 * FB)], [("w1", 0, 2 * P)], [("w1blk",)])
 
         def W():
             tc("s", ("w2bb",), ("w2blk",))
@@ -434,12 +466,12 @@ def rank_program(g, core, T, topo):
             tt(("yfb",), ("cnt", 512, 512 + FB), ("memblk",), OP.min)
             dma("y", "of", [(T.yf[:, :], T.yfb[:, :])], [("yfb",)], [])
 
-        def O():
-            dma("s", "o0", [(T.yv[:, 0:BS], T.yb[:, YO:YO + BS])], [("yb", YO, YO + BS)], [])
-        return {"s": gs, "v": gv, "X": X, "L": L, "C": C, "P": Pt, "S": S, "V": V, "F": F, "G": G, "N": N, "H": H,
-                "K": lambda c: L(c, 512), "h": hv, "E": E, "e": e, "O": O, "z": lambda: slots(s),
-                "w": wide, "o": own, "r": row, "t": theirs, "y": first_y, "Z": send_y,
-                "a": lambda: pack(s), "l": lambda: lists(s), "n": lambda: compact(s),
+        return {"O": O, "B": own_blocks, "s": gs, "v": gv, "X": X, "L": L, "C": C, "P": Pt, "S": S, "V": V, "F": F, "G": G, "N": N, "H": H,
+                "K": lambda c: L(c, 512), "h": hv, "E": E, "e": e, "z": lambda: slots(s),
+                "w": wide, "o": own, "t": theirs, "y": first_y, "Z": send_y,
+                "a": lambda: mm(("psB",), ("kI",), ("xw", BS * s, BS * s + BS), True, True), "A": lambda: pack(s),
+                "l": lambda: lists(s), "n": lambda: compact(s),
+                "b": lambda: scaled((("hX", "ident", XS / 2), ("hI", "ident", 0.5), ("qI", "ident", -0.25), ("nI", "ident", -1.0))),
                 "f": lambda: sfill(("comp", 0, CAP), 255 / XS), "D": D, "U": U, "Y": Y, "m": marks, "c": ck, "R": R, "M": M, "W": W}
 
     streams = {n: stream(n) for n in ("f0", "f1", "f2", "b2", "b1", "b0")}
@@ -453,72 +485,63 @@ def rank_program(g, core, T, topo):
         TAG[0] = ""
 
     h = P // 2
-    dma("y", "xa", [(T.xw[:, 0:h], T.x[:, 0:h])], [], [("xw", 0, h)])
     dma("s", "snd", [(T.snd32[:, :], T.snd[:, :])], [], [("snd32",)])
-    dma("s", "tl", [(T.tlb[:, :], T.tl[:, :])], [], [("tlb",)])
+    dma("y", "tl", [(T.tlb[:, :], T.tl[:, :])], [], [("tlb",)])
     dma("s", "xb", [(T.xw[:, h:P], T.x[:, h:P])], [], [("xw", h, P)])
-    fill(("ones",), 1.0)
+    dma("y", "xa", [(T.xw[:, 0:h], T.x[:, 0:h])], [], [("xw", 0, h)])
+    fill(("ones", 0, CAP), 1.0)
     fill(("sdrep",), 0.0)
     dma("y", "sd", [(T.sdrep[0::16, :], T.sd[:, :])], [], [("sdrep",)])
     dma("y", "cd0", [(T.cdt[:, 0:BS], T.cd[:, 0:BS])], [], [("cdt", 0, BS)])
 
     sel(("B",), ("ones", 0, 128), [[-16, 8], [0, 16]], OP.is_ge, 0.0, 0, 1)
     sel(("B",), ("B",), [[16, 8], [0, 16]], OP.is_ge, 0.0, 15, -1)
-    sel(("ident",), ("ones", 0, 128), [[-1, 128]], OP.is_equal, 0.0, 0, 1)
     iota(("io384",), [[1, NB]], -NB // 2, 0)
-    iota(("itp",), [[0, 128]], 0, 1)
-    iota(("it3",), [[16, 32]], BS, 0)
+    sel(("ident",), ("ones", 0, 128), [[-1, 128]], OP.is_equal, 0.0, 0, 1)
     sel(("A",), ("B",), [[1, 128]], OP.is_gt, 0.0, 0, -1)
     sel(("A",), ("A",), [[-1, 128]], OP.not_equal, -BIG, 0, 1)
-    iota(("it2",), [[0, 2], [16, 64]], ST, 0)
+    iota(("t512",), [[16, 32]], BS, 1)
+    iota(("itp",), [[0, 1]], 0, 1)
 
     fill(("C",), 0.0)
     act(("warm",), ("ones", 0, 8), AF.Tanh)
     for q in range(8):
         act(("C", 16 * q, 16 * q + 129 * 15 + 1, 129), ("B", 16 * q, 16 * q + 16), AF.Copy, scale=CS)
-    for n, m, c in (("kI", "ident", 1.0 / XS), ("fB", "B", -FAR / 16), ("hX", "ident", XS / 2),
-                    ("hI", "ident", 0.5), ("qI", "ident", -0.25), ("nI", "ident", -1.0), ("nA", "A", -1.0)):
-        act((n,), (m,), AF.Copy, scale=c)
-    fill(("w1", 2 * P, ST), 0.0)
+    scaled((("nA", "A", -1.0),))
     fill(("w1", BS, 3 * BS), float(NB // 2))
+    tc("v", ("snd16",), ("snd32",))
+    sca(("w1", 0, P), ("snd16",), ("io384",))
     fill(("one32",), 1.0)
     fill(("flw", 0, 1), 0.0)
-    tc("v", ("snd16",), ("snd32",))
+    fill(("zb",), 0.0)
+    sums(("psB", 0, 64), [(cmat(r), ("w1", BS + r, 3 * BS, 16)) for r in range(16)])
     ts(("tlf",), ("tlb",), 2.0, OP.mult, 1.0, OP.add)
     op("v", lambda: g.vector.reciprocal(ap(("rec",)), ap(("tlf",))), [("tlf",)], [("rec",)])
-    sca(("w1", 0, P), ("snd16",), ("io384",))
-    sums(("psB", 0, 64), [(cmat(r), ("w1", BS + r, 3 * BS, 16)) for r in range(16)])
-    ts(("itp",), ("itp",), 15, OP.bitwise_and)
     ts(("dS",), ("ident",), ("rec",), OP.mult)
-    tt(("t512",), ("it3",), ("itp", 0, 32), OP.add)
-    tt(("trash",), ("it2",), ("itp",), OP.add)
-    ts(("binv",), ("psB", 0, 64), 1.0 / (16 * CS), OP.mult, float(NB // 2), OP.add)
-    act(("dN",), ("dS",), AF.Copy, scale=-XS)
-    sfill(("comp", 0, CAP), 255 / XS)
-    for s in range(3):
-        ts(("vs%d" % s,), ("t512",), float(512 * s - 256), OP.add)
 
     gat("s", ("xsend", 192, NB), ("xw", 0, P), ("snd16", 12, 24))
     gat("v", ("xsend", 0, 192), ("xw", 0, P), ("snd16", 0, 12))
     send("x", "xsend", "xw", P, 1)
+    ts(("binv",), ("psB", 0, 64), 1.0 / (16 * CS), OP.mult, float(NB // 2), OP.add)
+    scaled((("kI", "ident", 1.0 / XS),))
     sfill(("zf",), 0.0)
+    for name, win, z in (("z1", "w1", "zb"), ("z2", "w2", "zf")):
+        dma("y", name, [(T[win][0::16, a:b], T[z][:, 0:(b - a) // 16]) for a, b in ((0, 1024), (3072, 2 * P))], [(z,)],
+            [(win, 0, 1024), (win, 3072, 2 * P)])
+    sfill(("comp", 0, CAP), 255 / XS)
+    scaled((("dN", "dS", -XS), ("fB", "B", -FAR / 16)))
     sfill(("w2", 1024, 3072), 0.0)
-    sfill(("w2", 2 * P, ST), 0.0)
-    for r, c in ((("zb",), 0), (("cst",), 30), (("sdblk",), 0), (("L0", NB, 400), 0), (("L1", NB, 400), 0), (("memblk",), 1),
-                 (("mw", 0, CAP), 2), (("mw", CAP, CAP + 1536), 1)):
+    iota(("trash",), [[16, 128]], ST, 1)
+    for r, c in ((("cst",), 30), (("w2", 2 * P, ST), 0), (("w1", 2 * P, ST), 0), (("ones", CAP, width("ones")), 1),
+                 (("L0", NB, 400), 0), (("L1", NB, 400), 0), (("sdblk",), 0), (("memblk",), 1)):
         iota(r, [[0, reg(r)[2] - reg(r)[1]]], c, 0)
-    iota(("d0",), [[0, 128], [-200, 16]], 191, 0)
     sums(("psA", 0, 32), [(cmat(r), ("sdrep", r, BS, 16)) for r in range(16)])
-    fill(("w1", 1024, 3072), 0.0)
     play("pre0")
-    need("y", [("rs_x", total["rs_x"])])
-    dma("y", "z2", [blocks("zf", "w2", 2 * FB)[::-1]], [("zf",)], [("w2", 0, 2 * P)])
-    dma("y", "z1", [blocks("zb", "w1", 2 * FB)[::-1]], [("zb",)], [("w1", 0, 2 * P)])
-    dma("y", "cd1", [(T.cdt[:, BS:3 * BS], T.cd[:, BS:3 * BS])], [], [("cdt", BS, 3 * BS)])
+    fill(("w1", 1024, 2304), 0.0)
+    sfill(("w1", 2304, 3072), 0.0)
+    landed("x")
     dma("y", "ya", [(T.ya[:, YO:YO + P], T.y0[:, :])], [], [("ya", YO, YO + P)])
-    dma("y", "yb", [(T.yb[:, YO:YO + P], T.y0[:, :])], [], [("yb", YO, YO + P)])
-    dma("y", "sk", [(T.sdblk[0::16, :], T.sd[:, 0:FB]), (T.sdblk[1::16, 0:BS - FB], T.sd[:, FB:BS])], [], [("sdblk",)])
-    dma("y", "z3", [blocks("zf", "w3", FB)[::-1]], [("zf",)], [("w3",)])
+    dma("y", "cd1", [(T.cdt[:, BS:2 * BS], T.cd[:, BS:2 * BS])], [], [("cdt", BS, 2 * BS)])
 
     for key in ("out0", "to1", "out1", "to2", "back2", "gap1", "back1", "gap0", "back0"):
         play(key)

from concourse.bass import DstId, RemoteDMATransfer
from concourse.mybir import AluOpType as OP, ActivationFunctionType as AF

P, PL, NB, BS, CAP, BK = 5376, 5760, 384, 512, 256, 128
ST = 2 * PL
WW = ST + 2176
BIG = 2048.0
CS = 32768.0
FAR = 7.5 * CS
RND = 12582912.0
YO = CAP
FB = P // 16
XS = 512.0
TAG = [""]

FT = (" s128-192 X1 K0 C0 s192-256 K1 P0-64 X2 S0-64 C1 X3 L2 P64-128 C2 K3 S80-128 V64-80 C3 P128-256"
      " S128-164 V164-256 G F")
BS_ = " s0-32 v32-64 s64-92 X0 v92-128"
BT = " s128-192 X1 K0 s192-256 X2 C0 N0-2 L1 X3 C1 L2 N2-3 C2 "
BE = " K3 N3-4 C3 H P h "
LAST = (128, 128, 128)
SCHED = {
    "pre0": "f0 l a A n c m",
    "out0": "f0 s0-32 v32-64 s64-88 X0 v88-128" + FT,
    "to1": "f1 w o a f ; f0 z y ; f1 t A b ; f0 Z ; f1 l n",
    "out1": "f1 s0-56 c m v56-64 X0 v64-112 s112-128" + FT,
    "to2": "f2 w o a f ; f0 M ; f1 z M ; f2 t A l n",
    "back2": "b2 s0-56 c m v56-64 X0 v64-96 s96-128 z" + BT + "; f2 s0-64 s64-128 s128-192 ; b2" + BE + "D U12 Y0 O",
    "gap1": "f2 X0 s192-256 X1 L0 C0 L1 X2 P0-64 S0-64 C1 X3 L2 C2 K3 P64-128 C3 P128-256",
    "back1": "b1" + BS_ + BT + "; f2 S64-128 S128-142 ; b1" + BE + "D U Y",
    "gap0": "f2 S142-192 V192-256 G F B",
    "back0": "b0" + BS_ + BT + "R ; f2 M ; b1 O ; b0 W" + BE + "E D U e O",
}

SCRATCH = {
    "xw": ("sbuf", [128, PL], "bfloat16"),
    "ya": ("sbuf", [128, YO + PL], "bfloat16"), "yb": ("sbuf", [128, YO + PL], "bfloat16"),
    "cdt": ("sbuf", [128, 1536], "int32"), "comp": ("sbuf", [128, 1152], "float32"),
    "c2b": ("sbuf", [128, 2 * NB], "bfloat16"), "L2f": ("sbuf", [128, NB], "float32"),
    "cdf": ("sbuf", [128, 512], "float32"), "kI": ("sbuf", [128, 128], "bfloat16"),
    "hX": ("sbuf", [128, 128], "bfloat16"), "fB": ("sbuf", [128, 128], "bfloat16"),
    "snd32": ("sbuf", [128, 24], "int32"), "snd16": ("sbuf", [128, 24], "uint16"),
    "cf": ("sbuf", [128, 4096], "bfloat16"), "cb": ("sbuf", [128, 4096], "bfloat16"),
    "scn": ("sbuf", [128, 4096], "bfloat16"),
    "d0": ("sbuf", [128, 2048], "bfloat16"), "mt": ("sbuf", [128, 256], "bfloat16"), "hi": ("sbuf", [128, 256], "float32"),
    "vo": ("sbuf", [128, 256], "uint16"), "trash": ("sbuf", [128, 128], "float32"),
    "w1": ("sbuf", [128, WW], "bfloat16"), "w2": ("sbuf", [128, WW], "float32"), "w3": ("sbuf", [128, P], "float32"),
    "zb": ("sbuf", [128, 480], "bfloat16"), "zf": ("sbuf", [128, 480], "float32"),
    "ones": ("sbuf", [128, 1536], "bfloat16"), "cst": ("sbuf", [128, 1024], "float32"),
    "C": ("sbuf", [128, 2048], "bfloat16"),
    "ident": ("sbuf", [128, 128], "bfloat16"), "B": ("sbuf", [128, 128], "bfloat16"),
    "A": ("sbuf", [128, 128], "bfloat16"), "nA": ("sbuf", [128, 128], "bfloat16"),
    "dS": ("sbuf", [128, 128], "bfloat16"), "dN": ("sbuf", [128, 128], "bfloat16"),
    "hI": ("sbuf", [128, 128], "bfloat16"), "qI": ("sbuf", [128, 128], "bfloat16"),
    "sdrep": ("sbuf", [128, 512], "bfloat16"), "sdblk": ("sbuf", [128, FB], "bfloat16"),
    "L0": ("sbuf", [128, 400], "bfloat16"), "L1": ("sbuf", [128, 400], "bfloat16"), "L2": ("sbuf", [128, NB], "bfloat16"),
    "Lg": ("sbuf", [128, 512], "bfloat16"), "fsend": ("sbuf", [128, NB], "bfloat16"),
    "xsend": ("sbuf", [128, NB], "bfloat16"), "ysend": ("sbuf", [128, NB], "bfloat16"),
    "io384": ("sbuf", [128, NB], "bfloat16"), "binv": ("sbuf", [128, 64], "uint16"),
    "c2w": ("sbuf", [128, 1024], "bfloat16"),
    "tlb": ("sbuf", [128, 1], "bfloat16"), "tlf": ("sbuf", [128, 1], "float32"), "rec": ("sbuf", [128, 1], "float32"),
    "warm": ("sbuf", [128, 8], "float32"),
    "flw": ("sbuf", [128, 33], "bfloat16"), "one32": ("sbuf", [128, 32], "float32"),
    "pp": ("sbuf", [128, 32], "float32"), "sl": ("sbuf", [128, 32], "float32"), "sl16": ("sbuf", [128, 32], "uint16"),
    "zz": ("sbuf", [128, 32], "float32"), "t512": ("sbuf", [128, 32], "float32"),
    "itp": ("sbuf", [128, 1], "int32"), "g16": ("sbuf", [128, 1], "float32"),
    "mw": ("sbuf", [128, CAP + 1536], "bfloat16"), "memrep": ("sbuf", [128, 1536], "bfloat16"),
    "memblk": ("sbuf", [128, FB], "bfloat16"), "w1blk": ("sbuf", [128, 2 * FB], "bfloat16"),
    "w2blk": ("sbuf", [128, 2 * FB], "float32"), "w2bb": ("sbuf", [128, 2 * FB], "bfloat16"),
    "nI": ("sbuf", [128, 128], "bfloat16"),
    "w3bb": ("sbuf", [128, FB], "bfloat16"), "w3blk": ("sbuf", [128, FB], "float32"), "yfb": ("sbuf", [128, FB], "bfloat16"),
    "nr": ("sbuf", [128, 2048], "bfloat16"), "pd": ("psum", [128, 2048], "float32"), "cnt": ("psum", [128, 1024], "float32"),
    "psA": ("psum", [128, 512], "float32"), "psB": ("psum", [128, 512], "float32"),
}
for _s in range(3):
    SCRATCH["c16_%d" % _s] = ("sbuf", [128, 256], "uint16")
    SCRATCH["xm%d" % _s] = ("sbuf", [128, 256], "bfloat16")
    SCRATCH["sb16_%d" % _s] = ("sbuf", [128, 32], "uint16")
    SCRATCH["vs%d" % _s] = ("sbuf", [128, 32], "float32")

_EX = ["x", "f0", "y", "f1", "b2", "f2", "b1"]
_DM = ["snd", "xa", "xb", "tl", "sd", "cd0", "cd1", "cd2", "sk", "z1", "z2", "z3", "ya", "yb", "bl1", "bl2", "bl3", "blm", "cy",
       "o2", "o1", "o0", "of"]
SEMAPHORES = ["qv", "qs", "qt", "qg"] + ["ls_" + e for e in _EX] + ["rs_" + e for e in _EX] + ["d_" + d for d in _DM]


def rank_program(g, core, T, topo):
    rank = T.rank_of(core)
    if rank is None:
        return
    nr_ranks = len(T.cores)
    eng = {"v": g.vector, "s": g.scalar, "t": g.tensor, "g": g, "y": g.sync}
    known = {q: {} for q in eng}
    clock = {}
    total = {}
    recs = {}

    def width(n):
        return SCRATCH[n][1][1]

    def reg(r):
        return r[0], (r[1] if len(r) > 1 else 0), (r[2] if len(r) > 2 else width(r[0]))

    def is_ps(n):
        return SCRATCH[n][0] == "psum"

    def banks(a, b):
        return a // 512 * 512, -(-b // 512) * 512

    def ap(r):
        n, a, b = reg(r)
        if len(r) > 3:
            return T[n][:, a:b:r[3]]
        return T[n][:, a:b]

    def need(q, evs):
        best = {}
        for sem, n in evs:
            if known[q].get(sem, 0) < n and best.get(sem, 0) < n:
                best[sem] = n
        for sem in list(best):
            n = best[sem]
            if any(o != sem and clock[(o, m)].get(sem, 0) >= n for o, m in best.items()):
                del best[sem]
        for sem, n in best.items():
            eng[q].wait_ge(T.sem[sem], n)
            for k, m in clock[(sem, n)].items():
                if known[q].get(k, 0) < m:
                    known[q][k] = m

    def deps(q, R, W):
        evs = []
        for r, w in [(r, is_ps(r[0])) for r in R] + [(r, True) for r in W]:
            n, a, b = reg(r)
            if is_ps(n):
                a, b = banks(a, b)
            for c0, c1, iw, qq, ev in recs.get(n, []):
                if c0 < b and a < c1 and (w or iw) and not (q == "t" and qq == "t"):
                    evs.append(ev)
        return evs

    def note(q, R, W, ev):
        for r in W:
            n, a, b = reg(r)
            if is_ps(n):
                a, b = banks(a, b)
                recs[n] = [e for e in recs.get(n, []) if not (a <= e[0] and e[1] <= b)]
            elif len(r) <= 3:
                recs[n] = [e for e in recs.get(n, []) if not (a <= e[0] and e[1] <= b)]
            recs.setdefault(n, []).append((a, b, True, q, ev))
        for r in R:
            n, a, b = reg(r)
            if is_ps(n):
                a, b = banks(a, b)
                recs[n] = [e for e in recs.get(n, []) if not (a <= e[0] and e[1] <= b)] + [(a, b, True, q, ev)]
            else:
                recs.setdefault(n, []).append((a, b, False, q, ev))

    def event(q, sem, n):
        total[sem] = total.get(sem, 0) + n
        ev = (sem, total[sem])
        clock[ev] = dict(known[q])
        clock[ev][sem] = total[sem]
        return ev

    def op(q, fn, R, W):
        need(q, deps(q, R, W))
        sem = "q" + q
        fn().then_inc(T.sem[sem], 1)
        note(q, R, W, event(q, sem, 1))

    def dma(q, name, pairs, R, W):
        need(q, deps(q, R, W))
        for o, i in pairs:
            eng[q].dma_start(o, i).then_inc(T.sem["d_" + name], 16)
        note(q, R, W, event(q, "d_" + name, 16 * len(pairs)))

    def act(o, i, f, **k):
        op("s", lambda: g.scalar.activation(ap(o), ap(i), f, **k), [i], [o])

    def tc(q, o, i):
        if q == "v":
            op("v", lambda: g.vector.tensor_copy(ap(o), ap(i)), [i], [o])
        else:
            act(o, i, AF.Copy)

    def gat(q, o, win, off):
        if q == "v":
            op("v", lambda: g.vector.tensor_copy(ap(o), ap(win).indirect(ap(off))), [win, off], [o])
        else:
            op("s", lambda: g.scalar.activation(ap(o), ap(win).indirect(ap(off)), AF.Copy), [win, off], [o])

    def sca(win, off, i):
        op("v", lambda: g.vector.tensor_copy(ap(win).indirect(ap(off)), ap(i)), [i, off], [win])

    def tt(o, a, b, f):
        op("v", lambda: g.vector.tensor_tensor(ap(o), ap(a), ap(b), f), [a, b], [o])

    def ts(o, a, s1, f1, s2=None, f2=None):
        cols = [s for s in (s1, s2) if isinstance(s, tuple)]
        s1, s2 = [ap(s) if isinstance(s, tuple) else s for s in (s1, s2)]
        if f2 is None:
            op("v", lambda: g.vector.tensor_scalar(ap(o), ap(a), s1, None, f1), [a] + cols, [o])
        else:
            op("v", lambda: g.vector.tensor_scalar(ap(o), ap(a), s1, s2, f1, f2), [a] + cols, [o])

    def scan(o, d0, d1, first, f0, f1):
        op("v", lambda: g.vector.tensor_tensor_scan(ap(o), ap(d0), ap(d1), first, f0, f1), [d0, d1], [o])

    def fill(o, c):
        op("v", lambda: g.vector.memset(ap(o), c), [], [o])

    def mm(o, l, r, start, stop):
        op("t", lambda: g.tensor.matmul(ap(o), ap(l), ap(r), start, stop), [l, r], [o])

    def sums(o, terms):
        for k, (l, r) in enumerate(terms):
            mm(o, l, r, k == 0, k == len(terms) - 1)

    def sel(o, i, pattern, cmp, fl, base, cm):
        op("g", lambda: g.affine_select(ap(o), ap(i), pattern, cmp, fl, base, cm), [i], [o])

    def iota(o, pattern, base, cm):
        if SCRATCH[o[0]][2] == "int32":
            op("g", lambda: g.iota(ap(o), pattern, base, cm), [], [o])
        else:
            op("g", lambda: g.iota(ap(o), pattern, base, cm, allow_small_or_imprecise_dtypes=True), [], [o])

    def send(name, src, dst, col, sign):
        need("g", deps("g", [(src,)], []))
        trs, cnt, at = [], 0, 0
        for d in range(1, nr_ranks):
            to = T.cores[(rank + sign * d) % nr_ranks]
            es = topo.engines(core, to)
            n = len(es) // 4
            a, b = topo.chip(core), topo.chip(to)
            if topo.mates(a, b) or topo.same_plane(a, b):
                mine = es[0::2][at:at + n]
                at += n
            else:
                mine = es[1::2]
            rid, pid, _ = topo.addr(to)
            c0 = col + (d - 1) * BK
            trs.append(RemoteDMATransfer(dst_ids=[DstId(rid=rid, pnc=pid)], dma_engine_mask=sum(1 << e for e in mine),
                                         remote_sem=T.sem["rs_" + name], src=T[src][:, (d - 1) * BK:d * BK],
                                         dst=T[dst][:, c0:c0 + BK]))
            cnt += len(mine)
        g.remote_dma_fused(trs, local_sem=T.sem["ls_" + name])
        note("g", [(src,)], [], event("g", "ls_" + name, cnt))
        total["rs_" + name] = cnt
        ev = ("rs_" + name, cnt)
        clock[ev] = {"rs_" + name: cnt}
        recs[dst] = [e for e in recs.get(dst, []) if not (col <= e[0] and e[1] <= col + 3 * BK)]
        recs[dst].append((col, col + 3 * BK, True, "r", ev))

    def landed(name):
        need("y", [("rs_" + name, total["rs_" + name])])

    def cmat(r):
        return ("C", 128 * r, 128 * r + 128)

    def blocks(blk, win, n):
        return T[blk][:, 0:n], T[win][0::16, 0:16 * n]

    def pack(s):
        tt(("cdf",), ("cdt", BS * s, BS * s + BS), ("psB",), OP.add)

    def offsets(s, a, b):
        ts(("c16_%d" % s, a, b), ("comp", a, b), 0.5, OP.mult, -0.375, OP.add)

    def sfill(o, c):
        n, a, b = reg(o)
        act(o, ("ones" if c else "C", 0, b - a), AF.Copy, scale=c)

    def scaled(mats):
        for n, m, c in mats:
            act((n,), (m,), AF.Copy, scale=c)

    def lists(s):
        now, was = ("flw", 1, 33), ("flw", 0, 32)
        ts(now, ("psA", 0, 32), 0.25, OP.is_gt)
        sums(("psB", 0, 32), [(("A",), now), (("B",), was), (("nA",), was)])
        scan(("pp",), ("one32",), ("psB", 0, 32), BIG, OP.mult, OP.add)
        tt(("sl",), ("pp",), ("t512",), OP.min)
        tc("v", ("sl16",), ("sl",))

    def compact(s):
        act(("zz",), ("pp",), AF.Identity, scale=8192.0, bias=-255.0 * 8192)
        sca(("comp",), ("sl16",), ("cdf",))
        offsets(s, 0, 64)

    def slots(s):
        if s == 0:
            ts(("itp",), ("itp",), 112, OP.bitwise_and)
            tc("v", ("g16",), ("itp",))
            for k in range(3):
                ts(("vs%d" % k,), ("t512",), ("g16",), OP.subtract, float(BS * k - CAP), OP.add)
        tt(("zz",), ("pp",), ("zz",), OP.max)
        tt(("zz",), ("zz",), ("vs%d" % s,), OP.min)
        tc("v", ("sb16_%d" % s,), ("zz",))

    def stream(name):
        s, out = int(name[1]), name[0] == "f"
        wn, w0, cand = ("xw", 0, "cf") if out else (("ya", "yb")[s % 2], YO, "cb")
        ot = ("yb", "ya")[s % 2]
        win, off, xm = (wn, w0, w0 + PL), "c16_%d" % s, "xm%d" % s

        def wide():
            tc("s", ("c2w",), ("w2", 2 * BS * s, 2 * BS * s + 1024))

        def own():
            for n, a in (("w1", 2 * BS * s), ("c2w", 0)):
                for k in range(32):
                    mm(("psA", 0, 32), cmat(k // 2), (n, a + k, a + 1024, 32), n == "w1" and k == 0, False)

        def theirs():
            w, k = ("L%d" % (s - 1),), 32 * s - 32
            gat("s", ("Lg", 256, 512), w, ("binv", k + 16, k + 32))
            gat("v", ("Lg", 0, 256), w, ("binv", k, k + 16))
            for r in range(16):
                mm(("psA", 0, 32), cmat(r), ("Lg", r, 512, 16), False, r == 15)

        def first_y():
            gat("s", ("ysend",), ("ya", YO, YO + P), ("snd16",))

        def send_y():
            need("g", [("rs_f0", total["rs_f0"])])
            send("y", "ysend", "ya", YO + P, 1)
            iota(("mw", 0, CAP), [[0, CAP]], 2, 0)
            iota(("mw", CAP, CAP + 3 * BS), [[0, 3 * BS]], 1, 0)
            iota(("d0",), [[0, 128], [-200, 16]], 191, 0)
            landed("y")
            dma("y", "cd2", [(T.cdt[:, 2 * BS:3 * BS], T.cd[:, 2 * BS:3 * BS])], [], [("cdt", 2 * BS, 3 * BS)])
            dma("y", "yb", [(T.yb[:, YO:YO + P], T.y0[:, :])], [], [("yb", YO, YO + P)])
            dma("y", "sk", [(T.sdblk[0::16, :], T.sd[:, 0:FB]), (T.sdblk[1::16, 0:BS - FB], T.sd[:, FB:BS])], [], [("sdblk",)])
            dma("y", "z3", [blocks("zf", "w3", FB)[::-1]], [("zf",)], [("w3",)])

        def gs(a, b):
            gat("s", (cand, 16 * a, 16 * b), win, (off, a, b))

        def gv(a, b):
            gat("v", (cand, 16 * a, 16 * b), win, (off, a, b))

        def X(c):
            for i in range(16):
                k = 1024 * (c % 2) + 64 * i
                sums(("pd", k, k + 64), [(("dN",), (xm, 64 * c, 64 * c + 64)), (("dS",), (cand, 1024 * c + i, 1024 * c + 1024, 16))])

        def L(c, n=1024):
            for k in range(1024 * (c % 2), 1024 * (c % 2) + 1024, n):
                ts(("nr", k, k + n), ("pd", k, k + n), RND, OP.add, RND, OP.not_equal)

        def cnt(a, b):
            k = a + (512 - LAST[s] if out and a >= LAST[s] else 0)
            return ("cnt", k, k + b - a)

        def C(c):
            k = 1024 * (c % 2)
            sums(cnt(64 * c, 64 * c + 64), [(("fB",), ("ones", 0, 64))] * out + [(cmat(i), ("nr", k + 64 * i, k + 64 * i + 64)) for i in range(16)])

        def Pt(a=0, b=CAP):
            cn = cnt(a, b)
            if out:
                m = ("cnt", cn[1] + 256, cn[2] + 256)
                tt(m, cn, ("comp", a, b), OP.max)
                tt(m, m, ("trash", a % 128, a % 128 + b - a), OP.min)
                tc("v", ("vo", a, b), m)
            else:
                ts(("mt", a, b), cn, FAR, OP.is_lt)
                mm(("psA", a, b), ("B",), ("mt", a, b), True, True)

        def S(a, b):
            w, o, i = ("w2",), ("vo", a, b), ("cst", 0, 16 * (b - a))
            op("s", lambda: g.scalar.activation(ap(w).indirect(ap(o)), ap(i), AF.Tanh), [o, i], [w])

        def V(a, b):
            sca(("w1",), ("vo", a, b), ("ones", 0, 16 * (b - a)))

        def G():
            tc("s", ("c2b",), ("w2", 2 * P, ST))
            for k, ps in enumerate(("psA", "psB")):
                for b in range(2):
                    mm((ps, 0, NB // 2), ("ident",), ("c2b", NB * k + b, NB * k + NB, 2), b == 0, False)

        def F():
            for k, ps in enumerate(("psA", "psB")):
                for b in range(2):
                    mm((ps, 0, NB // 2), ("ident",), ("w1", 2 * P + NB * k + b, 2 * P + NB * k + NB, 2), False, b == 1)
                tc("sv"[k] if s < 2 else "v", ("fsend", NB // 2 * k, NB // 2 * (k + 1)), (ps, 0, NB // 2))
            send("f%d" % s, "fsend", "L%d" % s, 0, -1)

        def N(a, b):
            r = (1024 * a, 1024 * b)
            scan(("scn",) + r, ("d0", 0, r[1] - r[0]), ("cb",) + r, 191.0, OP.max, OP.min)

        def H(a=0, b=CAP):
            sums(("psB", a, b), [(("hX",), (xm, a, b)), (("qI",), ("ones", a, b)), (("hI",), ("scn", 16 * a + 15, 16 * b, 16))])

        def hv(a=0, b=CAP):
            ts(("hi", a, b), ("psB", a, b), RND, OP.add, -RND, OP.add)

        def D(a=0, b=CAP):
            m = ("psA", CAP + a, CAP + b)
            ts(m, ("psA", a, b), 1.5, OP.is_ge, 255.0, OP.mult)
            tt((wn, a, b), ("hi", a, b), m, OP.max)

        def O():
            r = (ot, YO + BS * s, YO + BS * s + BS)
            if s:
                landed("b%d" % s)
            dma("s" if s == 0 else "y", "o%d" % s, [(T.yv[:, BS * s:BS * s + BS], ap(r))], [r], [])

        def U(k=16):
            a = YO + BS * s
            if k < 32:
                gat("s", (ot, a + 16 * k, a + 512), (wn, 0, YO + P), ("sb16_%d" % s, k, 32))
            if k:
                gat("v", (ot, a, a + 16 * k), (wn, 0, YO + P), ("sb16_%d" % s, 0, k))

        def Y(k=12):
            w = (ot, YO, YO + P)
            if k < 24:
                gat("s", ("ysend", 16 * k, 384), w, ("snd16", k, 24))
            if k:
                gat("v", ("ysend", 0, 16 * k), w, ("snd16", 0, k))
            send("b%d" % s, "ysend", ot, YO + P, 1)
            r = (YO + BS * s, YO + BS * s + BS)
            if s == 2:
                landed("b2")
                dma("y", "cy", [(ap((wn,) + r), ap((ot,) + r))], [(ot,) + r], [(wn,) + r])

        def ck():
            offsets(s, 64, 256)

        def marks(a=0, b=CAP):
            r = ("psA", CAP + a, CAP + b)
            ts(r, ("comp", a, b), RND, OP.add, -RND, OP.add)
            tt((xm, a, b), ("comp", a, b), r, OP.subtract)

        def R():
            w, o, i = ("w3",), ("snd16",), ("L2f",)
            act(i, ("L2",), AF.Copy, scale=30.0)
            op("s", lambda: g.scalar.activation(ap(w).indirect(ap(o)), ap(i), AF.Tanh), [o, i], [w])
            dma("y", "bl3", [blocks("w3blk", "w3", FB)], [w], [("w3blk",)])

        def M():
            gat("s", ("memrep", BS * s, BS * s + BS), ("mw",), ("sb16_%d" % s,))
            if s == 2:
                dma("y", "blm", [(T.memblk[b::16, 0:min(FB, 1536 - FB * b)], T.memrep[b::16, FB * b:min(1536, FB * b + FB)])
                                 for b in range(5)], [("memrep",)], [("memblk",)])

        def own_blocks():
            dma("y", "bl2", [blocks("w2blk", "w2", 2 * FB)], [("w2", 0, 2 * P)], [("w2blk",)])
            dma("y", "bl1", [blocks("w1blk", "w1", 2 * FB)], [("w1", 0, 2 * P)], [("w1blk",)])

        def W():
            tc("s", ("w2bb",), ("w2blk",))

        def E():
            i, o = ("ident",), ("cnt", 512, 512 + FB)
            tc("s", ("w3bb",), ("w3blk",))
            sums(o, [(i, ("sdblk",)), (i, ("w2bb", 0, 2 * FB, 2)), (i, ("w2bb", 1, 2 * FB, 2)), (i, ("w1blk", 0, 2 * FB, 2)),
                     (i, ("w1blk", 1, 2 * FB, 2)), (i, ("memblk",)), (("nI",), ("ones", 0, FB)), (i, ("w3bb",))])

        def e():
            tt(("yfb",), ("cnt", 512, 512 + FB), ("memblk",), OP.min)
            dma("y", "of", [(T.yf[:, :], T.yfb[:, :])], [("yfb",)], [])

        return {"O": O, "B": own_blocks, "s": gs, "v": gv, "X": X, "L": L, "C": C, "P": Pt, "S": S, "V": V, "F": F, "G": G, "N": N, "H": H,
                "K": lambda c: L(c, 512), "h": hv, "E": E, "e": e, "z": lambda: slots(s),
                "w": wide, "o": own, "t": theirs, "y": first_y, "Z": send_y,
                "a": lambda: mm(("psB",), ("kI",), ("xw", BS * s, BS * s + BS), True, True), "A": lambda: pack(s),
                "l": lambda: lists(s), "n": lambda: compact(s),
                "b": lambda: scaled((("hX", "ident", XS / 2), ("hI", "ident", 0.5), ("qI", "ident", -0.25), ("nI", "ident", -1.0))),
                "f": lambda: sfill(("comp", 0, CAP), 255 / XS), "D": D, "U": U, "Y": Y, "m": marks, "c": ck, "R": R, "M": M, "W": W}

    streams = {n: stream(n) for n in ("f0", "f1", "f2", "b2", "b1", "b0")}

    def play(key):
        for part in SCHED[key].split(";"):
            words = part.split()
            for w in words[1:]:
                TAG[0] = words[0] + w
                streams[words[0]][w[0]](*[int(a) for a in w[1:].split("-") if a])
        TAG[0] = ""

    h = P // 2
    dma("s", "snd", [(T.snd32[:, :], T.snd[:, :])], [], [("snd32",)])
    dma("y", "tl", [(T.tlb[:, :], T.tl[:, :])], [], [("tlb",)])
    dma("s", "xb", [(T.xw[:, h:P], T.x[:, h:P])], [], [("xw", h, P)])
    dma("y", "xa", [(T.xw[:, 0:h], T.x[:, 0:h])], [], [("xw", 0, h)])
    fill(("ones", 0, CAP), 1.0)
    fill(("sdrep",), 0.0)
    dma("y", "sd", [(T.sdrep[0::16, :], T.sd[:, :])], [], [("sdrep",)])
    dma("y", "cd0", [(T.cdt[:, 0:BS], T.cd[:, 0:BS])], [], [("cdt", 0, BS)])

    sel(("B",), ("ones", 0, 128), [[-16, 8], [0, 16]], OP.is_ge, 0.0, 0, 1)
    sel(("B",), ("B",), [[16, 8], [0, 16]], OP.is_ge, 0.0, 15, -1)
    iota(("io384",), [[1, NB]], -NB // 2, 0)
    sel(("ident",), ("ones", 0, 128), [[-1, 128]], OP.is_equal, 0.0, 0, 1)
    sel(("A",), ("B",), [[1, 128]], OP.is_gt, 0.0, 0, -1)
    sel(("A",), ("A",), [[-1, 128]], OP.not_equal, -BIG, 0, 1)
    iota(("t512",), [[16, 32]], BS, 1)
    iota(("itp",), [[0, 1]], 0, 1)

    fill(("C",), 0.0)
    act(("warm",), ("ones", 0, 8), AF.Tanh)
    for q in range(8):
        act(("C", 16 * q, 16 * q + 129 * 15 + 1, 129), ("B", 16 * q, 16 * q + 16), AF.Copy, scale=CS)
    scaled((("nA", "A", -1.0),))
    fill(("w1", BS, 3 * BS), float(NB // 2))
    tc("v", ("snd16",), ("snd32",))
    sca(("w1", 0, P), ("snd16",), ("io384",))
    fill(("one32",), 1.0)
    fill(("flw", 0, 1), 0.0)
    fill(("zb",), 0.0)
    sums(("psB", 0, 64), [(cmat(r), ("w1", BS + r, 3 * BS, 16)) for r in range(16)])
    ts(("tlf",), ("tlb",), 2.0, OP.mult, 1.0, OP.add)
    op("v", lambda: g.vector.reciprocal(ap(("rec",)), ap(("tlf",))), [("tlf",)], [("rec",)])
    ts(("dS",), ("ident",), ("rec",), OP.mult)

    gat("s", ("xsend", 192, NB), ("xw", 0, P), ("snd16", 12, 24))
    gat("v", ("xsend", 0, 192), ("xw", 0, P), ("snd16", 0, 12))
    send("x", "xsend", "xw", P, 1)
    ts(("binv",), ("psB", 0, 64), 1.0 / (16 * CS), OP.mult, float(NB // 2), OP.add)
    scaled((("kI", "ident", 1.0 / XS),))
    sfill(("zf",), 0.0)
    for name, win, z in (("z1", "w1", "zb"), ("z2", "w2", "zf")):
        dma("y", name, [(T[win][0::16, a:b], T[z][:, 0:(b - a) // 16]) for a, b in ((0, 1024), (3072, 2 * P))], [(z,)],
            [(win, 0, 1024), (win, 3072, 2 * P)])
    sfill(("comp", 0, CAP), 255 / XS)
    scaled((("dN", "dS", -XS), ("fB", "B", -FAR / 16)))
    sfill(("w2", 1024, 3072), 0.0)
    iota(("trash",), [[16, 128]], ST, 1)
    for r, c in ((("cst",), 30), (("w2", 2 * P, ST), 0), (("w1", 2 * P, ST), 0), (("ones", CAP, width("ones")), 1),
                 (("L0", NB, 400), 0), (("L1", NB, 400), 0), (("sdblk",), 0), (("memblk",), 1)):
        iota(r, [[0, reg(r)[2] - reg(r)[1]]], c, 0)
    sums(("psA", 0, 32), [(cmat(r), ("sdrep", r, BS, 16)) for r in range(16)])
    play("pre0")
    fill(("w1", 1024, 2304), 0.0)
    sfill(("w1", 2304, 3072), 0.0)
    landed("x")
    dma("y", "ya", [(T.ya[:, YO:YO + P], T.y0[:, :])], [], [("ya", YO, YO + P)])
    dma("y", "cd1", [(T.cdt[:, BS:2 * BS], T.cd[:, BS:2 * BS])], [], [("cdt", BS, 2 * BS)])

    for key in ("out0", "to1", "out1", "to2", "back2", "gap1", "back1", "gap0", "back0"):
        play(key)
    need("g", list(total.items()))
    for s, n in total.items():
        if s != "qg" and known["g"].get(s, 0) < n:
            g.wait_ge(T.sem[s], n)
